import numpy as np
import ml_dtypes


def mxq(x, axis, fmt="e4m3"):
    dtype, down = {"e4m3": (ml_dtypes.float8_e4m3fn, 7), "e5m2": (ml_dtypes.float8_e5m2, 14)}[fmt]
    v = np.moveaxis(np.asarray(x, np.float32).astype(ml_dtypes.bfloat16).astype(np.float64), axis, -1)
    blocks = v.reshape(v.shape[:-1] + (-1, 32))
    amax = np.abs(blocks).max(-1, keepdims=True)
    byte = np.maximum(np.where(amax > 0, np.frexp(amax)[1] - 1 + 127, 0) - down, 1)
    scale = np.exp2(byte - 127.0)
    codes = (blocks / scale).astype(np.float32).astype(dtype).astype(np.float64)
    return np.moveaxis((codes * scale).reshape(v.shape), -1, axis)


WIDE = False


def mx_kscale(k):
    if not WIDE:
        return np.ones(k)
    levels = np.array([10, -10, 5, -5, 0])
    if k % 512:
        return np.exp2(np.random.permutation(np.resize(levels, k // 32))).repeat(32)
    a = np.empty((k // 512, 16))
    for p in range(k // 512):
        a[p, :8] = np.random.permutation(np.resize(levels, 8))
        for g in range(8):
            far = levels[np.abs(levels - a[p, g]) >= 10]
            a[p, g + 8] = far[np.random.randint(len(far))]
    return np.exp2(a.ravel()).repeat(32)


def f64(x):
    return np.asarray(x).astype(np.float64)


def striped(idx):
    return np.tile(idx.reshape(-1, 16).T, (8, 1)).astype(np.uint16)


def unstriped(offs):
    return offs[:16].T.reshape(-1).astype(np.int64)


E2M1 = np.array([0.0, 0.5, 1.0, 1.5, 2.0, 3.0, 4.0, 6.0, -0.0, -0.5, -1.0, -1.5, -2.0, -3.0, -4.0, -6.0])


def pack_weight(w, fmt):
    k, n = w.shape
    w = f64(np.asarray(w, np.float32).astype(ml_dtypes.bfloat16)).reshape(k // 32, 32, n)
    amax = np.abs(w).max(1)
    if fmt == "e4m3":
        byte = np.frexp(amax)[1] - 1 + 127 - 7
    else:
        mant, ex = np.frexp(amax / 6.0)
        byte = np.where(mant > 0.5, ex, ex - 1) + 127
    byte = np.clip(np.where(amax > 0, byte, 1), 1, 254)
    scaled = (w * np.exp2(127.0 - byte)[:, None, :]).reshape(k, n).astype(np.float32)
    by_word = np.ascontiguousarray(scaled.reshape(k // 512, 128, 4, n).transpose(0, 1, 3, 2))
    if fmt == "e4m3":
        words = by_word.astype(ml_dtypes.float8_e4m3fn).view(np.uint8)
    else:
        c = by_word.astype(ml_dtypes.float4_e2m1fn).view(np.uint8) & 0xF
        words = (c[..., 0::2] | (c[..., 1::2] << 4)).reshape(k // 512, 128, 2 * n)
    return np.ascontiguousarray(words), np.ascontiguousarray(byte.astype(np.uint8).reshape(k // 512, 16, n))


def unpack_weight(words, scales, fmt):
    g, _, n = scales.shape
    words = np.ascontiguousarray(words).reshape(g, 128, n, -1)
    if fmt == "e4m3":
        vals = words.view(ml_dtypes.float8_e4m3fn).astype(np.float64)
    else:
        nib = np.empty((g, 128, n, 4), np.uint8)
        nib[..., 0::2] = words & 0xF
        nib[..., 1::2] = words >> 4
        vals = E2M1[nib]
    vals = vals * np.repeat(np.exp2(scales.astype(np.float64) - 127.0), 8, axis=1)[..., None]
    return vals.transpose(0, 1, 3, 2).reshape(g * 512, n)


def gelu(v):
    return 0.5 * v * (1.0 + np.tanh(np.sqrt(2.0 / np.pi) * (v + 0.044715 * v**3)))


K, H, N, T, S = 1024, 512, 768, 4096, 1024

def setup_inputs():
    n = np.random.standard_normal
    s = mx_kscale(K)[:, None]
    u = mx_kscale(H)[:, None]
    tab_words, tab_scales = pack_weight(n((K, T)) * s, "e4m3")
    w2_words, w2_scales = pack_weight(0.7 * n((K, H)) / np.sqrt(K) / s, "e2m1")
    w3_words, w3_scales = pack_weight(0.8 * n((K, H)) / np.sqrt(K) / s, "e4m3")
    return {
        "tab_words": tab_words, "tab_scales": tab_scales,
        "offs": striped(np.random.permutation(T)[:S]),
        "offs2": striped(np.random.permutation(T)[:S]),
        "offs3": striped(np.random.permutation(T)[:S]),
        "w1": (0.7 * n((K, H)) / np.sqrt(K) / s).astype(np.float32),
        "w2_words": w2_words, "w2_scales": w2_scales,
        "w3_words": w3_words, "w3_scales": w3_scales,
        "g": (np.exp(0.3 * n(H)) * u[:, 0]).astype(np.float32),
        "w4": (n((H, N)) / np.sqrt(H) / u).astype(np.float32),
        "b4": (0.3 * n(N)).astype(np.float32),
    }

def reference(tab_words, tab_scales, offs, offs2, offs3, w1, w2_words, w2_scales, w3_words, w3_scales, g, w4, b4):
    v = unpack_weight(tab_words, tab_scales, "e4m3")[:, unstriped(offs)]
    va = unpack_weight(tab_words, tab_scales, "e4m3")[:, unstriped(offs2)]
    vn = unpack_weight(tab_words, tab_scales, "e4m3")[:, unstriped(offs3)]
    w2 = unpack_weight(w2_words, w2_scales, "e2m1")
    w3 = unpack_weight(w3_words, w3_scales, "e4m3")
    p = mxq(f64(w1), 0, "e4m3").T @ v + w2.T @ va
    q = w3.T @ vn
    d = np.tanh(p) - q
    h = np.square(d) * f64(g)[:, None]
    y = mxq(f64(w4), 0, "e4m3").T @ mxq(h, 0, "e4m3")
    return y + f64(b4)[:, None]

@@ -1,0 +1,278 @@
+from contextlib import ExitStack
+
+import concourse.mybir as mybir
+
+K, H, N, T, S = 1024, 512, 768, 4096, 1024
+FLOPS = 2 * S * H * (3 * K + N)
+
+F32 = mybir.dt.float32
+BF16 = mybir.dt.bfloat16
+I32 = mybir.dt.int32
+U32 = mybir.dt.uint32
+U16 = mybir.dt.uint16
+U8 = mybir.dt.uint8
+FP8X4 = mybir.dt.float8_e4m3fn_x4
+FP4X4 = mybir.dt.float4_e2m1fn_x4
+ACT = mybir.ActivationFunctionType
+ALU = mybir.AluOpType
+
+P = 128
+PACK = 4
+PASSES = 2
+HALF = 512
+CHUNK = 128
+GROUPS = [[0,1],[2,3],[4,5],[6],[7]]
+LOADS = "a1 W0 a0 s s s w2 b1 g w3 b0 s s s s s W1 g B f f f f g g".split()
+TEXT = "G10A G10B G00A C1 C0 S1 f0 P2 S0 p10A3 G01A p10A1 S2 G11A p20A0 p10A2 p11A0 P3 p10A0 p20A2 G11B G21A p21A3 p21A0 G00B G01B p10B1 p10B0 p11A3 p20B3 p20A1 p21A1 p20B0 p11A2 tA0 G21B p20A3 p21A2 p11A1 p21B1 G20A G20B tA1 q2 tA2 f2 q0 p21B0 q1 p11B2 p10B2 q6 p21B3 p20B1 tA3 d1 p20B2 d0 p11B1 q3 s1 f1 p10B3 p11B3 p21B2 p11B0 tB3 q5 d2 s0 d3 m0 h0 q7 s2 tB1 s3 tB0 q4 tB2 m3 d5 m1 d4 h1 s5 s4 m4 m2 h3 h2 d6 y11 m5 y10 s6 h5 d7 m6 h6 y01 s7 y02 y30 m7 h7 h4 y31 y12 y21 y42 y20 y41 y40 y00 y32 y22".split()
+GP_MULT = [0,0,0,0,0,0,0,0]
+VEC_EVAC = {"0":[1],"1":[2],"2":[2],"3":[2,1],"4":[2,0]}
+SHARE = [["G10A","G21B"]]
+W4_ENG = ["act","act","dve"]
+PSUM_TAGS = {"p":["ps",8],"y":["ps",8],"feat":["ps",8]}
+RING = 4
+
+
+def tile_list_replay_curiosity_bonus_kernel(
+    tc, tab_words, tab_scales, offs, offs2, offs3, w1, w2_words, w2_scales, w3_words, w3_scales, g, w4, b4, out
+):
+    nc = tc.nc
+    with ExitStack() as ctx:
+        keep = ctx.enter_context(tc.tile_pool(name="keep", bufs=1))
+        ring = ctx.enter_context(tc.tile_pool(name="ring", bufs=RING))
+        psum = ctx.enter_context(tc.psum_pool(name="psum", bufs=1))
+        ctx.enter_context(nc.allow_non_contiguous_dma(reason="per-partition gains and biases"))
+
+        lists = [keep.tile([P, S // 16], U16, name=f"list{x}") for x in range(3)]
+        tsc = keep.tile([P, T // 4], I32, name="tsc")
+        wsc_raw = keep.tile([P, PASSES, H // 4], I32, name="wsc_raw")
+        shifted = keep.tile([P, S // 4], I32, name="shifted", align_bytes=64)
+        nc.vector.memset(tsc[:], 0)
+        nc.vector.memset(wsc_raw[:], 0)
+        nc.vector.memset(shifted[:], 0)
+
+        nc.sync.dma_start(lists[1][:], offs2)
+        nc.sync.dma_start(lists[0][:], offs)
+        nc.sync.dma_start(lists[2][:], offs3)
+        for r in range(4):
+            for a in range(PASSES):
+                rows = tab_scales[a].rearrange("(q r) n -> r q n", r=4)[r]
+                nc.sync.dma_start(tsc[4 * a + r : P : 32, :], rows.bitcast(I32))
+
+        words = [keep.tile([P, T], I32, name=f"words{a}") for a in range(PASSES)]
+        w1_raw = [[keep.tile([P, PACK, H // 2], F32, name=f"w1_raw{a}{b}") for b in range(2)] for a in range(PASSES)]
+        w2_raw = keep.tile([P, PASSES, H // 2], I32, name="w2_raw")
+        w3_raw = keep.tile([P, PASSES, H], I32, name="w3_raw")
+        w4_raw = keep.tile([P, PACK, N], F32, name="w4_raw")
+        g_pad = keep.tile([P, PACK, 8], F32, name="g_pad")
+        bias = keep.tile([P, N // P], F32, name="bias")
+
+        seen = {"s": 0, "g": 0, "f": 0}
+        for o in LOADS:
+            if o in ("a0", "a1", "b0", "b1"):
+                a, b = {"a": 0, "b": 1}[o[0]], int(o[1])
+                rows = w1[512 * a : 512 * (a + 1), :].rearrange("(p j) r -> p j r", j=PACK)
+                nc.sync.dma_start(w1_raw[a][b][:], rows[:, :, 256 * b : 256 * (b + 1)])
+            elif o == "s":
+                w, r = divmod(seen[o], 4)
+                rows = (w2_scales, w3_scales)[w].rearrange("a (q r) n -> r q a n", r=4)[r]
+                nc.sync.dma_start(wsc_raw[4 * w + r : P : 32, :, :], rows.bitcast(I32))
+            elif o == "g":
+                t = seen[o]
+                nc.sync.dma_start(g_pad[:, t, 0:1], g.rearrange("(c t i o) -> t c i o", t=4, i=4, o=1)[t])
+            elif o == "f":
+                t = seen[o]
+                nc.sync.dma_start(w4_raw[:, t, :], w4.rearrange("(c t i) n -> t c i n", t=4, i=4)[t])
+            elif o == "B":
+                nc.sync.dma_start(bias[:], b4.rearrange("(u p) -> p u", p=P))
+            elif o == "w2":
+                nc.sync.dma_start(w2_raw[:], w2_words.rearrange("a p n -> p a n").bitcast(I32))
+            elif o == "w3":
+                nc.sync.dma_start(w3_raw[:], w3_words.rearrange("a p n i -> p a (n i)").bitcast(I32))
+            else:
+                a = int(o[1])
+                nc.sync.dma_start(words[a][:], tab_words[a].rearrange("p t i -> p (t i)").bitcast(I32))
+            if o in seen:
+                seen[o] = seen[o] + 1
+
+        gsc = [keep.tile([P, S], U8, name=f"gsc{x}", align_bytes=64) for x in range(3)]
+        w1_bf = [keep.tile([P, PACK, 32, 4, PACK], BF16, name=f"w1_bf{a}", align_bytes=64) for a in range(PASSES)]
+        w1q = keep.tile([P, PASSES, H], U32, name="w1q", align_bytes=64)
+        w1s = keep.tile([P, PASSES, H], U8, name="w1s", align_bytes=64)
+        w2p = keep.tile([P, PASSES, H // 2], I32, name="w2p", align_bytes=64)
+        w3p = keep.tile([P, PASSES, H], I32, name="w3p", align_bytes=64)
+        wsc = keep.tile([P, PASSES, H // 4], I32, name="wsc", align_bytes=64)
+        w4q = keep.tile([P, N], U32, name="w4q", align_bytes=64)
+        w4s = keep.tile([P, N], U8, name="w4s", align_bytes=64)
+        gain = keep.tile([P, PACK], F32, name="gain")
+        pred = [keep.tile([P, PACK, HALF], F32, name=f"pred{h}") for h in range(2)]
+        hq = [keep.tile([P, CHUNK * len(G)], U32, name=f"hq{i}", align_bytes=64) for i, G in enumerate(GROUPS)]
+        hs = [keep.tile([P, CHUNK * len(G)], U8, name=f"hs{i}", align_bytes=64) for i, G in enumerate(GROUPS)]
+        out_v = out.rearrange("(u p) j -> p u j", p=P)
+
+        nc.vector.tensor_copy(
+            wsc[:].rearrange("p a (t c) -> p a t c", t=4), wsc_raw[:].rearrange("p a (c t) -> p a t c", t=4)
+        )
+        nc.scalar.copy(gain[:], g_pad[:, :, 0])
+
+        def permute(dst, src, run):
+            for a in range(PASSES):
+                nc.vector.tensor_copy(
+                    dst[:, a, :].rearrange("p (t c i) -> p t c i", t=4, i=run),
+                    src[:, a, :].rearrange("p (c t i) -> p t c i", t=4, i=run),
+                )
+
+        def bank(kind, shape, name):
+            return psum.tile(shape, F32, name=name, tag=PSUM_TAGS[kind][0], bufs=PSUM_TAGS[kind][1])
+
+        gw, acc, done, feat, diff, sq, hb = {}, {}, {}, {}, {}, {}, {}
+        half = {"A": 0, "B": 1}
+        for s in TEXT:
+            k = s[0]
+            if k == "S":
+                x = int(s[1])
+                nc.vector.tensor_copy(gsc[x][:], tsc[:].bitcast(U8).indirect(lists[x][:]))
+                if x == 1:
+                    nc.scalar.dma_start(shifted[0:100, :], gsc[1][4:104, :].bitcast(I32))
+            elif k == "G":
+                x, a, h = int(s[1]), int(s[2]), half[s[3]]
+                tag = s
+                for pair in SHARE:
+                    if s in pair:
+                        tag = pair[0]
+                gw[x, a, h] = keep.tile([P, HALF], U32, name=s, tag=tag, align_bytes=64)
+                nc.vector.tensor_copy(
+                    gw[x, a, h][:], words[a][:].bitcast(U32).indirect(lists[x][:, 32 * h : 32 * (h + 1)])
+                )
+            elif k == "C":
+                a = int(s[1])
+                for b in range(2):
+                    src = w1_raw[a][b][:].rearrange("p j (c t i) -> p t c j i", t=4, i=4)
+                    for t in range(PACK):
+                        dst = w1_bf[a][:, t, 16 * b : 16 * (b + 1), :, :].rearrange("p c i j -> p c j i")
+                        nc.scalar.activation(dst, src[:, t], ACT.Copy)
+                nc.vector.quantize_mx(
+                    out=w1q[:, a, :].bitcast(FP8X4),
+                    scales=w1s[:, a, :],
+                    in_=w1_bf[a][:].rearrange("p t c i j -> p (t c i j)"),
+                )
+            elif s == "P2":
+                permute(w2p, w2_raw, 2)
+            elif s == "P3":
+                permute(w3p, w3_raw, 4)
+            elif k == "p":
+                w, a, h, t = int(s[1]), int(s[2]), half[s[3]], int(s[4])
+                if (h, t) not in acc:
+                    acc[h, t] = bank("p", [P, HALF], f"acc{h}{t}")
+                    done[h, t] = 0
+                cols = slice(HALF * h, HALF * (h + 1))
+                m = slice(P * t, P * (t + 1))
+                if w == 1:
+                    lhs, lhs_s = w1q[:, a, m].bitcast(FP8X4), w1s[:, a, m]
+                    rhs, rhs_s = gw[0, a, h][:], gsc[0][4 * a : P, cols]
+                else:
+                    lhs = w2p[:, a, :].bitcast(U8)[:, 2 * P * t : 2 * P * (t + 1)].bitcast(FP4X4)
+                    lhs_s = wsc[:, a, :].bitcast(U8)[:, m]
+                    rhs = gw[1, a, h][:]
+                    rhs_s = gsc[1][:, cols] if a == 0 else shifted[:].bitcast(U8)[:, cols]
+                nc.tensor.matmul_mx(
+                    acc[h, t][:],
+                    lhsT=lhs,
+                    lhsT_scale=lhs_s,
+                    rhs=rhs.bitcast(FP8X4),
+                    rhs_scale=rhs_s,
+                    start=(done[h, t] == 0),
+                    stop=(done[h, t] == 3),
+                )
+                done[h, t] = done[h, t] + 1
+            elif k == "t":
+                h, t = half[s[1]], int(s[2])
+                nc.scalar.activation(pred[h][:, t, :], acc[h, t][:], ACT.Tanh)
+            elif k == "f":
+                b = int(s[1])
+                cols = slice(256 * b, 256 * (b + 1))
+                w4_bf = keep.tile([P, 256, PACK], BF16, name=f"w4_bf{b}", align_bytes=64)
+                if W4_ENG[b] == "dve":
+                    nc.vector.tensor_copy(
+                        w4_bf[:].rearrange("p (c i) t -> p c t i", i=4),
+                        w4_raw[:, :, cols].rearrange("p t (c i) -> p c t i", i=4),
+                    )
+                else:
+                    nc.scalar.activation(
+                        w4_bf[:].rearrange("p (c i) t -> p c t i", i=4),
+                        w4_raw[:, :, cols].rearrange("p t (c i) -> p c t i", i=4),
+                        ACT.Copy,
+                    )
+                nc.vector.quantize_mx(
+                    out=w4q[:, cols].bitcast(FP8X4), scales=w4s[:, cols], in_=w4_bf[:].rearrange("p n t -> p (n t)")
+                )
+            elif k == "q":
+                c = int(s[1])
+                h = c // 4
+                cols = slice(CHUNK * (c % 4), CHUNK * (c % 4 + 1))
+                gcols = slice(CHUNK * c, CHUNK * (c + 1))
+                feat[c] = bank("feat", [P, PACK, CHUNK], f"feat{c}")
+                for t in range(PACK):
+                    m = slice(P * t, P * (t + 1))
+                    for a in range(PASSES):
+                        nc.tensor.matmul_mx(
+                            feat[c][:, t, :],
+                            lhsT=w3p[:, a, m].bitcast(FP8X4),
+                            lhsT_scale=wsc[4:P, a, :].bitcast(U8)[:, m],
+                            rhs=gw[2, a, h][:, cols].bitcast(FP8X4),
+                            rhs_scale=gsc[2][4 * a : P, gcols],
+                            start=(a == 0),
+                            stop=(a == PASSES - 1),
+                        )
+            elif k == "d":
+                c = int(s[1])
+                cols = slice(CHUNK * (c % 4), CHUNK * (c % 4 + 1))
+                diff[c] = ring.tile([P, PACK, CHUNK], F32, name="diff")
+                nc.vector.tensor_tensor(diff[c][:], pred[c // 4][:, :, cols], feat[c][:], ALU.subtract)
+            elif k == "s":
+                c = int(s[1])
+                sq[c] = ring.tile([P, CHUNK, PACK], F32, name="sq")
+                nc.scalar.activation(
+                    sq[c][:].rearrange("p (c i) t -> p c t i", i=4),
+                    diff[c][:].rearrange("p t (c i) -> p c t i", i=4),
+                    ACT.Square,
+                )
+            elif k == "m":
+                c = int(s[1])
+                hb[c] = ring.tile([P, CHUNK, PACK], BF16, name="hb", align_bytes=64)
+                eng = nc.gpsimd if GP_MULT[c] else nc.vector
+                eng.tensor_tensor(hb[c][:], sq[c][:], gain[:].unsqueeze(1).to_broadcast([P, CHUNK, PACK]), ALU.mult)
+            elif k == "h":
+                c = int(s[1])
+                gi = [i for i, G in enumerate(GROUPS) if c in G][0]
+                c0 = CHUNK * GROUPS[gi].index(c)
+                nc.vector.quantize_mx(
+                    out=hq[gi][:, c0 : c0 + CHUNK].bitcast(FP8X4),
+                    scales=hs[gi][:, c0 : c0 + CHUNK],
+                    in_=hb[c][:].rearrange("p j t -> p (j t)"),
+                )
+            else:
+                gi, b = int(s[1]), int(s[2])
+                width = CHUNK * len(GROUPS[gi])
+                ocols = slice(CHUNK * GROUPS[gi][0], CHUNK * GROUPS[gi][0] + width)
+                y = bank("y", [P, 2, width], f"y{gi}{b}")
+                res = keep.tile([P, 2, width], F32, name=f"res{gi}{b}")
+                for e in range(2):
+                    m = slice(P * (2 * b + e), P * (2 * b + e + 1))
+                    nc.tensor.matmul_mx(
+                        y[:, e, :],
+                        lhsT=w4q[:, m].bitcast(FP8X4),
+                        lhsT_scale=w4s[:, m],
+                        rhs=hq[gi][:].bitcast(FP8X4),
+                        rhs_scale=hs[gi][:],
+                        start=True,
+                        stop=True,
+                    )
+                if b in VEC_EVAC.get(str(gi), ()):
+                    nc.vector.tensor_tensor(
+                        res[:], y[:], bias[:, 2 * b : 2 * b + 2].unsqueeze(2).to_broadcast([P, 2, width]), ALU.add
+                    )
+                else:
+                    for e in range(2):
+                        u = 2 * b + e
+                        nc.scalar.activation(res[:, e, :], y[:, e, :], ACT.Identity, bias=bias[:, u : u + 1])
+                nc.sync.dma_start(out_v[:, 2 * b : 2 * b + 2, ocols], res[:])

@@ -1,6 +1,7 @@
 from contextlib import ExitStack
 
 import concourse.mybir as mybir
+from concourse.masks import make_identity
 
 K, H, N, T, S = 1024, 512, 768, 4096, 1024
 FLOPS = 2 * S * H * (3 * K + N)
@@ -21,15 +22,15 @@ PACK = 4
 PASSES = 2
 HALF = 512
 CHUNK = 128
-GROUPS = [[0,1],[2,3],[4,5],[6],[7]]
-LOADS = "a1 W0 a0 s s s w2 b1 g w3 b0 s s s s s W1 g B f f f f g g".split()
-TEXT = "G10A G10B G00A C1 C0 S1 f0 P2 S0 p10A3 G01A p10A1 S2 G11A p20A0 p10A2 p11A0 P3 p10A0 p20A2 G11B G21A p21A3 p21A0 G00B G01B p10B1 p10B0 p11A3 p20B3 p20A1 p21A1 p20B0 p11A2 tA0 G21B p20A3 p21A2 p11A1 p21B1 G20A G20B tA1 q2 tA2 f2 q0 p21B0 q1 p11B2 p10B2 q6 p21B3 p20B1 tA3 d1 p20B2 d0 p11B1 q3 s1 f1 p10B3 p11B3 p21B2 p11B0 tB3 q5 d2 s0 d3 m0 h0 q7 s2 tB1 s3 tB0 q4 tB2 m3 d5 m1 d4 h1 s5 s4 m4 m2 h3 h2 d6 y11 m5 y10 s6 h5 d7 m6 h6 y01 s7 y02 y30 m7 h7 h4 y31 y12 y21 y42 y20 y41 y40 y00 y32 y22".split()
-GP_MULT = [0,0,0,0,0,0,0,0]
-VEC_EVAC = {"0":[1],"1":[2],"2":[2],"3":[2,1],"4":[2,0]}
-SHARE = [["G10A","G21B"]]
-W4_ENG = ["act","act","dve"]
+GROUPS = [[0,1],[2,3],[4,5],[6,7]]
+LOADS = "w2 s s a0 s s W0 s s b0 s s W1 w3 f f f f".split()
+TEXT = "S0 S1 S2 P2 C0 C1 P3 G00A G10A G20A G00B Q0 Q1 p20A0 p10A0 p20A1 p10A1 p20A2 p10A2 p20A3 p10A3 G01A G11A p11A0 p21A0 tA0 p11A1 p21A1 tA1 p11A2 p21A2 tA2 p11A3 p21A3 tA3 G10B G21A q0 q1 q2 q3 G11B d0 s0 G01B f0 f1 f2 d1 s1 d2 s2 d3 s3 p10B0 p20B0 p11B0 p21B0 tB0 p10B1 p20B1 p11B1 p21B1 tB1 p10B2 p20B2 p11B2 p21B2 tB2 p10B3 p20B3 p11B3 p21B3 tB3 m0 m1 F0 F1 F2 h0 y00 y01 y02 G20B m2 m3 h1 e00 e01 e02 G21B y10 y11 y12 q4 q5 q6 q7 e10 d4 s4 d5 s5 d6 s6 m4 e11 e12 m5 d7 s7 h2 y20 y21 y22 m6 m7 h3 y30 y31 y32 e20 e21 e22 e30 e31 e32".split()
+GP_MULT = [1,0,0,1,0,0,0,0]
+VEC_EVAC = {"1":[0],"2":[2],"3":[1]}
+SHARE = []
+W4_ENG = ["pool","pool","pool"]
 PSUM_TAGS = {"p":["ps",8],"y":["ps",8],"feat":["ps",8]}
-RING = 4
+COUNT = {"v":38,"a":17,"g":4}
 
 
 def tile_list_replay_curiosity_bonus_kernel(
@@ -38,9 +39,8 @@ def tile_list_replay_curiosity_bonus_kernel(
     nc = tc.nc
     with ExitStack() as ctx:
         keep = ctx.enter_context(tc.tile_pool(name="keep", bufs=1))
-        ring = ctx.enter_context(tc.tile_pool(name="ring", bufs=RING))
+        line = ctx.enter_context(tc.tile_pool(name="line", bufs=1))
         psum = ctx.enter_context(tc.psum_pool(name="psum", bufs=1))
-        ctx.enter_context(nc.allow_non_contiguous_dma(reason="per-partition gains and biases"))
 
         lists = [keep.tile([P, S // 16], U16, name=f"list{x}") for x in range(3)]
         tsc = keep.tile([P, T // 4], I32, name="tsc")
@@ -49,41 +49,54 @@ def tile_list_replay_curiosity_bonus_kernel(
         nc.vector.memset(tsc[:], 0)
         nc.vector.memset(wsc_raw[:], 0)
         nc.vector.memset(shifted[:], 0)
+        rows_t = keep.tile([P, PACK, P], F32, name="rows_t")
+        nc.gpsimd.memset(rows_t[:], 0.0)
+        ident = keep.tile([P, P], F32, name="ident")
+        make_identity(nc, ident[:])
+        g_row = keep.tile([1, H], F32, name="g_row")
 
         nc.sync.dma_start(lists[1][:], offs2)
+        nc.sync.dma_start(g_row[:], g.rearrange("(o r) -> o r", o=1))
         nc.sync.dma_start(lists[0][:], offs)
-        nc.sync.dma_start(lists[2][:], offs3)
         for r in range(4):
             for a in range(PASSES):
                 rows = tab_scales[a].rearrange("(q r) n -> r q n", r=4)[r]
                 nc.sync.dma_start(tsc[4 * a + r : P : 32, :], rows.bitcast(I32))
 
+        nc.sync.dma_start(lists[2][:], offs3)
+        nc.gpsimd.dma_start(rows_t[1 : 1 + N // P, 0, :], b4.rearrange("(u p) -> u p", p=P))
+        nc.scalar.activation(
+            rows_t[0:1, :, :].rearrange("o t (c i) -> o t c i", i=4),
+            g_row[:].rearrange("o (c t i) -> o t c i", t=4, i=4),
+            ACT.Copy,
+        )
+        cols_t = psum.tile([P, PACK, P], F32, name="cols_t", tag=PSUM_TAGS["y"][0], bufs=PSUM_TAGS["y"][1])
+        for t in range(PACK):
+            nc.tensor.transpose(cols_t[:, t, :], rows_t[:, t, :], ident[:])
+        gain = keep.tile([P, PACK], F32, name="gain")
+        bias = keep.tile([P, N // P], F32, name="bias")
+        nc.scalar.copy(gain[:], cols_t[:, :, 0])
+        nc.scalar.copy(bias[:], cols_t[:, 0, 1 : 1 + N // P])
+
         words = [keep.tile([P, T], I32, name=f"words{a}") for a in range(PASSES)]
-        w1_raw = [[keep.tile([P, PACK, H // 2], F32, name=f"w1_raw{a}{b}") for b in range(2)] for a in range(PASSES)]
+        w1_raw = [keep.tile([P, PACK, H], F32, name=f"w1_raw{a}") for a in range(PASSES)]
         w2_raw = keep.tile([P, PASSES, H // 2], I32, name="w2_raw")
         w3_raw = keep.tile([P, PASSES, H], I32, name="w3_raw")
         w4_raw = keep.tile([P, PACK, N], F32, name="w4_raw")
-        g_pad = keep.tile([P, PACK, 8], F32, name="g_pad")
-        bias = keep.tile([P, N // P], F32, name="bias")
 
         seen = {"s": 0, "g": 0, "f": 0}
         for o in LOADS:
             if o in ("a0", "a1", "b0", "b1"):
                 a, b = {"a": 0, "b": 1}[o[0]], int(o[1])
                 rows = w1[512 * a : 512 * (a + 1), :].rearrange("(p j) r -> p j r", j=PACK)
-                nc.sync.dma_start(w1_raw[a][b][:], rows[:, :, 256 * b : 256 * (b + 1)])
+                nc.sync.dma_start(w1_raw[a][:], rows)
             elif o == "s":
                 w, r = divmod(seen[o], 4)
                 rows = (w2_scales, w3_scales)[w].rearrange("a (q r) n -> r q a n", r=4)[r]
                 nc.sync.dma_start(wsc_raw[4 * w + r : P : 32, :, :], rows.bitcast(I32))
-            elif o == "g":
-                t = seen[o]
-                nc.sync.dma_start(g_pad[:, t, 0:1], g.rearrange("(c t i o) -> t c i o", t=4, i=4, o=1)[t])
             elif o == "f":
                 t = seen[o]
                 nc.sync.dma_start(w4_raw[:, t, :], w4.rearrange("(c t i) n -> t c i n", t=4, i=4)[t])
-            elif o == "B":
-                nc.sync.dma_start(bias[:], b4.rearrange("(u p) -> p u", p=P))
             elif o == "w2":
                 nc.sync.dma_start(w2_raw[:], w2_words.rearrange("a p n -> p a n").bitcast(I32))
             elif o == "w3":
@@ -94,29 +107,23 @@ def tile_list_replay_curiosity_bonus_kernel(
             if o in seen:
                 seen[o] = seen[o] + 1
 
-        gsc = [keep.tile([P, S], U8, name=f"gsc{x}", align_bytes=64) for x in range(3)]
         w1_bf = [keep.tile([P, PACK, 32, 4, PACK], BF16, name=f"w1_bf{a}", align_bytes=64) for a in range(PASSES)]
-        w1q = keep.tile([P, PASSES, H], U32, name="w1q", align_bytes=64)
         w1s = keep.tile([P, PASSES, H], U8, name="w1s", align_bytes=64)
         w2p = keep.tile([P, PASSES, H // 2], I32, name="w2p", align_bytes=64)
         w3p = keep.tile([P, PASSES, H], I32, name="w3p", align_bytes=64)
         wsc = keep.tile([P, PASSES, H // 4], I32, name="wsc", align_bytes=64)
-        w4q = keep.tile([P, N], U32, name="w4q", align_bytes=64)
         w4s = keep.tile([P, N], U8, name="w4s", align_bytes=64)
-        gain = keep.tile([P, PACK], F32, name="gain")
         pred = [keep.tile([P, PACK, HALF], F32, name=f"pred{h}") for h in range(2)]
-        hq = [keep.tile([P, CHUNK * len(G)], U32, name=f"hq{i}", align_bytes=64) for i, G in enumerate(GROUPS)]
         hs = [keep.tile([P, CHUNK * len(G)], U8, name=f"hs{i}", align_bytes=64) for i, G in enumerate(GROUPS)]
         out_v = out.rearrange("(u p) j -> p u j", p=P)
 
-        nc.vector.tensor_copy(
+        nc.gpsimd.tensor_copy(
             wsc[:].rearrange("p a (t c) -> p a t c", t=4), wsc_raw[:].rearrange("p a (c t) -> p a t c", t=4)
         )
-        nc.scalar.copy(gain[:], g_pad[:, :, 0])
 
         def permute(dst, src, run):
             for a in range(PASSES):
-                nc.vector.tensor_copy(
+                nc.gpsimd.tensor_copy(
                     dst[:, a, :].rearrange("p (t c i) -> p t c i", t=4, i=run),
                     src[:, a, :].rearrange("p (c t i) -> p t c i", t=4, i=run),
                 )
@@ -124,34 +131,36 @@ def tile_list_replay_curiosity_bonus_kernel(
         def bank(kind, shape, name):
             return psum.tile(shape, F32, name=name, tag=PSUM_TAGS[kind][0], bufs=PSUM_TAGS[kind][1])
 
+        def queued(eng, shape, dtype, name):
+            return line.tile(shape, dtype, name=name, tag=eng, bufs=COUNT[eng], align_bytes=64)
+
         gw, acc, done, feat, diff, sq, hb = {}, {}, {}, {}, {}, {}, {}
+        gsc, w1q, w4q, w4_bf, hq, ys = {}, {}, {}, {}, {}, {}
         half = {"A": 0, "B": 1}
         for s in TEXT:
             k = s[0]
             if k == "S":
                 x = int(s[1])
+                gsc[x] = queued("v", [P, S], U8, s)
                 nc.vector.tensor_copy(gsc[x][:], tsc[:].bitcast(U8).indirect(lists[x][:]))
                 if x == 1:
-                    nc.scalar.dma_start(shifted[0:100, :], gsc[1][4:104, :].bitcast(I32))
+                    nc.gpsimd.dma_start(shifted[0:100, :], gsc[1][4:104, :].bitcast(I32))
             elif k == "G":
                 x, a, h = int(s[1]), int(s[2]), half[s[3]]
-                tag = s
-                for pair in SHARE:
-                    if s in pair:
-                        tag = pair[0]
-                gw[x, a, h] = keep.tile([P, HALF], U32, name=s, tag=tag, align_bytes=64)
+                gw[x, a, h] = queued("v", [P, HALF], U32, s)
                 nc.vector.tensor_copy(
                     gw[x, a, h][:], words[a][:].bitcast(U32).indirect(lists[x][:, 32 * h : 32 * (h + 1)])
                 )
             elif k == "C":
                 a = int(s[1])
-                for b in range(2):
-                    src = w1_raw[a][b][:].rearrange("p j (c t i) -> p t c j i", t=4, i=4)
-                    for t in range(PACK):
-                        dst = w1_bf[a][:, t, 16 * b : 16 * (b + 1), :, :].rearrange("p c i j -> p c j i")
-                        nc.scalar.activation(dst, src[:, t], ACT.Copy)
+                src = w1_raw[a][:].rearrange("p j (c t i) -> p t c j i", t=4, i=4)
+                for t in range(PACK):
+                    nc.scalar.activation(w1_bf[a][:, t].rearrange("p c i j -> p c j i"), src[:, t], ACT.Copy)
+            elif k == "Q":
+                a = int(s[1])
+                w1q[a] = queued("v", [P, H], U32, s)
                 nc.vector.quantize_mx(
-                    out=w1q[:, a, :].bitcast(FP8X4),
+                    out=w1q[a][:].bitcast(FP8X4),
                     scales=w1s[:, a, :],
                     in_=w1_bf[a][:].rearrange("p t c i j -> p (t c i j)"),
                 )
@@ -167,7 +176,7 @@ def tile_list_replay_curiosity_bonus_kernel(
                 cols = slice(HALF * h, HALF * (h + 1))
                 m = slice(P * t, P * (t + 1))
                 if w == 1:
-                    lhs, lhs_s = w1q[:, a, m].bitcast(FP8X4), w1s[:, a, m]
+                    lhs, lhs_s = w1q[a][:, m].bitcast(FP8X4), w1s[:, a, m]
                     rhs, rhs_s = gw[0, a, h][:], gsc[0][4 * a : P, cols]
                 else:
                     lhs = w2p[:, a, :].bitcast(U8)[:, 2 * P * t : 2 * P * (t + 1)].bitcast(FP4X4)
@@ -190,20 +199,28 @@ def tile_list_replay_curiosity_bonus_kernel(
             elif k == "f":
                 b = int(s[1])
                 cols = slice(256 * b, 256 * (b + 1))
-                w4_bf = keep.tile([P, 256, PACK], BF16, name=f"w4_bf{b}", align_bytes=64)
-                if W4_ENG[b] == "dve":
+                w4_bf[b] = queued({"dve": "v", "act": "a", "pool": "g"}[W4_ENG[b]], [P, 256, PACK], BF16, s)
+                if W4_ENG[b] == "pool":
+                    nc.gpsimd.tensor_scalar(
+                        w4_bf[b][:], w4_raw[:, :, cols].rearrange("p t n -> p n t"), 1.0, 0.0, ALU.mult, ALU.add
+                    )
+                elif W4_ENG[b] == "dve":
                     nc.vector.tensor_copy(
-                        w4_bf[:].rearrange("p (c i) t -> p c t i", i=4),
+                        w4_bf[b][:].rearrange("p (c i) t -> p c t i", i=4),
                         w4_raw[:, :, cols].rearrange("p t (c i) -> p c t i", i=4),
                     )
                 else:
                     nc.scalar.activation(
-                        w4_bf[:].rearrange("p (c i) t -> p c t i", i=4),
+                        w4_bf[b][:].rearrange("p (c i) t -> p c t i", i=4),
                         w4_raw[:, :, cols].rearrange("p t (c i) -> p c t i", i=4),
                         ACT.Copy,
                     )
+            elif k == "F":
+                b = int(s[1])
+                cols = slice(256 * b, 256 * (b + 1))
+                w4q[b] = queued("v", [P, 256], U32, s)
                 nc.vector.quantize_mx(
-                    out=w4q[:, cols].bitcast(FP8X4), scales=w4s[:, cols], in_=w4_bf[:].rearrange("p n t -> p (n t)")
+                    out=w4q[b][:].bitcast(FP8X4), scales=w4s[:, cols], in_=w4_bf[b][:].rearrange("p n t -> p (n t)")
                 )
             elif k == "q":
                 c = int(s[1])
@@ -226,11 +243,11 @@ def tile_list_replay_curiosity_bonus_kernel(
             elif k == "d":
                 c = int(s[1])
                 cols = slice(CHUNK * (c % 4), CHUNK * (c % 4 + 1))
-                diff[c] = ring.tile([P, PACK, CHUNK], F32, name="diff")
+                diff[c] = queued("v", [P, PACK, CHUNK], F32, s)
                 nc.vector.tensor_tensor(diff[c][:], pred[c // 4][:, :, cols], feat[c][:], ALU.subtract)
             elif k == "s":
                 c = int(s[1])
-                sq[c] = ring.tile([P, CHUNK, PACK], F32, name="sq")
+                sq[c] = queued("a", [P, CHUNK, PACK], F32, s)
                 nc.scalar.activation(
                     sq[c][:].rearrange("p (c i) t -> p c t i", i=4),
                     diff[c][:].rearrange("p t (c i) -> p c t i", i=4),
@@ -238,35 +255,42 @@ def tile_list_replay_curiosity_bonus_kernel(
                 )
             elif k == "m":
                 c = int(s[1])
-                hb[c] = ring.tile([P, CHUNK, PACK], BF16, name="hb", align_bytes=64)
-                eng = nc.gpsimd if GP_MULT[c] else nc.vector
-                eng.tensor_tensor(hb[c][:], sq[c][:], gain[:].unsqueeze(1).to_broadcast([P, CHUNK, PACK]), ALU.mult)
-            elif k == "h":
-                c = int(s[1])
                 gi = [i for i, G in enumerate(GROUPS) if c in G][0]
+                if gi not in hb:
+                    hb[gi] = queued("g" if GP_MULT[c] else "v", [P, CHUNK * len(GROUPS[gi]), PACK], BF16, s)
                 c0 = CHUNK * GROUPS[gi].index(c)
+                eng = nc.gpsimd if GP_MULT[c] else nc.vector
+                eng.tensor_tensor(hb[gi][:, c0 : c0 + CHUNK, :], sq[c][:], gain[:].unsqueeze(1).to_broadcast([P, CHUNK, PACK]), ALU.mult)
+            elif k == "h":
+                gi = int(s[1])
+                hq[gi] = queued("v", [P, CHUNK * len(GROUPS[gi])], U32, s)
                 nc.vector.quantize_mx(
-                    out=hq[gi][:, c0 : c0 + CHUNK].bitcast(FP8X4),
-                    scales=hs[gi][:, c0 : c0 + CHUNK],
-                    in_=hb[c][:].rearrange("p j t -> p (j t)"),
+                    out=hq[gi][:].bitcast(FP8X4),
+                    scales=hs[gi][:],
+                    in_=hb[gi][:].rearrange("p j t -> p (j t)"),
                 )
-            else:
+            elif k == "y":
                 gi, b = int(s[1]), int(s[2])
                 width = CHUNK * len(GROUPS[gi])
-                ocols = slice(CHUNK * GROUPS[gi][0], CHUNK * GROUPS[gi][0] + width)
                 y = bank("y", [P, 2, width], f"y{gi}{b}")
-                res = keep.tile([P, 2, width], F32, name=f"res{gi}{b}")
+                ys[gi, b] = y
                 for e in range(2):
                     m = slice(P * (2 * b + e), P * (2 * b + e + 1))
                     nc.tensor.matmul_mx(
                         y[:, e, :],
-                        lhsT=w4q[:, m].bitcast(FP8X4),
+                        lhsT=w4q[b][:, P * e : P * (e + 1)].bitcast(FP8X4),
                         lhsT_scale=w4s[:, m],
                         rhs=hq[gi][:].bitcast(FP8X4),
                         rhs_scale=hs[gi][:],
                         start=True,
                         stop=True,
                     )
+            else:
+                gi, b = int(s[1]), int(s[2])
+                width = CHUNK * len(GROUPS[gi])
+                ocols = slice(CHUNK * GROUPS[gi][0], CHUNK * GROUPS[gi][0] + width)
+                y = ys[gi, b]
+                res = queued("v" if b in VEC_EVAC.get(str(gi), ()) else "a", [P, 2, width], F32, s)
                 if b in VEC_EVAC.get(str(gi), ()):
                     nc.vector.tensor_tensor(
                         res[:], y[:], bias[:, 2 * b : 2 * b + 2].unsqueeze(2).to_broadcast([P, 2, width]), ALU.add

@@ -22,15 +22,10 @@ PACK = 4
 PASSES = 2
 HALF = 512
 CHUNK = 128
-GROUPS = [[0,1],[2,3],[4,5],[6,7]]
-LOADS = "w2 s s a0 s s W0 s s b0 s s W1 w3 f f f f".split()
-TEXT = "S0 S1 S2 P2 C0 C1 P3 G00A G10A G20A G00B Q0 Q1 p20A0 p10A0 p20A1 p10A1 p20A2 p10A2 p20A3 p10A3 G01A G11A p11A0 p21A0 tA0 p11A1 p21A1 tA1 p11A2 p21A2 tA2 p11A3 p21A3 tA3 G10B G21A q0 q1 q2 q3 G11B d0 s0 G01B f0 f1 f2 d1 s1 d2 s2 d3 s3 p10B0 p20B0 p11B0 p21B0 tB0 p10B1 p20B1 p11B1 p21B1 tB1 p10B2 p20B2 p11B2 p21B2 tB2 p10B3 p20B3 p11B3 p21B3 tB3 m0 m1 F0 F1 F2 h0 y00 y01 y02 G20B m2 m3 h1 e00 e01 e02 G21B y10 y11 y12 q4 q5 q6 q7 e10 d4 s4 d5 s5 d6 s6 m4 e11 e12 m5 d7 s7 h2 y20 y21 y22 m6 m7 h3 y30 y31 y32 e20 e21 e22 e30 e31 e32".split()
-GP_MULT = [1,0,0,1,0,0,0,0]
-VEC_EVAC = {"1":[0],"2":[2],"3":[1]}
-SHARE = []
-W4_ENG = ["pool","pool","pool"]
-PSUM_TAGS = {"p":["ps",8],"y":["ps",8],"feat":["ps",8]}
-COUNT = {"v":38,"a":17,"g":4}
+GROUP = 256
+STATE, ACTION, NEXT = 0, 1, 2
+A, B = 0, 1
+QUEUE_BUFS = {"vector": 30, "scalar": 9, "gpsimd": 10}
 
 
 def tile_list_replay_curiosity_bonus_kernel(
@@ -42,261 +37,301 @@ def tile_list_replay_curiosity_bonus_kernel(
         line = ctx.enter_context(tc.tile_pool(name="line", bufs=1))
         psum = ctx.enter_context(tc.psum_pool(name="psum", bufs=1))
 
+        def bank(shape, name):
+            return psum.tile(shape, F32, name=name, tag="bank", bufs=8)
+
+        def queued(eng, shape, dtype, name):
+            return line.tile(shape, dtype, name=name, tag=eng, bufs=QUEUE_BUFS[eng], align_bytes=64)
+
         lists = [keep.tile([P, S // 16], U16, name=f"list{x}") for x in range(3)]
         tsc = keep.tile([P, T // 4], I32, name="tsc")
-        wsc_raw = keep.tile([P, PASSES, H // 4], I32, name="wsc_raw")
+        wsc_raw = {w: keep.tile([P, PASSES, H // 4], I32, name=f"wsc_raw{w}") for w in (2, 3)}
         shifted = keep.tile([P, S // 4], I32, name="shifted", align_bytes=64)
-        nc.vector.memset(tsc[:], 0)
-        nc.vector.memset(wsc_raw[:], 0)
+        nc.gpsimd.memset(tsc[:, 0:640], 0)
+        nc.vector.memset(tsc[:, 640:], 0)
+        nc.vector.memset(wsc_raw[2][:], 0)
         nc.vector.memset(shifted[:], 0)
-        rows_t = keep.tile([P, PACK, P], F32, name="rows_t")
-        nc.gpsimd.memset(rows_t[:], 0.0)
+        nc.vector.memset(wsc_raw[3][:], 0)
+        rows = keep.tile([P, P], F32, name="rows")
+        nc.gpsimd.memset(rows[:], 0.0)
+        nc.gpsimd.dma_start(
+            rows[0:PACK, :].rearrange("t (c i) -> t c i", i=4), g.rearrange("(c t i) -> t c i", t=4, i=4)
+        )
+        nc.gpsimd.dma_start(rows[PACK : PACK + N // P, :], b4.rearrange("(u p) -> u p", p=P))
         ident = keep.tile([P, P], F32, name="ident")
         make_identity(nc, ident[:])
-        g_row = keep.tile([1, H], F32, name="g_row")
-
-        nc.sync.dma_start(lists[1][:], offs2)
-        nc.sync.dma_start(g_row[:], g.rearrange("(o r) -> o r", o=1))
-        nc.sync.dma_start(lists[0][:], offs)
-        for r in range(4):
-            for a in range(PASSES):
-                rows = tab_scales[a].rearrange("(q r) n -> r q n", r=4)[r]
-                nc.sync.dma_start(tsc[4 * a + r : P : 32, :], rows.bitcast(I32))
-
-        nc.sync.dma_start(lists[2][:], offs3)
-        nc.gpsimd.dma_start(rows_t[1 : 1 + N // P, 0, :], b4.rearrange("(u p) -> u p", p=P))
-        nc.scalar.activation(
-            rows_t[0:1, :, :].rearrange("o t (c i) -> o t c i", i=4),
-            g_row[:].rearrange("o (c t i) -> o t c i", t=4, i=4),
-            ACT.Copy,
-        )
-        cols_t = psum.tile([P, PACK, P], F32, name="cols_t", tag=PSUM_TAGS["y"][0], bufs=PSUM_TAGS["y"][1])
-        for t in range(PACK):
-            nc.tensor.transpose(cols_t[:, t, :], rows_t[:, t, :], ident[:])
-        gain = keep.tile([P, PACK], F32, name="gain")
-        bias = keep.tile([P, N // P], F32, name="bias")
-        nc.scalar.copy(gain[:], cols_t[:, :, 0])
-        nc.scalar.copy(bias[:], cols_t[:, 0, 1 : 1 + N // P])
+        cols = bank([P, P], "cols")
+        nc.tensor.transpose(cols[:], rows[:], ident[:])
+        consts = keep.tile([P, 16], F32, name="consts")
+        nc.scalar.activation(consts[:], cols[:, 0:16], ACT.Copy)
+        gain = consts[:, 0:PACK]
 
         words = [keep.tile([P, T], I32, name=f"words{a}") for a in range(PASSES)]
         w1_raw = [keep.tile([P, PACK, H], F32, name=f"w1_raw{a}") for a in range(PASSES)]
         w2_raw = keep.tile([P, PASSES, H // 2], I32, name="w2_raw")
         w3_raw = keep.tile([P, PASSES, H], I32, name="w3_raw")
-        w4_raw = keep.tile([P, PACK, N], F32, name="w4_raw")
+        w4_raw = [keep.tile([P, PACK, 256], F32, name=f"w4_raw{b}") for b in range(3)]
 
-        seen = {"s": 0, "g": 0, "f": 0}
-        for o in LOADS:
-            if o in ("a0", "a1", "b0", "b1"):
-                a, b = {"a": 0, "b": 1}[o[0]], int(o[1])
-                rows = w1[512 * a : 512 * (a + 1), :].rearrange("(p j) r -> p j r", j=PACK)
-                nc.sync.dma_start(w1_raw[a][:], rows)
-            elif o == "s":
-                w, r = divmod(seen[o], 4)
-                rows = (w2_scales, w3_scales)[w].rearrange("a (q r) n -> r q a n", r=4)[r]
-                nc.sync.dma_start(wsc_raw[4 * w + r : P : 32, :, :], rows.bitcast(I32))
-            elif o == "f":
-                t = seen[o]
-                nc.sync.dma_start(w4_raw[:, t, :], w4.rearrange("(c t i) n -> t c i n", t=4, i=4)[t])
-            elif o == "w2":
-                nc.sync.dma_start(w2_raw[:], w2_words.rearrange("a p n -> p a n").bitcast(I32))
-            elif o == "w3":
-                nc.sync.dma_start(w3_raw[:], w3_words.rearrange("a p n i -> p a (n i)").bitcast(I32))
-            else:
-                a = int(o[1])
-                nc.sync.dma_start(words[a][:], tab_words[a].rearrange("p t i -> p (t i)").bitcast(I32))
-            if o in seen:
-                seen[o] = seen[o] + 1
+        def load_words(a):
+            nc.sync.dma_start(words[a][:], tab_words[a].rearrange("p t i -> p (t i)").bitcast(I32))
 
-        w1_bf = [keep.tile([P, PACK, 32, 4, PACK], BF16, name=f"w1_bf{a}", align_bytes=64) for a in range(PASSES)]
+        def load_w1(a):
+            nc.sync.dma_start(w1_raw[a][:], w1[512 * a : 512 * (a + 1), :].rearrange("(p j) r -> p j r", j=PACK))
+
+        def load_weight_scales(w, scales):
+            for r in range(4):
+                nc.sync.dma_start(
+                    wsc_raw[w][r:P:32, :, :], scales.rearrange("a (q r) n -> r q a n", r=4)[r].bitcast(I32)
+                )
+
+        nc.sync.dma_start(lists[ACTION][:], offs2)
+        nc.sync.dma_start(lists[STATE][:], offs)
+        for r in range(4):
+            for a in range(PASSES):
+                scale_rows = tab_scales[a].rearrange("(q r) n -> r q n", r=4)[r]
+                nc.sync.dma_start(tsc[4 * a + r : P : 32, :], scale_rows.bitcast(I32))
+        load_words(0)
+        nc.sync.dma_start(lists[NEXT][:], offs3)
+        load_weight_scales(2, w2_scales)
+        nc.sync.dma_start(w2_raw[:], w2_words.rearrange("a p n -> p a n").bitcast(I32))
+        load_w1(0)
+        load_words(1)
+        load_w1(1)
+        load_weight_scales(3, w3_scales)
+        nc.sync.dma_start(w3_raw[:], w3_words.rearrange("a p n i -> p a (n i)").bitcast(I32))
+        for b in range(3):
+            for t in range(PACK):
+                nc.sync.dma_start(
+                    w4_raw[b][:, t, :], w4[:, 256 * b : 256 * (b + 1)].rearrange("(c t i) n -> t c i n", t=4, i=4)[t]
+                )
+
         w1s = keep.tile([P, PASSES, H], U8, name="w1s", align_bytes=64)
-        w2p = keep.tile([P, PASSES, H // 2], I32, name="w2p", align_bytes=64)
-        w3p = keep.tile([P, PASSES, H], I32, name="w3p", align_bytes=64)
-        wsc = keep.tile([P, PASSES, H // 4], I32, name="wsc", align_bytes=64)
         w4s = keep.tile([P, N], U8, name="w4s", align_bytes=64)
-        pred = [keep.tile([P, PACK, HALF], F32, name=f"pred{h}") for h in range(2)]
-        hs = [keep.tile([P, CHUNK * len(G)], U8, name=f"hs{i}", align_bytes=64) for i, G in enumerate(GROUPS)]
+        hs = [keep.tile([P, GROUP], U8, name=f"hs{i}", align_bytes=64) for i in range(S // GROUP)]
         out_v = out.rearrange("(u p) j -> p u j", p=P)
 
-        nc.gpsimd.tensor_copy(
-            wsc[:].rearrange("p a (t c) -> p a t c", t=4), wsc_raw[:].rearrange("p a (c t) -> p a t c", t=4)
-        )
+        gsc, gw, w1_bf, w1q, wp, wsc, acc, done = {}, {}, {}, {}, {}, {}, {}, {}
+        pred, feat, diff, sq, hb, hq, w4_bf, w4q, ys = {}, {}, {}, {}, {}, {}, {}, {}, {}
 
-        def permute(dst, src, run):
+        def reorder_scales(w):
+            wsc[w] = queued("gpsimd", [P, PASSES, H // 4], I32, f"wsc{w}")
+            nc.gpsimd.tensor_copy(
+                wsc[w][:].rearrange("p a (t c) -> p a t c", t=4), wsc_raw[w][:].rearrange("p a (c t) -> p a t c", t=4)
+            )
+
+        def reorder_words(w, raw, run):
             for a in range(PASSES):
+                wp[w, a] = queued("gpsimd", [P, P * run], I32, f"wp{w}{a}")
                 nc.gpsimd.tensor_copy(
-                    dst[:, a, :].rearrange("p (t c i) -> p t c i", t=4, i=run),
-                    src[:, a, :].rearrange("p (c t i) -> p t c i", t=4, i=run),
+                    wp[w, a][:].rearrange("p (t c i) -> p t c i", t=4, i=run),
+                    raw[:, a, :].rearrange("p (c t i) -> p t c i", t=4, i=run),
                 )
 
-        def bank(kind, shape, name):
-            return psum.tile(shape, F32, name=name, tag=PSUM_TAGS[kind][0], bufs=PSUM_TAGS[kind][1])
+        def gather_scales(x):
+            gsc[x] = queued("vector", [P, S], U8, f"gsc{x}")
+            nc.vector.tensor_copy(gsc[x][:], tsc[:].bitcast(U8).indirect(lists[x][:]))
 
-        def queued(eng, shape, dtype, name):
-            return line.tile(shape, dtype, name=name, tag=eng, bufs=COUNT[eng], align_bytes=64)
+        def gather_words(x, a, h):
+            gw[x, a, h] = queued("vector", [P, HALF], U32, f"gw{x}{a}{h}")
+            nc.vector.tensor_copy(
+                gw[x, a, h][:], words[a][:].bitcast(U32).indirect(lists[x][:, 32 * h : 32 * (h + 1)])
+            )
 
-        gw, acc, done, feat, diff, sq, hb = {}, {}, {}, {}, {}, {}, {}
-        gsc, w1q, w4q, w4_bf, hq, ys = {}, {}, {}, {}, {}, {}
-        half = {"A": 0, "B": 1}
-        for s in TEXT:
-            k = s[0]
-            if k == "S":
-                x = int(s[1])
-                gsc[x] = queued("v", [P, S], U8, s)
-                nc.vector.tensor_copy(gsc[x][:], tsc[:].bitcast(U8).indirect(lists[x][:]))
-                if x == 1:
-                    nc.gpsimd.dma_start(shifted[0:100, :], gsc[1][4:104, :].bitcast(I32))
-            elif k == "G":
-                x, a, h = int(s[1]), int(s[2]), half[s[3]]
-                gw[x, a, h] = queued("v", [P, HALF], U32, s)
-                nc.vector.tensor_copy(
-                    gw[x, a, h][:], words[a][:].bitcast(U32).indirect(lists[x][:, 32 * h : 32 * (h + 1)])
-                )
-            elif k == "C":
-                a = int(s[1])
+        def round_w1(a, on_gpsimd=0):
+            for t in range(PACK - on_gpsimd):
+                w1_bf[a, t] = queued("scalar", [P, 32, 4, PACK], BF16, f"w1_bf{a}{t}")
                 src = w1_raw[a][:].rearrange("p j (c t i) -> p t c j i", t=4, i=4)
-                for t in range(PACK):
-                    nc.scalar.activation(w1_bf[a][:, t].rearrange("p c i j -> p c j i"), src[:, t], ACT.Copy)
-            elif k == "Q":
-                a = int(s[1])
-                w1q[a] = queued("v", [P, H], U32, s)
+                nc.scalar.activation(w1_bf[a, t][:].rearrange("p c i j -> p c j i"), src[:, t], ACT.Copy)
+            for t in range(PACK - on_gpsimd, PACK):
+                w1_bf[a, t] = queued("gpsimd", [P, 32, 4, PACK], BF16, f"w1_bf{a}{t}")
+                src = w1_raw[a][:].rearrange("p j (c t i) -> p t c i j", t=4, i=4)
+                nc.gpsimd.tensor_scalar(w1_bf[a, t][:], src[:, t], 1.0, 0.0, ALU.mult, ALU.add)
+
+        def quantize_w1(a):
+            for t in range(PACK):
+                w1q[a, t] = queued("vector", [P, P], U32, f"w1q{a}{t}")
                 nc.vector.quantize_mx(
-                    out=w1q[a][:].bitcast(FP8X4),
-                    scales=w1s[:, a, :],
-                    in_=w1_bf[a][:].rearrange("p t c i j -> p (t c i j)"),
+                    out=w1q[a, t][:].bitcast(FP8X4),
+                    scales=w1s[:, a, P * t : P * (t + 1)],
+                    in_=w1_bf[a, t][:].rearrange("p c i j -> p (c i j)"),
                 )
-            elif s == "P2":
-                permute(w2p, w2_raw, 2)
-            elif s == "P3":
-                permute(w3p, w3_raw, 4)
-            elif k == "p":
-                w, a, h, t = int(s[1]), int(s[2]), half[s[3]], int(s[4])
+
+        def p_pass(x, a, h):
+            tok = slice(HALF * h, HALF * (h + 1))
+            for t in range(PACK):
                 if (h, t) not in acc:
-                    acc[h, t] = bank("p", [P, HALF], f"acc{h}{t}")
+                    acc[h, t] = bank([P, HALF], f"acc{h}{t}")
                     done[h, t] = 0
-                cols = slice(HALF * h, HALF * (h + 1))
                 m = slice(P * t, P * (t + 1))
-                if w == 1:
-                    lhs, lhs_s = w1q[a][:, m].bitcast(FP8X4), w1s[:, a, m]
-                    rhs, rhs_s = gw[0, a, h][:], gsc[0][4 * a : P, cols]
+                if x == STATE:
+                    lhs, lhs_s = w1q[a, t][:].bitcast(FP8X4), w1s[:, a, m]
+                    rhs_s = gsc[STATE][4 * a : P, tok]
                 else:
-                    lhs = w2p[:, a, :].bitcast(U8)[:, 2 * P * t : 2 * P * (t + 1)].bitcast(FP4X4)
-                    lhs_s = wsc[:, a, :].bitcast(U8)[:, m]
-                    rhs = gw[1, a, h][:]
-                    rhs_s = gsc[1][:, cols] if a == 0 else shifted[:].bitcast(U8)[:, cols]
+                    lhs = wp[2, a][:].bitcast(U8)[:, 2 * P * t : 2 * P * (t + 1)].bitcast(FP4X4)
+                    lhs_s = wsc[2][:, a, :].bitcast(U8)[:, m]
+                    rhs_s = gsc[ACTION][:, tok] if a == 0 else shifted[:].bitcast(U8)[:, tok]
                 nc.tensor.matmul_mx(
                     acc[h, t][:],
                     lhsT=lhs,
                     lhsT_scale=lhs_s,
-                    rhs=rhs.bitcast(FP8X4),
+                    rhs=gw[x, a, h][:].bitcast(FP8X4),
                     rhs_scale=rhs_s,
                     start=(done[h, t] == 0),
-                    stop=(done[h, t] == 3),
+                    stop=(done[h, t] == 2 * PASSES - 1),
                 )
                 done[h, t] = done[h, t] + 1
-            elif k == "t":
-                h, t = half[s[1]], int(s[2])
+
+        def predict(h):
+            pred[h] = queued("scalar", [P, PACK, HALF], F32, f"pred{h}")
+            for t in range(PACK):
                 nc.scalar.activation(pred[h][:, t, :], acc[h, t][:], ACT.Tanh)
-            elif k == "f":
-                b = int(s[1])
-                cols = slice(256 * b, 256 * (b + 1))
-                w4_bf[b] = queued({"dve": "v", "act": "a", "pool": "g"}[W4_ENG[b]], [P, 256, PACK], BF16, s)
-                if W4_ENG[b] == "pool":
-                    nc.gpsimd.tensor_scalar(
-                        w4_bf[b][:], w4_raw[:, :, cols].rearrange("p t n -> p n t"), 1.0, 0.0, ALU.mult, ALU.add
-                    )
-                elif W4_ENG[b] == "dve":
-                    nc.vector.tensor_copy(
-                        w4_bf[b][:].rearrange("p (c i) t -> p c t i", i=4),
-                        w4_raw[:, :, cols].rearrange("p t (c i) -> p c t i", i=4),
-                    )
-                else:
-                    nc.scalar.activation(
-                        w4_bf[b][:].rearrange("p (c i) t -> p c t i", i=4),
-                        w4_raw[:, :, cols].rearrange("p t (c i) -> p c t i", i=4),
-                        ACT.Copy,
-                    )
-            elif k == "F":
-                b = int(s[1])
-                cols = slice(256 * b, 256 * (b + 1))
-                w4q[b] = queued("v", [P, 256], U32, s)
-                nc.vector.quantize_mx(
-                    out=w4q[b][:].bitcast(FP8X4), scales=w4s[:, cols], in_=w4_bf[b][:].rearrange("p n t -> p (n t)")
-                )
-            elif k == "q":
-                c = int(s[1])
-                h = c // 4
-                cols = slice(CHUNK * (c % 4), CHUNK * (c % 4 + 1))
-                gcols = slice(CHUNK * c, CHUNK * (c + 1))
-                feat[c] = bank("feat", [P, PACK, CHUNK], f"feat{c}")
-                for t in range(PACK):
-                    m = slice(P * t, P * (t + 1))
-                    for a in range(PASSES):
-                        nc.tensor.matmul_mx(
-                            feat[c][:, t, :],
-                            lhsT=w3p[:, a, m].bitcast(FP8X4),
-                            lhsT_scale=wsc[4:P, a, :].bitcast(U8)[:, m],
-                            rhs=gw[2, a, h][:, cols].bitcast(FP8X4),
-                            rhs_scale=gsc[2][4 * a : P, gcols],
-                            start=(a == 0),
-                            stop=(a == PASSES - 1),
-                        )
-            elif k == "d":
-                c = int(s[1])
-                cols = slice(CHUNK * (c % 4), CHUNK * (c % 4 + 1))
-                diff[c] = queued("v", [P, PACK, CHUNK], F32, s)
-                nc.vector.tensor_tensor(diff[c][:], pred[c // 4][:, :, cols], feat[c][:], ALU.subtract)
-            elif k == "s":
-                c = int(s[1])
-                sq[c] = queued("a", [P, CHUNK, PACK], F32, s)
-                nc.scalar.activation(
-                    sq[c][:].rearrange("p (c i) t -> p c t i", i=4),
-                    diff[c][:].rearrange("p t (c i) -> p c t i", i=4),
-                    ACT.Square,
-                )
-            elif k == "m":
-                c = int(s[1])
-                gi = [i for i, G in enumerate(GROUPS) if c in G][0]
-                if gi not in hb:
-                    hb[gi] = queued("g" if GP_MULT[c] else "v", [P, CHUNK * len(GROUPS[gi]), PACK], BF16, s)
-                c0 = CHUNK * GROUPS[gi].index(c)
-                eng = nc.gpsimd if GP_MULT[c] else nc.vector
-                eng.tensor_tensor(hb[gi][:, c0 : c0 + CHUNK, :], sq[c][:], gain[:].unsqueeze(1).to_broadcast([P, CHUNK, PACK]), ALU.mult)
-            elif k == "h":
-                gi = int(s[1])
-                hq[gi] = queued("v", [P, CHUNK * len(GROUPS[gi])], U32, s)
-                nc.vector.quantize_mx(
-                    out=hq[gi][:].bitcast(FP8X4),
-                    scales=hs[gi][:],
-                    in_=hb[gi][:].rearrange("p j t -> p (j t)"),
-                )
-            elif k == "y":
-                gi, b = int(s[1]), int(s[2])
-                width = CHUNK * len(GROUPS[gi])
-                y = bank("y", [P, 2, width], f"y{gi}{b}")
-                ys[gi, b] = y
-                for e in range(2):
-                    m = slice(P * (2 * b + e), P * (2 * b + e + 1))
+
+        def round_w4(b):
+            w4_bf[b] = queued("gpsimd", [P, 256, PACK], BF16, f"w4_bf{b}")
+            nc.gpsimd.tensor_scalar(
+                w4_bf[b][:], w4_raw[b][:].rearrange("p t n -> p n t"), 1.0, 0.0, ALU.mult, ALU.add
+            )
+
+        def quantize_w4(b):
+            w4q[b] = queued("vector", [P, 256], U32, f"w4q{b}")
+            nc.vector.quantize_mx(
+                out=w4q[b][:].bitcast(FP8X4),
+                scales=w4s[:, 256 * b : 256 * (b + 1)],
+                in_=w4_bf[b][:].rearrange("p n t -> p (n t)"),
+            )
+
+        def features(c):
+            h = c // 4
+            feat[c] = bank([P, PACK, CHUNK], f"feat{c}")
+            for t in range(PACK):
+                m = slice(P * t, P * (t + 1))
+                for a in range(PASSES):
                     nc.tensor.matmul_mx(
-                        y[:, e, :],
+                        feat[c][:, t, :],
+                        lhsT=wp[3, a][:, m].bitcast(FP8X4),
+                        lhsT_scale=wsc[3][:, a, :].bitcast(U8)[:, m],
+                        rhs=gw[NEXT, a, h][:, CHUNK * (c % 4) : CHUNK * (c % 4 + 1)].bitcast(FP8X4),
+                        rhs_scale=gsc[NEXT][4 * a : P, CHUNK * c : CHUNK * (c + 1)],
+                        start=(a == 0),
+                        stop=(a == PASSES - 1),
+                    )
+
+        def subtract(c):
+            diff[c] = queued("vector", [P, PACK, CHUNK], F32, f"diff{c}")
+            nc.vector.tensor_tensor(
+                diff[c][:], pred[c // 4][:, :, CHUNK * (c % 4) : CHUNK * (c % 4 + 1)], feat[c][:], ALU.subtract
+            )
+
+        def square(c):
+            sq[c] = queued("scalar", [P, CHUNK, PACK], F32, f"sq{c}")
+            nc.scalar.activation(
+                sq[c][:].rearrange("p (c i) t -> p c t i", i=4),
+                diff[c][:].rearrange("p t (c i) -> p c t i", i=4),
+                ACT.Square,
+            )
+
+        def weigh(c, eng):
+            gi = c // 2
+            if gi not in hb:
+                hb[gi] = queued(eng, [P, GROUP, PACK], BF16, f"hb{gi}")
+            c0 = CHUNK * (c % 2)
+            engine = nc.gpsimd if eng == "gpsimd" else nc.vector
+            engine.tensor_tensor(
+                hb[gi][:, c0 : c0 + CHUNK, :], sq[c][:], gain.unsqueeze(1).to_broadcast([P, CHUNK, PACK]), ALU.mult
+            )
+
+        def quantize_h(gi):
+            hq[gi] = queued("vector", [P, GROUP], U32, f"hq{gi}")
+            nc.vector.quantize_mx(
+                out=hq[gi][:].bitcast(FP8X4), scales=hs[gi][:], in_=hb[gi][:].rearrange("p j t -> p (j t)")
+            )
+
+        def readout(gi):
+            for b in range(3):
+                ys[gi, b] = bank([P, 2, GROUP], f"y{gi}{b}")
+                for e in range(2):
+                    nc.tensor.matmul_mx(
+                        ys[gi, b][:, e, :],
                         lhsT=w4q[b][:, P * e : P * (e + 1)].bitcast(FP8X4),
-                        lhsT_scale=w4s[:, m],
+                        lhsT_scale=w4s[:, P * (2 * b + e) : P * (2 * b + e + 1)],
                         rhs=hq[gi][:].bitcast(FP8X4),
                         rhs_scale=hs[gi][:],
                         start=True,
                         stop=True,
                     )
+
+        def finish(gi, b, eng):
+            res = queued(eng, [P, 2, GROUP], F32, f"res{gi}{b}")
+            bias = consts[:, PACK + 2 * b : PACK + 2 * b + 2]
+            if eng == "vector":
+                nc.vector.tensor_tensor(res[:], ys[gi, b][:], bias.unsqueeze(2).to_broadcast([P, 2, GROUP]), ALU.add)
             else:
-                gi, b = int(s[1]), int(s[2])
-                width = CHUNK * len(GROUPS[gi])
-                ocols = slice(CHUNK * GROUPS[gi][0], CHUNK * GROUPS[gi][0] + width)
-                y = ys[gi, b]
-                res = queued("v" if b in VEC_EVAC.get(str(gi), ()) else "a", [P, 2, width], F32, s)
-                if b in VEC_EVAC.get(str(gi), ()):
-                    nc.vector.tensor_tensor(
-                        res[:], y[:], bias[:, 2 * b : 2 * b + 2].unsqueeze(2).to_broadcast([P, 2, width]), ALU.add
-                    )
-                else:
-                    for e in range(2):
-                        u = 2 * b + e
-                        nc.scalar.activation(res[:, e, :], y[:, e, :], ACT.Identity, bias=bias[:, u : u + 1])
-                nc.sync.dma_start(out_v[:, 2 * b : 2 * b + 2, ocols], res[:])
+                for e in range(2):
+                    nc.scalar.activation(res[:, e, :], ys[gi, b][:, e, :], ACT.Identity, bias=bias[:, e : e + 1])
+            nc.sync.dma_start(out_v[:, 2 * b : 2 * b + 2, GROUP * gi : GROUP * (gi + 1)], res[:])
+
+        gather_scales(ACTION)
+        nc.gpsimd.dma_start(shifted[0:100, :], gsc[ACTION][4:104, :].bitcast(I32))
+        gather_scales(STATE)
+        reorder_scales(2)
+        reorder_words(2, w2_raw, 2)
+        gather_words(ACTION, 0, A)
+        gather_words(ACTION, 0, B)
+        for h in (A, B):
+            p_pass(ACTION, 0, h)
+        gather_words(STATE, 0, A)
+        gather_words(NEXT, 0, A)
+        round_w1(0)
+        gather_scales(NEXT)
+        quantize_w1(0)
+        p_pass(STATE, 0, A)
+        gather_words(ACTION, 1, A)
+        p_pass(ACTION, 1, A)
+        gather_words(STATE, 1, A)
+        gather_words(NEXT, 1, A)
+        round_w1(1, 2)
+        quantize_w1(1)
+        p_pass(STATE, 1, A)
+        predict(A)
+        reorder_scales(3)
+        reorder_words(3, w3_raw, 4)
+        gather_words(STATE, 0, B)
+        p_pass(STATE, 0, B)
+        for c in range(3):
+            features(c)
+        gather_words(ACTION, 1, B)
+        p_pass(ACTION, 1, B)
+        gather_words(STATE, 1, B)
+        p_pass(STATE, 1, B)
+        features(3)
+        for b in range(3):
+            round_w4(b)
+        for step in range(10):
+            if step == 3:
+                predict(B)
+                gather_words(NEXT, 0, B)
+                gather_words(NEXT, 1, B)
+                features(4)
+            if step in (3, 4, 5):
+                features(step + 2)
+            if step < 8:
+                subtract(step)
+                square(step)
+            if step < 7:
+                weigh(step, "gpsimd")
+            if step == 3:
+                for b in range(3):
+                    quantize_w4(b)
+            gi = (step - 3) // 2
+            if step >= 3 and step % 2 == 1:
+                quantize_h(gi)
+                readout(gi)
+                if gi > 0:
+                    finish(gi - 1, 2, "scalar" if gi < 3 else "vector")
+            if step >= 4 and step % 2 == 0:
+                finish(gi, 0, "scalar")
+                if step == 8:
+                    weigh(7, "vector")
+                finish(gi, 1, "vector" if step < 8 else "scalar")
+        for b in range(3):
+            finish(3, b, ("scalar", "vector")[b % 2])

@@ -45,32 +45,31 @@ def tile_list_replay_curiosity_bonus_kernel(
 
         lists = [keep.tile([P, S // 16], U16, name=f"list{x}") for x in range(3)]
         tsc = keep.tile([P, T // 4], I32, name="tsc")
+        picked = keep.tile([P, 3 * S], U8, name="picked")
+        runs = [(0, STATE, NEXT), (1, STATE, NEXT + 1), (0, NEXT, NEXT + 1)]
+        planes = {
+            run: keep.tile([P, S // 4 * (run[2] - run[1])], I32, name=f"planes{i}", align_bytes=64)
+            for i, run in enumerate(runs)
+        }
         wsc_raw = {w: keep.tile([P, PASSES, H // 4], I32, name=f"wsc_raw{w}") for w in (2, 3)}
-        shifted = keep.tile([P, S // 4], I32, name="shifted", align_bytes=64)
         nc.gpsimd.memset(tsc[:, 0:640], 0)
         nc.vector.memset(tsc[:, 640:], 0)
         nc.vector.memset(wsc_raw[2][:], 0)
-        nc.vector.memset(shifted[:], 0)
         nc.vector.memset(wsc_raw[3][:], 0)
+        for run in runs:
+            nc.vector.memset(planes[run][:], 0)
         rows = keep.tile([P, P], F32, name="rows")
         nc.gpsimd.memset(rows[:], 0.0)
-        nc.gpsimd.dma_start(
-            rows[0:PACK, :].rearrange("t (c i) -> t c i", i=4), g.rearrange("(c t i) -> t c i", t=4, i=4)
-        )
-        nc.gpsimd.dma_start(rows[PACK : PACK + N // P, :], b4.rearrange("(u p) -> u p", p=P))
         ident = keep.tile([P, P], F32, name="ident")
         make_identity(nc, ident[:])
-        cols = bank([P, P], "cols")
-        nc.tensor.transpose(cols[:], rows[:], ident[:])
         consts = keep.tile([P, 16], F32, name="consts")
-        nc.scalar.activation(consts[:], cols[:, 0:16], ACT.Copy)
         gain = consts[:, 0:PACK]
 
         words = [keep.tile([P, T], I32, name=f"words{a}") for a in range(PASSES)]
         w1_raw = [keep.tile([P, PACK, H], F32, name=f"w1_raw{a}") for a in range(PASSES)]
         w2_raw = keep.tile([P, PASSES, H // 2], I32, name="w2_raw")
         w3_raw = keep.tile([P, PASSES, H], I32, name="w3_raw")
-        w4_raw = [keep.tile([P, PACK, 256], F32, name=f"w4_raw{b}") for b in range(3)]
+        w4_raw = keep.tile([P, PACK, N], F32, name="w4_raw")
 
         def load_words(a):
             nc.sync.dma_start(words[a][:], tab_words[a].rearrange("p t i -> p (t i)").bitcast(I32))
@@ -80,37 +79,31 @@ def tile_list_replay_curiosity_bonus_kernel(
 
         def load_weight_scales(w, scales):
             for r in range(4):
-                nc.sync.dma_start(
+                nc.gpsimd.dma_start(
                     wsc_raw[w][r:P:32, :, :], scales.rearrange("a (q r) n -> r q a n", r=4)[r].bitcast(I32)
                 )
 
         nc.sync.dma_start(lists[ACTION][:], offs2)
         nc.sync.dma_start(lists[STATE][:], offs)
-        for r in range(4):
-            for a in range(PASSES):
-                scale_rows = tab_scales[a].rearrange("(q r) n -> r q n", r=4)[r]
-                nc.sync.dma_start(tsc[4 * a + r : P : 32, :], scale_rows.bitcast(I32))
-        load_words(0)
+        nc.sync.dma_start(tsc[0:P:4, :], tab_scales.rearrange("a q n -> (a q) n").bitcast(I32))
         nc.sync.dma_start(lists[NEXT][:], offs3)
         load_weight_scales(2, w2_scales)
+        load_weight_scales(3, w3_scales)
+        load_words(0)
+        nc.sync.dma_start(
+            rows[0:PACK, :].rearrange("t (c i) -> t c i", i=4), g.rearrange("(c t i) -> t c i", t=4, i=4)
+        )
+        nc.sync.dma_start(rows[PACK : PACK + N // P, :], b4.rearrange("(u p) -> u p", p=P))
         nc.sync.dma_start(w2_raw[:], w2_words.rearrange("a p n -> p a n").bitcast(I32))
         load_w1(0)
-        load_words(1)
         load_w1(1)
-        load_weight_scales(3, w3_scales)
-        nc.sync.dma_start(w3_raw[:], w3_words.rearrange("a p n i -> p a (n i)").bitcast(I32))
-        for b in range(3):
-            for t in range(PACK):
-                nc.sync.dma_start(
-                    w4_raw[b][:, t, :], w4[:, 256 * b : 256 * (b + 1)].rearrange("(c t i) n -> t c i n", t=4, i=4)[t]
-                )
 
         w1s = keep.tile([P, PASSES, H], U8, name="w1s", align_bytes=64)
         w4s = keep.tile([P, N], U8, name="w4s", align_bytes=64)
         hs = [keep.tile([P, GROUP], U8, name=f"hs{i}", align_bytes=64) for i in range(S // GROUP)]
         out_v = out.rearrange("(u p) j -> p u j", p=P)
 
-        gsc, gw, w1_bf, w1q, wp, wsc, acc, done = {}, {}, {}, {}, {}, {}, {}, {}
+        gw, w1_bf, w1q, wp, wsc, acc, done = {}, {}, {}, {}, {}, {}, {}
         pred, feat, diff, sq, hb, hq, w4_bf, w4q, ys = {}, {}, {}, {}, {}, {}, {}, {}, {}
 
         def reorder_scales(w):
@@ -128,8 +121,31 @@ def tile_list_replay_curiosity_bonus_kernel(
                 )
 
         def gather_scales(x):
-            gsc[x] = queued("vector", [P, S], U8, f"gsc{x}")
-            nc.vector.tensor_copy(gsc[x][:], tsc[:].bitcast(U8).indirect(lists[x][:]))
+            nc.vector.tensor_copy(picked[:, S * x : S * (x + 1)], tsc[:].bitcast(U8).indirect(lists[x][:]))
+
+        def move_planes(a, x0, x1):
+            for r in range(4):
+                first = 64 * a + 4 * r
+                nc.sync.dma_start(
+                    planes[a, x0, x1][r:P:32, :],
+                    picked[first : first + 49 : 16, S * x0 : S * x1].bitcast(I32),
+                )
+
+        def load_w3():
+            nc.sync.dma_start(w3_raw[:], w3_words.rearrange("a p n i -> p a (n i)").bitcast(I32))
+
+        def load_w4(t):
+            nc.sync.dma_start(w4_raw[:, t, :], w4.rearrange("(c t i) n -> t c i n", t=4, i=4)[t])
+
+        def table_plane(x, a, j0, width):
+            run = [n for n in runs if n[0] == a and n[1] <= x < n[2]][0]
+            first = S * (x - run[1]) + j0
+            return planes[run][:].bitcast(U8)[:, first : first + width]
+
+        def spread_constants():
+            cols = bank([P, P], "cols")
+            nc.tensor.transpose(cols[:], rows[:], ident[:])
+            nc.scalar.activation(consts[:], cols[:, 0:16], ACT.Copy)
 
         def gather_words(x, a, h):
             gw[x, a, h] = queued("vector", [P, HALF], U32, f"gw{x}{a}{h}")
@@ -137,45 +153,37 @@ def tile_list_replay_curiosity_bonus_kernel(
                 gw[x, a, h][:], words[a][:].bitcast(U32).indirect(lists[x][:, 32 * h : 32 * (h + 1)])
             )
 
-        def round_w1(a, on_gpsimd=0):
-            for t in range(PACK - on_gpsimd):
-                w1_bf[a, t] = queued("scalar", [P, 32, 4, PACK], BF16, f"w1_bf{a}{t}")
-                src = w1_raw[a][:].rearrange("p j (c t i) -> p t c j i", t=4, i=4)
-                nc.scalar.activation(w1_bf[a, t][:].rearrange("p c i j -> p c j i"), src[:, t], ACT.Copy)
-            for t in range(PACK - on_gpsimd, PACK):
-                w1_bf[a, t] = queued("gpsimd", [P, 32, 4, PACK], BF16, f"w1_bf{a}{t}")
-                src = w1_raw[a][:].rearrange("p j (c t i) -> p t c i j", t=4, i=4)
-                nc.gpsimd.tensor_scalar(w1_bf[a, t][:], src[:, t], 1.0, 0.0, ALU.mult, ALU.add)
+        def round_w1(a):
+            src = w1_raw[a][:].rearrange("p j (c t i) -> p t c j i", t=4, i=4)
+            w1_bf[a] = queued("scalar", [P, PACK, 32, 4, PACK], BF16, f"w1_bf{a}")
+            for t in range(PACK):
+                nc.scalar.activation(w1_bf[a][:, t].rearrange("p c i j -> p c j i"), src[:, t], ACT.Copy)
 
         def quantize_w1(a):
-            for t in range(PACK):
-                w1q[a, t] = queued("vector", [P, P], U32, f"w1q{a}{t}")
-                nc.vector.quantize_mx(
-                    out=w1q[a, t][:].bitcast(FP8X4),
-                    scales=w1s[:, a, P * t : P * (t + 1)],
-                    in_=w1_bf[a, t][:].rearrange("p c i j -> p (c i j)"),
-                )
+            w1q[a] = queued("vector", [P, H], U32, f"w1q{a}")
+            nc.vector.quantize_mx(
+                out=w1q[a][:].bitcast(FP8X4),
+                scales=w1s[:, a, :],
+                in_=w1_bf[a][:].rearrange("p t c i j -> p (t c i j)"),
+            )
 
         def p_pass(x, a, h):
-            tok = slice(HALF * h, HALF * (h + 1))
             for t in range(PACK):
                 if (h, t) not in acc:
                     acc[h, t] = bank([P, HALF], f"acc{h}{t}")
                     done[h, t] = 0
                 m = slice(P * t, P * (t + 1))
                 if x == STATE:
-                    lhs, lhs_s = w1q[a, t][:].bitcast(FP8X4), w1s[:, a, m]
-                    rhs_s = gsc[STATE][4 * a : P, tok]
+                    lhs, lhs_s = w1q[a][:, m].bitcast(FP8X4), w1s[:, a, m]
                 else:
                     lhs = wp[2, a][:].bitcast(U8)[:, 2 * P * t : 2 * P * (t + 1)].bitcast(FP4X4)
                     lhs_s = wsc[2][:, a, :].bitcast(U8)[:, m]
-                    rhs_s = gsc[ACTION][:, tok] if a == 0 else shifted[:].bitcast(U8)[:, tok]
                 nc.tensor.matmul_mx(
                     acc[h, t][:],
                     lhsT=lhs,
                     lhsT_scale=lhs_s,
                     rhs=gw[x, a, h][:].bitcast(FP8X4),
-                    rhs_scale=rhs_s,
+                    rhs_scale=table_plane(x, a, HALF * h, HALF),
                     start=(done[h, t] == 0),
                     stop=(done[h, t] == 2 * PASSES - 1),
                 )
@@ -187,9 +195,11 @@ def tile_list_replay_curiosity_bonus_kernel(
                 nc.scalar.activation(pred[h][:, t, :], acc[h, t][:], ACT.Tanh)
 
         def round_w4(b):
-            w4_bf[b] = queued("gpsimd", [P, 256, PACK], BF16, f"w4_bf{b}")
-            nc.gpsimd.tensor_scalar(
-                w4_bf[b][:], w4_raw[b][:].rearrange("p t n -> p n t"), 1.0, 0.0, ALU.mult, ALU.add
+            w4_bf[b] = queued("scalar", [P, 256, PACK], BF16, f"w4_bf{b}")
+            nc.scalar.activation(
+                w4_bf[b][:].rearrange("p (c i) t -> p c t i", i=4),
+                w4_raw[:, :, 256 * b : 256 * (b + 1)].rearrange("p t (c i) -> p c t i", i=4),
+                ACT.Copy,
             )
 
         def quantize_w4(b):
@@ -211,7 +221,7 @@ def tile_list_replay_curiosity_bonus_kernel(
                         lhsT=wp[3, a][:, m].bitcast(FP8X4),
                         lhsT_scale=wsc[3][:, a, :].bitcast(U8)[:, m],
                         rhs=gw[NEXT, a, h][:, CHUNK * (c % 4) : CHUNK * (c % 4 + 1)].bitcast(FP8X4),
-                        rhs_scale=gsc[NEXT][4 * a : P, CHUNK * c : CHUNK * (c + 1)],
+                        rhs_scale=table_plane(NEXT, a, CHUNK * c, CHUNK),
                         start=(a == 0),
                         stop=(a == PASSES - 1),
                     )
@@ -271,67 +281,98 @@ def tile_list_replay_curiosity_bonus_kernel(
             nc.sync.dma_start(out_v[:, 2 * b : 2 * b + 2, GROUP * gi : GROUP * (gi + 1)], res[:])
 
         gather_scales(ACTION)
-        nc.gpsimd.dma_start(shifted[0:100, :], gsc[ACTION][4:104, :].bitcast(I32))
         gather_scales(STATE)
+        gather_scales(NEXT)
+        move_planes(0, STATE, NEXT)
+        load_words(1)
+        move_planes(1, STATE, NEXT + 1)
+        load_w3()
+        load_w4(0)
+        load_w4(1)
+        move_planes(0, NEXT, NEXT + 1)
+        load_w4(2)
+        load_w4(3)
         reorder_scales(2)
         reorder_words(2, w2_raw, 2)
-        gather_words(ACTION, 0, A)
-        gather_words(ACTION, 0, B)
-        for h in (A, B):
-            p_pass(ACTION, 0, h)
-        gather_words(STATE, 0, A)
-        gather_words(NEXT, 0, A)
+        reorder_scales(3)
         round_w1(0)
-        gather_scales(NEXT)
+        round_w1(1)
+        gather_words(ACTION, 0, A)
+        gather_words(STATE, 0, A)
+        gather_words(ACTION, 0, B)
         quantize_w1(0)
+        p_pass(ACTION, 0, A)
         p_pass(STATE, 0, A)
+        p_pass(ACTION, 0, B)
+        gather_words(STATE, 0, B)
+        p_pass(STATE, 0, B)
+        quantize_w1(1)
         gather_words(ACTION, 1, A)
         p_pass(ACTION, 1, A)
         gather_words(STATE, 1, A)
-        gather_words(NEXT, 1, A)
-        round_w1(1, 2)
-        quantize_w1(1)
         p_pass(STATE, 1, A)
         predict(A)
-        reorder_scales(3)
+        spread_constants()
         reorder_words(3, w3_raw, 4)
-        gather_words(STATE, 0, B)
-        p_pass(STATE, 0, B)
-        for c in range(3):
+        gather_words(NEXT, 0, A)
+        gather_words(NEXT, 1, A)
+        round_w4(0)
+        for c in range(4):
             features(c)
+        gather_words(NEXT, 0, B)
+        for c in (0, 1):
+            subtract(c)
+            square(c)
+            weigh(c, "gpsimd")
         gather_words(ACTION, 1, B)
         p_pass(ACTION, 1, B)
         gather_words(STATE, 1, B)
         p_pass(STATE, 1, B)
-        features(3)
-        for b in range(3):
-            round_w4(b)
-        for step in range(10):
-            if step == 3:
-                predict(B)
-                gather_words(NEXT, 0, B)
-                gather_words(NEXT, 1, B)
-                features(4)
-            if step in (3, 4, 5):
-                features(step + 2)
-            if step < 8:
-                subtract(step)
-                square(step)
-            if step < 7:
-                weigh(step, "gpsimd")
-            if step == 3:
-                for b in range(3):
-                    quantize_w4(b)
-            gi = (step - 3) // 2
-            if step >= 3 and step % 2 == 1:
-                quantize_h(gi)
-                readout(gi)
-                if gi > 0:
-                    finish(gi - 1, 2, "scalar" if gi < 3 else "vector")
-            if step >= 4 and step % 2 == 0:
-                finish(gi, 0, "scalar")
-                if step == 8:
-                    weigh(7, "vector")
-                finish(gi, 1, "vector" if step < 8 else "scalar")
-        for b in range(3):
-            finish(3, b, ("scalar", "vector")[b % 2])
+        round_w4(1)
+        round_w4(2)
+        for c in (2, 3):
+            subtract(c)
+            square(c)
+        weigh(2, "gpsimd")
+        predict(B)
+        gather_words(NEXT, 1, B)
+        features(4)
+        features(5)
+        quantize_w4(0)
+        quantize_h(0)
+        quantize_w4(1)
+        quantize_w4(2)
+        readout(0)
+        weigh(3, "gpsimd")
+        features(6)
+        subtract(4)
+        subtract(5)
+        features(7)
+        finish(0, 0, "scalar")
+        square(4)
+        square(5)
+        quantize_h(1)
+        readout(1)
+        weigh(4, "vector")
+        weigh(5, "gpsimd")
+        finish(0, 1, "scalar")
+        subtract(6)
+        finish(0, 2, "vector")
+        subtract(7)
+        finish(1, 0, "scalar")
+        square(6)
+        finish(1, 1, "scalar")
+        square(7)
+        quantize_h(2)
+        readout(2)
+        weigh(6, "gpsimd")
+        finish(1, 2, "vector")
+        finish(2, 0, "vector")
+        weigh(7, "vector")
+        finish(2, 1, "scalar")
+        quantize_h(3)
+        readout(3)
+        finish(2, 2, "scalar")
+        finish(3, 0, "vector")
+        finish(3, 1, "scalar")
+        finish(3, 2, "vector")

@@ -194,13 +194,15 @@ def tile_list_replay_curiosity_bonus_kernel(
             for t in range(PACK):
                 nc.scalar.activation(pred[h][:, t, :], acc[h, t][:], ACT.Tanh)
 
-        def round_w4(b):
-            w4_bf[b] = queued("scalar", [P, 256, PACK], BF16, f"w4_bf{b}")
-            nc.scalar.activation(
-                w4_bf[b][:].rearrange("p (c i) t -> p c t i", i=4),
-                w4_raw[:, :, 256 * b : 256 * (b + 1)].rearrange("p t (c i) -> p c t i", i=4),
-                ACT.Copy,
-            )
+        def round_w4(b, eng="scalar"):
+            w4_bf[b] = queued(eng, [P, 256, PACK], BF16, f"w4_bf{b}")
+            src = w4_raw[:, :, 256 * b : 256 * (b + 1)]
+            if eng == "scalar":
+                nc.scalar.activation(
+                    w4_bf[b][:].rearrange("p (c i) t -> p c t i", i=4), src.rearrange("p t (c i) -> p c t i", i=4), ACT.Copy
+                )
+            else:
+                nc.gpsimd.tensor_scalar(w4_bf[b][:], src.rearrange("p t n -> p n t"), 1.0, 0.0, ALU.mult, ALU.add)
 
         def quantize_w4(b):
             w4q[b] = queued("vector", [P, 256], U32, f"w4q{b}")
@@ -243,7 +245,7 @@ def tile_list_replay_curiosity_bonus_kernel(
         def weigh(c, eng):
             gi = c // 2
             if gi not in hb:
-                hb[gi] = queued(eng, [P, GROUP, PACK], BF16, f"hb{gi}")
+                hb[gi] = line.tile([P, GROUP, PACK], BF16, name=f"hb{gi}", tag="hb", bufs=1, align_bytes=64)
             c0 = CHUNK * (c % 2)
             engine = nc.gpsimd if eng == "gpsimd" else nc.vector
             engine.tensor_tensor(
@@ -307,6 +309,7 @@ def tile_list_replay_curiosity_bonus_kernel(
         gather_words(STATE, 0, B)
         p_pass(STATE, 0, B)
         quantize_w1(1)
+        gather_words(NEXT, 0, A)
         gather_words(ACTION, 1, A)
         p_pass(ACTION, 1, A)
         gather_words(STATE, 1, A)
@@ -314,65 +317,41 @@ def tile_list_replay_curiosity_bonus_kernel(
         predict(A)
         spread_constants()
         reorder_words(3, w3_raw, 4)
-        gather_words(NEXT, 0, A)
-        gather_words(NEXT, 1, A)
-        round_w4(0)
-        for c in range(4):
-            features(c)
-        gather_words(NEXT, 0, B)
-        for c in (0, 1):
-            subtract(c)
-            square(c)
-            weigh(c, "gpsimd")
         gather_words(ACTION, 1, B)
         p_pass(ACTION, 1, B)
         gather_words(STATE, 1, B)
         p_pass(STATE, 1, B)
-        round_w4(1)
-        round_w4(2)
-        for c in (2, 3):
-            subtract(c)
-            square(c)
-        weigh(2, "gpsimd")
         predict(B)
-        gather_words(NEXT, 1, B)
-        features(4)
-        features(5)
-        quantize_w4(0)
-        quantize_h(0)
-        quantize_w4(1)
-        quantize_w4(2)
-        readout(0)
-        weigh(3, "gpsimd")
-        features(6)
-        subtract(4)
-        subtract(5)
-        features(7)
-        finish(0, 0, "scalar")
-        square(4)
-        square(5)
-        quantize_h(1)
-        readout(1)
-        weigh(4, "vector")
-        weigh(5, "gpsimd")
-        finish(0, 1, "scalar")
-        subtract(6)
-        finish(0, 2, "vector")
-        subtract(7)
-        finish(1, 0, "scalar")
-        square(6)
-        finish(1, 1, "scalar")
-        square(7)
-        quantize_h(2)
-        readout(2)
-        weigh(6, "gpsimd")
-        finish(1, 2, "vector")
-        finish(2, 0, "vector")
-        weigh(7, "vector")
-        finish(2, 1, "scalar")
-        quantize_h(3)
-        readout(3)
-        finish(2, 2, "scalar")
-        finish(3, 0, "vector")
-        finish(3, 1, "scalar")
-        finish(3, 2, "vector")
+        for b in range(3):
+            round_w4(b, "gpsimd")
+        gather_words(NEXT, 1, A)
+        for c in range(4):
+            features(c)
+        gather_words(NEXT, 0, B)
+        subtract(0)
+        square(0)
+        for g in range(4):
+            weigh(2 * g, "gpsimd")
+            subtract(2 * g + 1)
+            square(2 * g + 1)
+            if g == 0:
+                gather_words(NEXT, 1, B)
+            if g < 2:
+                features(2 * g + 4)
+                features(2 * g + 5)
+            if g > 0:
+                finish(g - 1, 0, "scalar")
+            if g < 3:
+                subtract(2 * g + 2)
+                square(2 * g + 2)
+            if g > 0:
+                finish(g - 1, 1, "vector")
+                finish(g - 1, 2, "scalar")
+            weigh(2 * g + 1, "vector")
+            if g == 0:
+                for b in range(3):
+                    quantize_w4(b)
+            quantize_h(g)
+            readout(g)
+        for b in range(3):
+            finish(3, b, ("vector", "scalar")[b % 2])

@@ -258,8 +258,8 @@ def tile_list_replay_curiosity_bonus_kernel(
                 out=hq[gi][:].bitcast(FP8X4), scales=hs[gi][:], in_=hb[gi][:].rearrange("p j t -> p (j t)")
             )
 
-        def readout(gi):
-            for b in range(3):
+        def readout(gi, thirds=(0, 1, 2)):
+            for b in thirds:
                 ys[gi, b] = bank([P, 2, GROUP], f"y{gi}{b}")
                 for e in range(2):
                     nc.tensor.matmul_mx(
@@ -322,35 +322,45 @@ def tile_list_replay_curiosity_bonus_kernel(
         gather_words(STATE, 1, B)
         p_pass(STATE, 1, B)
         predict(B)
-        for b in range(3):
-            round_w4(b, "gpsimd")
+        round_w4(1, "gpsimd")
         gather_words(NEXT, 1, A)
         for c in range(4):
             features(c)
         gather_words(NEXT, 0, B)
         subtract(0)
         square(0)
-        for g in range(4):
+        weigh(0, "gpsimd")
+        subtract(1)
+        square(1)
+        round_w4(0)
+        gather_words(NEXT, 1, B)
+        features(4)
+        features(5)
+        subtract(2)
+        square(2)
+        round_w4(2)
+        weigh(1, "vector")
+        quantize_w4(0)
+        quantize_w4(1)
+        quantize_h(0)
+        readout(0, (0, 1))
+        for g in range(1, 4):
             weigh(2 * g, "gpsimd")
             subtract(2 * g + 1)
             square(2 * g + 1)
-            if g == 0:
-                gather_words(NEXT, 1, B)
-            if g < 2:
-                features(2 * g + 4)
-                features(2 * g + 5)
-            if g > 0:
-                finish(g - 1, 0, "scalar")
+            if g == 1:
+                features(6)
+                features(7)
+            finish(g - 1, 0, "scalar")
             if g < 3:
                 subtract(2 * g + 2)
                 square(2 * g + 2)
-            if g > 0:
-                finish(g - 1, 1, "vector")
-                finish(g - 1, 2, "scalar")
+            finish(g - 1, 1, "vector")
             weigh(2 * g + 1, "vector")
-            if g == 0:
-                for b in range(3):
-                    quantize_w4(b)
+            if g == 1:
+                quantize_w4(2)
+                readout(0, (2,))
+            finish(g - 1, 2, "scalar")
             quantize_h(g)
             readout(g)
         for b in range(3):

@@ -262,15 +262,18 @@ def tile_list_replay_curiosity_bonus_kernel(
             for b in thirds:
                 ys[gi, b] = bank([P, 2, GROUP], f"y{gi}{b}")
                 for e in range(2):
-                    nc.tensor.matmul_mx(
-                        ys[gi, b][:, e, :],
-                        lhsT=w4q[b][:, P * e : P * (e + 1)].bitcast(FP8X4),
-                        lhsT_scale=w4s[:, P * (2 * b + e) : P * (2 * b + e + 1)],
-                        rhs=hq[gi][:].bitcast(FP8X4),
-                        rhs_scale=hs[gi][:],
-                        start=True,
-                        stop=True,
-                    )
+                    product(ys[gi, b][:, e, :], gi, 2 * b + e)
+
+        def product(y, gi, u):
+            nc.tensor.matmul_mx(
+                y,
+                lhsT=w4q[u // 2][:, P * (u % 2) : P * (u % 2 + 1)].bitcast(FP8X4),
+                lhsT_scale=w4s[:, P * u : P * (u + 1)],
+                rhs=hq[gi][:].bitcast(FP8X4),
+                rhs_scale=hs[gi][:],
+                start=True,
+                stop=True,
+            )
 
         def finish(gi, b, eng):
             res = queued(eng, [P, 2, GROUP], F32, f"res{gi}{b}")
@@ -281,6 +284,20 @@ def tile_list_replay_curiosity_bonus_kernel(
                 for e in range(2):
                     nc.scalar.activation(res[:, e, :], ys[gi, b][:, e, :], ACT.Identity, bias=bias[:, e : e + 1])
             nc.sync.dma_start(out_v[:, 2 * b : 2 * b + 2, GROUP * gi : GROUP * (gi + 1)], res[:])
+
+        def last_readout(gi):
+            y = [bank([P, GROUP], f"y{gi}{u}") for u in range(N // P)]
+            for u in range(N // P):
+                product(y[u][:], gi, u)
+            for u in range(N // P):
+                eng = ("vector", "scalar")[u % 2]
+                res = queued(eng, [P, GROUP], F32, f"res{gi}{u}")
+                bias = consts[:, PACK + u : PACK + u + 1]
+                if eng == "vector":
+                    nc.vector.tensor_scalar(res[:], y[u][:], bias, None, ALU.add)
+                else:
+                    nc.scalar.activation(res[:], y[u][:], ACT.Identity, bias=bias)
+                nc.sync.dma_start(out_v[:, u, GROUP * gi : GROUP * (gi + 1)], res[:])
 
         gather_scales(ACTION)
         gather_scales(STATE)
@@ -297,6 +314,7 @@ def tile_list_replay_curiosity_bonus_kernel(
         reorder_scales(2)
         reorder_words(2, w2_raw, 2)
         reorder_scales(3)
+        spread_constants()
         round_w1(0)
         round_w1(1)
         gather_words(ACTION, 0, A)
@@ -315,7 +333,6 @@ def tile_list_replay_curiosity_bonus_kernel(
         gather_words(STATE, 1, A)
         p_pass(STATE, 1, A)
         predict(A)
-        spread_constants()
         reorder_words(3, w3_raw, 4)
         gather_words(ACTION, 1, B)
         p_pass(ACTION, 1, B)
@@ -362,6 +379,6 @@ def tile_list_replay_curiosity_bonus_kernel(
                 readout(0, (2,))
             finish(g - 1, 2, "scalar")
             quantize_h(g)
-            readout(g)
-        for b in range(3):
-            finish(3, b, ("vector", "scalar")[b % 2])
+            if g < 3:
+                readout(g)
+        last_readout(3)

@@ -19,13 +19,22 @@ ALU = mybir.AluOpType
 
 P = 128
 PACK = 4
-PASSES = 2
+PASSES = K // (P * PACK)
 HALF = 512
 CHUNK = 128
 GROUP = 256
+GROUPS = S // GROUP
+THIRD = N // 3
+ROW_TILES = N // P
+QUADRANT = 32
+RUN = 4
 STATE, ACTION, NEXT = 0, 1, 2
-A, B = 0, 1
-QUEUE_BUFS = {"vector": 30, "scalar": 9, "gpsimd": 10}
+FIRST, SECOND = 0, 1
+BANKS = 8
+QUEUE_DEPTH = {"vector": 30, "scalar": 9, "gpsimd": 10}
+ZERO_SPLIT = 640
+WEIGHT_OFFSET = {2: 0, 3: 8}
+MOVE_OFFSET = (0, 0, 4)
 
 
 def tile_list_replay_curiosity_bonus_kernel(
@@ -38,31 +47,31 @@ def tile_list_replay_curiosity_bonus_kernel(
         psum = ctx.enter_context(tc.psum_pool(name="psum", bufs=1))
 
         def bank(shape, name):
-            return psum.tile(shape, F32, name=name, tag="bank", bufs=8)
+            return psum.tile(shape, F32, name=name, tag="bank", bufs=BANKS)
 
         def queued(eng, shape, dtype, name):
-            return line.tile(shape, dtype, name=name, tag=eng, bufs=QUEUE_BUFS[eng], align_bytes=64)
+            return line.tile(shape, dtype, name=name, tag=eng, bufs=QUEUE_DEPTH[eng], align_bytes=64)
 
         lists = [keep.tile([P, S // 16], U16, name=f"list{x}") for x in range(3)]
-        tsc = keep.tile([P, T // 4], I32, name="tsc")
+        window = keep.tile([P, T // 4], I32, name="tsc")
         picked = keep.tile([P, 3 * S], U8, name="picked")
-        runs = [(0, STATE, NEXT), (1, STATE, NEXT + 1), (0, NEXT, NEXT + 1)]
+        moves = [(0, STATE, NEXT), (1, STATE, NEXT + 1), (0, NEXT, NEXT + 1)]
         planes = {
-            run: keep.tile([P, S // 4 * (run[2] - run[1])], I32, name=f"planes{i}", align_bytes=64)
-            for i, run in enumerate(runs)
+            move: keep.tile([P, S // 4 * (move[2] - move[1])], I32, name=f"planes{i}", align_bytes=64)
+            for i, move in enumerate(moves)
         }
         wsc_raw = {w: keep.tile([P, PASSES, H // 4], I32, name=f"wsc_raw{w}") for w in (2, 3)}
-        nc.gpsimd.memset(tsc[:, 0:640], 0)
-        nc.vector.memset(tsc[:, 640:], 0)
+        nc.gpsimd.memset(window[:, 0:ZERO_SPLIT], 0)
+        nc.vector.memset(window[:, ZERO_SPLIT:], 0)
         nc.vector.memset(wsc_raw[2][:], 0)
         nc.vector.memset(wsc_raw[3][:], 0)
-        for run in runs:
-            nc.vector.memset(planes[run][:], 0)
+        for move in moves:
+            nc.vector.memset(planes[move][:], 0)
         rows = keep.tile([P, P], F32, name="rows")
         nc.gpsimd.memset(rows[:], 0.0)
         ident = keep.tile([P, P], F32, name="ident")
         make_identity(nc, ident[:])
-        consts = keep.tile([P, 16], F32, name="consts")
+        consts = keep.tile([P, PACK + ROW_TILES], F32, name="consts")
         gain = consts[:, 0:PACK]
 
         words = [keep.tile([P, T], I32, name=f"words{a}") for a in range(PASSES)]
@@ -75,32 +84,37 @@ def tile_list_replay_curiosity_bonus_kernel(
             nc.sync.dma_start(words[a][:], tab_words[a].rearrange("p t i -> p (t i)").bitcast(I32))
 
         def load_w1(a):
-            nc.sync.dma_start(w1_raw[a][:], w1[512 * a : 512 * (a + 1), :].rearrange("(p j) r -> p j r", j=PACK))
+            pass_rows = w1[P * PACK * a : P * PACK * (a + 1), :]
+            nc.sync.dma_start(w1_raw[a][:], pass_rows.rearrange("(p j) r -> p j r", j=PACK))
 
         def load_weight_scales(w, scales):
-            for r in range(4):
+            for r in range(RUN):
                 nc.gpsimd.dma_start(
-                    wsc_raw[w][r:P:32, :, :], scales.rearrange("a (q r) n -> r q a n", r=4)[r].bitcast(I32)
+                    wsc_raw[w][WEIGHT_OFFSET[w] + r : P : QUADRANT, :, :],
+                    scales.rearrange("a (q r) n -> r q a n", r=RUN)[r].bitcast(I32),
                 )
+
+        def load_w4(t):
+            nc.sync.dma_start(w4_raw[:, t, :], w4.rearrange("(c t i) n -> t c i n", t=PACK, i=4)[t])
 
         nc.sync.dma_start(lists[ACTION][:], offs2)
         nc.sync.dma_start(lists[STATE][:], offs)
-        nc.sync.dma_start(tsc[0:P:4, :], tab_scales.rearrange("a q n -> (a q) n").bitcast(I32))
+        nc.sync.dma_start(window[0:P:4, :], tab_scales.rearrange("a q n -> (a q) n").bitcast(I32))
         nc.sync.dma_start(lists[NEXT][:], offs3)
         load_weight_scales(2, w2_scales)
         load_weight_scales(3, w3_scales)
         load_words(0)
         nc.sync.dma_start(
-            rows[0:PACK, :].rearrange("t (c i) -> t c i", i=4), g.rearrange("(c t i) -> t c i", t=4, i=4)
+            rows[0:PACK, :].rearrange("t (c i) -> t c i", i=4), g.rearrange("(c t i) -> t c i", t=PACK, i=4)
         )
-        nc.sync.dma_start(rows[PACK : PACK + N // P, :], b4.rearrange("(u p) -> u p", p=P))
+        nc.sync.dma_start(rows[PACK : PACK + ROW_TILES, :], b4.rearrange("(u p) -> u p", p=P))
         nc.sync.dma_start(w2_raw[:], w2_words.rearrange("a p n -> p a n").bitcast(I32))
         load_w1(0)
         load_w1(1)
 
         w1s = keep.tile([P, PASSES, H], U8, name="w1s", align_bytes=64)
         w4s = keep.tile([P, N], U8, name="w4s", align_bytes=64)
-        hs = [keep.tile([P, GROUP], U8, name=f"hs{i}", align_bytes=64) for i in range(S // GROUP)]
+        hs = [keep.tile([P, GROUP], U8, name=f"hs{i}", align_bytes=64) for i in range(GROUPS)]
         out_v = out.rearrange("(u p) j -> p u j", p=P)
 
         gw, w1_bf, w1q, wp, wsc, acc, done = {}, {}, {}, {}, {}, {}, {}
@@ -109,53 +123,48 @@ def tile_list_replay_curiosity_bonus_kernel(
         def reorder_scales(w):
             wsc[w] = queued("gpsimd", [P, PASSES, H // 4], I32, f"wsc{w}")
             nc.gpsimd.tensor_copy(
-                wsc[w][:].rearrange("p a (t c) -> p a t c", t=4), wsc_raw[w][:].rearrange("p a (c t) -> p a t c", t=4)
+                wsc[w][:].rearrange("p a (t c) -> p a t c", t=PACK),
+                wsc_raw[w][:].rearrange("p a (c t) -> p a t c", t=PACK),
             )
 
-        def reorder_words(w, raw, run):
+        def reorder_words(w, raw, span):
             for a in range(PASSES):
-                wp[w, a] = queued("gpsimd", [P, P * run], I32, f"wp{w}{a}")
+                wp[w, a] = queued("gpsimd", [P, P * span], I32, f"wp{w}{a}")
                 nc.gpsimd.tensor_copy(
-                    wp[w, a][:].rearrange("p (t c i) -> p t c i", t=4, i=run),
-                    raw[:, a, :].rearrange("p (c t i) -> p t c i", t=4, i=run),
+                    wp[w, a][:].rearrange("p (t c i) -> p t c i", t=PACK, i=span),
+                    raw[:, a, :].rearrange("p (c t i) -> p t c i", t=PACK, i=span),
                 )
 
         def gather_scales(x):
-            nc.vector.tensor_copy(picked[:, S * x : S * (x + 1)], tsc[:].bitcast(U8).indirect(lists[x][:]))
+            nc.vector.tensor_copy(picked[:, S * x : S * (x + 1)], window[:].bitcast(U8).indirect(lists[x][:]))
 
-        def move_planes(a, x0, x1):
-            for r in range(4):
+        def move_scales(move):
+            a, x0, x1 = move
+            for r in range(RUN):
                 first = 64 * a + 4 * r
                 nc.sync.dma_start(
-                    planes[a, x0, x1][r:P:32, :],
-                    picked[first : first + 49 : 16, S * x0 : S * x1].bitcast(I32),
+                    planes[move][MOVE_OFFSET[moves.index(move)] + r : P : QUADRANT, :],
+                    picked[first : first + 3 * 16 + 1 : 16, S * x0 : S * x1].bitcast(I32),
                 )
 
-        def load_w3():
-            nc.sync.dma_start(w3_raw[:], w3_words.rearrange("a p n i -> p a (n i)").bitcast(I32))
-
-        def load_w4(t):
-            nc.sync.dma_start(w4_raw[:, t, :], w4.rearrange("(c t i) n -> t c i n", t=4, i=4)[t])
-
         def table_plane(x, a, j0, width):
-            run = [n for n in runs if n[0] == a and n[1] <= x < n[2]][0]
-            first = S * (x - run[1]) + j0
-            return planes[run][:].bitcast(U8)[:, first : first + width]
+            move = [m for m in moves if m[0] == a and m[1] <= x < m[2]][0]
+            first = S * (x - move[1]) + j0
+            return planes[move][MOVE_OFFSET[moves.index(move)] :, :].bitcast(U8)[:, first : first + width]
 
         def spread_constants():
             cols = bank([P, P], "cols")
             nc.tensor.transpose(cols[:], rows[:], ident[:])
-            nc.scalar.activation(consts[:], cols[:, 0:16], ACT.Copy)
+            nc.scalar.activation(consts[:], cols[:, 0:PACK + ROW_TILES], ACT.Copy)
 
-        def gather_words(x, a, h):
-            gw[x, a, h] = queued("vector", [P, HALF], U32, f"gw{x}{a}{h}")
-            nc.vector.tensor_copy(
-                gw[x, a, h][:], words[a][:].bitcast(U32).indirect(lists[x][:, 32 * h : 32 * (h + 1)])
-            )
+        def gather_words(x, a, half):
+            gw[x, a, half] = queued("vector", [P, HALF], U32, f"gw{x}{a}{half}")
+            offsets = lists[x][:, HALF // 16 * half : HALF // 16 * (half + 1)]
+            nc.vector.tensor_copy(gw[x, a, half][:], words[a][:].bitcast(U32).indirect(offsets))
 
         def round_w1(a):
-            src = w1_raw[a][:].rearrange("p j (c t i) -> p t c j i", t=4, i=4)
-            w1_bf[a] = queued("scalar", [P, PACK, 32, 4, PACK], BF16, f"w1_bf{a}")
+            src = w1_raw[a][:].rearrange("p j (c t i) -> p t c j i", t=PACK, i=4)
+            w1_bf[a] = queued("scalar", [P, PACK, P // 4, 4, PACK], BF16, f"w1_bf{a}")
             for t in range(PACK):
                 nc.scalar.activation(w1_bf[a][:, t].rearrange("p c i j -> p c j i"), src[:, t], ACT.Copy)
 
@@ -167,11 +176,11 @@ def tile_list_replay_curiosity_bonus_kernel(
                 in_=w1_bf[a][:].rearrange("p t c i j -> p (t c i j)"),
             )
 
-        def p_pass(x, a, h):
+        def p_pass(x, a, half):
             for t in range(PACK):
-                if (h, t) not in acc:
-                    acc[h, t] = bank([P, HALF], f"acc{h}{t}")
-                    done[h, t] = 0
+                if (half, t) not in acc:
+                    acc[half, t] = bank([P, HALF], f"acc{half}{t}")
+                    done[half, t] = 0
                 m = slice(P * t, P * (t + 1))
                 if x == STATE:
                     lhs, lhs_s = w1q[a][:, m].bitcast(FP8X4), w1s[:, a, m]
@@ -179,62 +188,65 @@ def tile_list_replay_curiosity_bonus_kernel(
                     lhs = wp[2, a][:].bitcast(U8)[:, 2 * P * t : 2 * P * (t + 1)].bitcast(FP4X4)
                     lhs_s = wsc[2][:, a, :].bitcast(U8)[:, m]
                 nc.tensor.matmul_mx(
-                    acc[h, t][:],
+                    acc[half, t][:],
                     lhsT=lhs,
                     lhsT_scale=lhs_s,
-                    rhs=gw[x, a, h][:].bitcast(FP8X4),
-                    rhs_scale=table_plane(x, a, HALF * h, HALF),
-                    start=(done[h, t] == 0),
-                    stop=(done[h, t] == 2 * PASSES - 1),
+                    rhs=gw[x, a, half][:].bitcast(FP8X4),
+                    rhs_scale=table_plane(x, a, HALF * half, HALF),
+                    start=(done[half, t] == 0),
+                    stop=(done[half, t] == 2 * PASSES - 1),
                 )
-                done[h, t] = done[h, t] + 1
+                done[half, t] = done[half, t] + 1
 
-        def predict(h):
-            pred[h] = queued("scalar", [P, PACK, HALF], F32, f"pred{h}")
+        def predict(half):
+            pred[half] = queued("scalar", [P, PACK, HALF], F32, f"pred{half}")
             for t in range(PACK):
-                nc.scalar.activation(pred[h][:, t, :], acc[h, t][:], ACT.Tanh)
+                nc.scalar.activation(pred[half][:, t, :], acc[half, t][:], ACT.Tanh)
 
-        def round_w4(b, eng="scalar"):
-            w4_bf[b] = queued(eng, [P, 256, PACK], BF16, f"w4_bf{b}")
-            src = w4_raw[:, :, 256 * b : 256 * (b + 1)]
+        def round_w4(b, eng):
+            w4_bf[b] = queued(eng, [P, THIRD, PACK], BF16, f"w4_bf{b}")
+            src = w4_raw[:, :, THIRD * b : THIRD * (b + 1)]
             if eng == "scalar":
                 nc.scalar.activation(
-                    w4_bf[b][:].rearrange("p (c i) t -> p c t i", i=4), src.rearrange("p t (c i) -> p c t i", i=4), ACT.Copy
+                    w4_bf[b][:].rearrange("p (c i) t -> p c t i", i=4),
+                    src.rearrange("p t (c i) -> p c t i", i=4),
+                    ACT.Copy,
                 )
             else:
                 nc.gpsimd.tensor_scalar(w4_bf[b][:], src.rearrange("p t n -> p n t"), 1.0, 0.0, ALU.mult, ALU.add)
 
         def quantize_w4(b):
-            w4q[b] = queued("vector", [P, 256], U32, f"w4q{b}")
+            w4q[b] = queued("vector", [P, THIRD], U32, f"w4q{b}")
             nc.vector.quantize_mx(
                 out=w4q[b][:].bitcast(FP8X4),
-                scales=w4s[:, 256 * b : 256 * (b + 1)],
+                scales=w4s[:, THIRD * b : THIRD * (b + 1)],
                 in_=w4_bf[b][:].rearrange("p n t -> p (n t)"),
             )
 
+        def place_in_half(c):
+            j0 = CHUNK * c % HALF
+            return CHUNK * c // HALF, slice(j0, j0 + CHUNK)
+
         def features(c):
-            h = c // 4
+            half, cols = place_in_half(c)
             feat[c] = bank([P, PACK, CHUNK], f"feat{c}")
             for t in range(PACK):
-                m = slice(P * t, P * (t + 1))
                 for a in range(PASSES):
+                    m = slice(P * t, P * (t + 1))
                     nc.tensor.matmul_mx(
                         feat[c][:, t, :],
                         lhsT=wp[3, a][:, m].bitcast(FP8X4),
-                        lhsT_scale=wsc[3][:, a, :].bitcast(U8)[:, m],
-                        rhs=gw[NEXT, a, h][:, CHUNK * (c % 4) : CHUNK * (c % 4 + 1)].bitcast(FP8X4),
+                        lhsT_scale=wsc[3][WEIGHT_OFFSET[3] :, a, :].bitcast(U8)[:, m],
+                        rhs=gw[NEXT, a, half][:, cols].bitcast(FP8X4),
                         rhs_scale=table_plane(NEXT, a, CHUNK * c, CHUNK),
                         start=(a == 0),
                         stop=(a == PASSES - 1),
                     )
 
-        def subtract(c):
+        def error(c):
+            half, cols = place_in_half(c)
             diff[c] = queued("vector", [P, PACK, CHUNK], F32, f"diff{c}")
-            nc.vector.tensor_tensor(
-                diff[c][:], pred[c // 4][:, :, CHUNK * (c % 4) : CHUNK * (c % 4 + 1)], feat[c][:], ALU.subtract
-            )
-
-        def square(c):
+            nc.vector.tensor_tensor(diff[c][:], pred[half][:, :, cols], feat[c][:], ALU.subtract)
             sq[c] = queued("scalar", [P, CHUNK, PACK], F32, f"sq{c}")
             nc.scalar.activation(
                 sq[c][:].rearrange("p (c i) t -> p c t i", i=4),
@@ -242,73 +254,71 @@ def tile_list_replay_curiosity_bonus_kernel(
                 ACT.Square,
             )
 
-        def weigh(c, eng):
-            gi = c // 2
-            if gi not in hb:
-                hb[gi] = line.tile([P, GROUP, PACK], BF16, name=f"hb{gi}", tag="hb", bufs=1, align_bytes=64)
-            c0 = CHUNK * (c % 2)
-            engine = nc.gpsimd if eng == "gpsimd" else nc.vector
+        def weigh(c, engine):
+            group, c0 = c // 2, CHUNK * (c % 2)
+            if group not in hb:
+                hb[group] = line.tile([P, GROUP, PACK], BF16, name=f"hb{group}", tag="hb", bufs=1, align_bytes=64)
             engine.tensor_tensor(
-                hb[gi][:, c0 : c0 + CHUNK, :], sq[c][:], gain.unsqueeze(1).to_broadcast([P, CHUNK, PACK]), ALU.mult
+                hb[group][:, c0 : c0 + CHUNK, :], sq[c][:], gain.unsqueeze(1).to_broadcast([P, CHUNK, PACK]), ALU.mult
             )
 
-        def quantize_h(gi):
-            hq[gi] = queued("vector", [P, GROUP], U32, f"hq{gi}")
+        def quantize_h(group):
+            hq[group] = queued("vector", [P, GROUP], U32, f"hq{group}")
             nc.vector.quantize_mx(
-                out=hq[gi][:].bitcast(FP8X4), scales=hs[gi][:], in_=hb[gi][:].rearrange("p j t -> p (j t)")
+                out=hq[group][:].bitcast(FP8X4), scales=hs[group][:], in_=hb[group][:].rearrange("p j t -> p (j t)")
             )
 
-        def readout(gi, thirds=(0, 1, 2)):
-            for b in thirds:
-                ys[gi, b] = bank([P, 2, GROUP], f"y{gi}{b}")
-                for e in range(2):
-                    product(ys[gi, b][:, e, :], gi, 2 * b + e)
-
-        def product(y, gi, u):
+        def product(y, group, u):
             nc.tensor.matmul_mx(
                 y,
                 lhsT=w4q[u // 2][:, P * (u % 2) : P * (u % 2 + 1)].bitcast(FP8X4),
                 lhsT_scale=w4s[:, P * u : P * (u + 1)],
-                rhs=hq[gi][:].bitcast(FP8X4),
-                rhs_scale=hs[gi][:],
+                rhs=hq[group][:].bitcast(FP8X4),
+                rhs_scale=hs[group][:],
                 start=True,
                 stop=True,
             )
 
-        def finish(gi, b, eng):
-            res = queued(eng, [P, 2, GROUP], F32, f"res{gi}{b}")
+        def readout(group, thirds):
+            for b in thirds:
+                ys[group, b] = bank([P, 2, GROUP], f"y{group}{b}")
+                for e in range(2):
+                    product(ys[group, b][:, e, :], group, 2 * b + e)
+
+        def finish(group, b, eng):
+            res = queued(eng, [P, 2, GROUP], F32, f"res{group}{b}")
             bias = consts[:, PACK + 2 * b : PACK + 2 * b + 2]
+            y = ys[group, b]
             if eng == "vector":
-                nc.vector.tensor_tensor(res[:], ys[gi, b][:], bias.unsqueeze(2).to_broadcast([P, 2, GROUP]), ALU.add)
+                nc.vector.tensor_tensor(res[:], y[:], bias.unsqueeze(2).to_broadcast([P, 2, GROUP]), ALU.add)
             else:
                 for e in range(2):
-                    nc.scalar.activation(res[:, e, :], ys[gi, b][:, e, :], ACT.Identity, bias=bias[:, e : e + 1])
-            nc.sync.dma_start(out_v[:, 2 * b : 2 * b + 2, GROUP * gi : GROUP * (gi + 1)], res[:])
+                    nc.scalar.activation(res[:, e, :], y[:, e, :], ACT.Identity, bias=bias[:, e : e + 1])
+            nc.sync.dma_start(out_v[:, 2 * b : 2 * b + 2, GROUP * group : GROUP * (group + 1)], res[:])
 
-        def last_readout(gi):
-            y = [bank([P, GROUP], f"y{gi}{u}") for u in range(N // P)]
-            for u in range(N // P):
-                product(y[u][:], gi, u)
-            for u in range(N // P):
+        def last_readout(group):
+            y = [bank([P, GROUP], f"y{group}{u}") for u in range(ROW_TILES)]
+            for u in range(ROW_TILES):
+                product(y[u][:], group, u)
+            for u in range(ROW_TILES):
                 eng = ("vector", "scalar")[u % 2]
-                res = queued(eng, [P, GROUP], F32, f"res{gi}{u}")
+                res = queued(eng, [P, GROUP], F32, f"res{group}{u}")
                 bias = consts[:, PACK + u : PACK + u + 1]
                 if eng == "vector":
                     nc.vector.tensor_scalar(res[:], y[u][:], bias, None, ALU.add)
                 else:
                     nc.scalar.activation(res[:], y[u][:], ACT.Identity, bias=bias)
-                nc.sync.dma_start(out_v[:, u, GROUP * gi : GROUP * (gi + 1)], res[:])
+                nc.sync.dma_start(out_v[:, u, GROUP * group : GROUP * (group + 1)], res[:])
 
-        gather_scales(ACTION)
-        gather_scales(STATE)
-        gather_scales(NEXT)
-        move_planes(0, STATE, NEXT)
+        for x in (ACTION, STATE, NEXT):
+            gather_scales(x)
+        move_scales(moves[0])
         load_words(1)
-        move_planes(1, STATE, NEXT + 1)
-        load_w3()
+        move_scales(moves[1])
+        nc.sync.dma_start(w3_raw[:], w3_words.rearrange("a p n i -> p a (n i)").bitcast(I32))
         load_w4(0)
         load_w4(1)
-        move_planes(0, NEXT, NEXT + 1)
+        move_scales(moves[2])
         load_w4(2)
         load_w4(3)
         reorder_scales(2)
@@ -317,68 +327,64 @@ def tile_list_replay_curiosity_bonus_kernel(
         spread_constants()
         round_w1(0)
         round_w1(1)
-        gather_words(ACTION, 0, A)
-        gather_words(STATE, 0, A)
-        gather_words(ACTION, 0, B)
+
+        gather_words(ACTION, 0, FIRST)
+        gather_words(STATE, 0, FIRST)
+        gather_words(ACTION, 0, SECOND)
         quantize_w1(0)
-        p_pass(ACTION, 0, A)
-        p_pass(STATE, 0, A)
-        p_pass(ACTION, 0, B)
-        gather_words(STATE, 0, B)
-        p_pass(STATE, 0, B)
+        p_pass(ACTION, 0, FIRST)
+        p_pass(STATE, 0, FIRST)
+        p_pass(ACTION, 0, SECOND)
+        gather_words(STATE, 0, SECOND)
+        p_pass(STATE, 0, SECOND)
         quantize_w1(1)
-        gather_words(NEXT, 0, A)
-        gather_words(ACTION, 1, A)
-        p_pass(ACTION, 1, A)
-        gather_words(STATE, 1, A)
-        p_pass(STATE, 1, A)
-        predict(A)
-        reorder_words(3, w3_raw, 4)
-        gather_words(ACTION, 1, B)
-        p_pass(ACTION, 1, B)
-        gather_words(STATE, 1, B)
-        p_pass(STATE, 1, B)
-        predict(B)
+        gather_words(NEXT, 0, FIRST)
+
+        for half in (FIRST, SECOND):
+            for x in (ACTION, STATE):
+                gather_words(x, 1, half)
+                p_pass(x, 1, half)
+            predict(half)
+            if half == FIRST:
+                reorder_words(3, w3_raw, 4)
         round_w4(1, "gpsimd")
-        gather_words(NEXT, 1, A)
-        for c in range(4):
+        gather_words(NEXT, 1, FIRST)
+        for c in range(HALF // CHUNK):
             features(c)
-        gather_words(NEXT, 0, B)
-        subtract(0)
-        square(0)
-        weigh(0, "gpsimd")
-        subtract(1)
-        square(1)
-        round_w4(0)
-        gather_words(NEXT, 1, B)
+        gather_words(NEXT, 0, SECOND)
+
+        error(0)
+        weigh(0, nc.gpsimd)
+        error(1)
+        round_w4(0, "scalar")
+        gather_words(NEXT, 1, SECOND)
         features(4)
         features(5)
-        subtract(2)
-        square(2)
-        round_w4(2)
-        weigh(1, "vector")
+        error(2)
+        round_w4(2, "scalar")
+        weigh(1, nc.vector)
         quantize_w4(0)
         quantize_w4(1)
         quantize_h(0)
         readout(0, (0, 1))
-        for g in range(1, 4):
-            weigh(2 * g, "gpsimd")
-            subtract(2 * g + 1)
-            square(2 * g + 1)
-            if g == 1:
+
+        last = GROUPS - 1
+        for group in range(1, GROUPS):
+            weigh(2 * group, nc.gpsimd)
+            error(2 * group + 1)
+            if group == 1:
                 features(6)
                 features(7)
-            finish(g - 1, 0, "scalar")
-            if g < 3:
-                subtract(2 * g + 2)
-                square(2 * g + 2)
-            finish(g - 1, 1, "vector")
-            weigh(2 * g + 1, "vector")
-            if g == 1:
+            finish(group - 1, 0, "scalar")
+            if group < last:
+                error(2 * group + 2)
+            finish(group - 1, 1, "vector")
+            weigh(2 * group + 1, nc.vector)
+            if group == 1:
                 quantize_w4(2)
                 readout(0, (2,))
-            finish(g - 1, 2, "scalar")
-            quantize_h(g)
-            if g < 3:
-                readout(g)
-        last_readout(3)
+            finish(group - 1, 2, "scalar")
+            quantize_h(group)
+            if group < last:
+                readout(group, (0, 1, 2))
+        last_readout(last)

@@ -31,8 +31,8 @@ RUN = 4
 STATE, ACTION, NEXT = 0, 1, 2
 FIRST, SECOND = 0, 1
 BANKS = 8
-QUEUE_DEPTH = {"vector": 30, "scalar": 9, "gpsimd": 10}
-ZERO_SPLIT = 640
+QUEUE_DEPTH = {"vector": 18, "scalar": 8, "gpsimd": 9}
+SCALE_ROW0 = 96
 WEIGHT_OFFSET = {2: 0, 3: 8}
 MOVE_OFFSET = (0, 0, 4)
 
@@ -60,13 +60,8 @@ def tile_list_replay_curiosity_bonus_kernel(
             move: keep.tile([P, S // 4 * (move[2] - move[1])], I32, name=f"planes{i}", align_bytes=64)
             for i, move in enumerate(moves)
         }
-        wsc_raw = {w: keep.tile([P, PASSES, H // 4], I32, name=f"wsc_raw{w}") for w in (2, 3)}
-        nc.gpsimd.memset(window[:, 0:ZERO_SPLIT], 0)
-        nc.vector.memset(window[:, ZERO_SPLIT:], 0)
-        nc.vector.memset(wsc_raw[2][:], 0)
-        nc.vector.memset(wsc_raw[3][:], 0)
-        for move in moves:
-            nc.vector.memset(planes[move][:], 0)
+        wsc_raw = {}
+        nc.vector.memset(window[0:SCALE_ROW0, :], 0)
         rows = keep.tile([P, P], F32, name="rows")
         nc.gpsimd.memset(rows[:], 0.0)
         ident = keep.tile([P, P], F32, name="ident")
@@ -78,7 +73,8 @@ def tile_list_replay_curiosity_bonus_kernel(
         w1_raw = [keep.tile([P, PACK, H], F32, name=f"w1_raw{a}") for a in range(PASSES)]
         w2_raw = keep.tile([P, PASSES, H // 2], I32, name="w2_raw")
         w3_raw = keep.tile([P, PASSES, H], I32, name="w3_raw")
-        w4_raw = keep.tile([P, PACK, N], F32, name="w4_raw")
+        w4_parts = [(0, THIRD), (THIRD, N)]
+        w4_raw = [keep.tile([P, PACK, n1 - n0], F32, name=f"w4_raw{n0}") for n0, n1 in w4_parts]
 
         def load_words(a):
             nc.sync.dma_start(words[a][:], tab_words[a].rearrange("p t i -> p (t i)").bitcast(I32))
@@ -88,26 +84,35 @@ def tile_list_replay_curiosity_bonus_kernel(
             nc.sync.dma_start(w1_raw[a][:], pass_rows.rearrange("(p j) r -> p j r", j=PACK))
 
         def load_weight_scales(w, scales):
+            wsc_raw[w] = queued("gpsimd", [P, PASSES, H // 4], I32, f"wsc_raw{w}")
+            nc.gpsimd.memset(wsc_raw[w][:], 0)
             for r in range(RUN):
                 nc.gpsimd.dma_start(
                     wsc_raw[w][WEIGHT_OFFSET[w] + r : P : QUADRANT, :, :],
                     scales.rearrange("a (q r) n -> r q a n", r=RUN)[r].bitcast(I32),
                 )
 
-        def load_w4(t):
-            nc.sync.dma_start(w4_raw[:, t, :], w4.rearrange("(c t i) n -> t c i n", t=PACK, i=4)[t])
+        def load_w4(part):
+            n0, n1 = w4_parts[part]
+            for t in range(PACK):
+                nc.sync.dma_start(w4_raw[part][:, t, :], w4.rearrange("(c t i) n -> t c i n", t=PACK, i=4)[t][:, :, n0:n1])
 
+        nc.sync.dma_start(window[SCALE_ROW0:P, :], tab_scales.rearrange("a q n -> (a q) n").bitcast(I32))
         nc.sync.dma_start(lists[ACTION][:], offs2)
         nc.sync.dma_start(lists[STATE][:], offs)
-        nc.sync.dma_start(window[0:P:4, :], tab_scales.rearrange("a q n -> (a q) n").bitcast(I32))
         nc.sync.dma_start(lists[NEXT][:], offs3)
-        load_weight_scales(2, w2_scales)
-        load_weight_scales(3, w3_scales)
-        load_words(0)
-        nc.sync.dma_start(
+        nc.scalar.dma_start(
             rows[0:PACK, :].rearrange("t (c i) -> t c i", i=4), g.rearrange("(c t i) -> t c i", t=PACK, i=4)
         )
-        nc.sync.dma_start(rows[PACK : PACK + ROW_TILES, :], b4.rearrange("(u p) -> u p", p=P))
+        bias_rows = b4.rearrange("(u p) -> u p", p=P)
+        nc.scalar.dma_start(rows[PACK : 2 * PACK, :], bias_rows[0:PACK])
+        nc.scalar.dma_start(rows[2 * PACK : PACK + ROW_TILES, :], bias_rows[PACK:ROW_TILES])
+        load_weight_scales(2, w2_scales)
+        load_weight_scales(3, w3_scales)
+        nc.vector.memset(planes[moves[0]][:], 0)
+        for move in moves[1:]:
+            nc.gpsimd.memset(planes[move][:], 0)
+        load_words(0)
         nc.sync.dma_start(w2_raw[:], w2_words.rearrange("a p n -> p a n").bitcast(I32))
         load_w1(0)
         load_w1(1)
@@ -141,10 +146,10 @@ def tile_list_replay_curiosity_bonus_kernel(
         def move_scales(move):
             a, x0, x1 = move
             for r in range(RUN):
-                first = 64 * a + 4 * r
+                first = SCALE_ROW0 + 16 * a + r
                 nc.sync.dma_start(
                     planes[move][MOVE_OFFSET[moves.index(move)] + r : P : QUADRANT, :],
-                    picked[first : first + 3 * 16 + 1 : 16, S * x0 : S * x1].bitcast(I32),
+                    picked[first : first + 3 * RUN + 1 : RUN, S * x0 : S * x1].bitcast(I32),
                 )
 
         def table_plane(x, a, j0, width):
@@ -158,9 +163,16 @@ def tile_list_replay_curiosity_bonus_kernel(
             nc.scalar.activation(consts[:], cols[:, 0:PACK + ROW_TILES], ACT.Copy)
 
         def gather_words(x, a, half):
-            gw[x, a, half] = queued("vector", [P, HALF], U32, f"gw{x}{a}{half}")
+            picked_words = queued("vector", [P, HALF], U32, f"gw{x}{a}{half}")
             offsets = lists[x][:, HALF // 16 * half : HALF // 16 * (half + 1)]
-            nc.vector.tensor_copy(gw[x, a, half][:], words[a][:].bitcast(U32).indirect(offsets))
+            nc.vector.tensor_copy(picked_words[:], words[a][:].bitcast(U32).indirect(offsets))
+            gw[x, a, half] = picked_words[:]
+
+        def gather_list(x, a):
+            picked_words = queued("vector", [P, S], U32, f"gw{x}{a}")
+            nc.vector.tensor_copy(picked_words[:], words[a][:].bitcast(U32).indirect(lists[x][:]))
+            for half in (FIRST, SECOND):
+                gw[x, a, half] = picked_words[:, HALF * half : HALF * (half + 1)]
 
         def round_w1(a):
             src = w1_raw[a][:].rearrange("p j (c t i) -> p t c j i", t=PACK, i=4)
@@ -176,8 +188,8 @@ def tile_list_replay_curiosity_bonus_kernel(
                 in_=w1_bf[a][:].rearrange("p t c i j -> p (t c i j)"),
             )
 
-        def p_pass(x, a, half):
-            for t in range(PACK):
+        def p_pass(x, a, half, slots=range(PACK)):
+            for t in slots:
                 if (half, t) not in acc:
                     acc[half, t] = bank([P, HALF], f"acc{half}{t}")
                     done[half, t] = 0
@@ -191,7 +203,7 @@ def tile_list_replay_curiosity_bonus_kernel(
                     acc[half, t][:],
                     lhsT=lhs,
                     lhsT_scale=lhs_s,
-                    rhs=gw[x, a, half][:].bitcast(FP8X4),
+                    rhs=gw[x, a, half].bitcast(FP8X4),
                     rhs_scale=table_plane(x, a, HALF * half, HALF),
                     start=(done[half, t] == 0),
                     stop=(done[half, t] == 2 * PASSES - 1),
@@ -205,7 +217,8 @@ def tile_list_replay_curiosity_bonus_kernel(
 
         def round_w4(b, eng):
             w4_bf[b] = queued(eng, [P, THIRD, PACK], BF16, f"w4_bf{b}")
-            src = w4_raw[:, :, THIRD * b : THIRD * (b + 1)]
+            part = min(b, 1)
+            src = w4_raw[part][:, :, THIRD * (b - part) : THIRD * (b - part + 1)]
             if eng == "scalar":
                 nc.scalar.activation(
                     w4_bf[b][:].rearrange("p (c i) t -> p c t i", i=4),
@@ -243,10 +256,12 @@ def tile_list_replay_curiosity_bonus_kernel(
                         stop=(a == PASSES - 1),
                     )
 
-        def error(c):
+        def subtract(c):
             half, cols = place_in_half(c)
             diff[c] = queued("vector", [P, PACK, CHUNK], F32, f"diff{c}")
             nc.vector.tensor_tensor(diff[c][:], pred[half][:, :, cols], feat[c][:], ALU.subtract)
+
+        def square(c):
             sq[c] = queued("scalar", [P, CHUNK, PACK], F32, f"sq{c}")
             nc.scalar.activation(
                 sq[c][:].rearrange("p (c i) t -> p c t i", i=4),
@@ -316,75 +331,83 @@ def tile_list_replay_curiosity_bonus_kernel(
         load_words(1)
         move_scales(moves[1])
         nc.sync.dma_start(w3_raw[:], w3_words.rearrange("a p n i -> p a (n i)").bitcast(I32))
+        move_scales(moves[2])
         load_w4(0)
         load_w4(1)
-        move_scales(moves[2])
-        load_w4(2)
-        load_w4(3)
         reorder_scales(2)
         reorder_words(2, w2_raw, 2)
         reorder_scales(3)
+        reorder_words(3, w3_raw, 4)
         spread_constants()
         round_w1(0)
         round_w1(1)
 
-        gather_words(ACTION, 0, FIRST)
-        gather_words(STATE, 0, FIRST)
-        gather_words(ACTION, 0, SECOND)
+        gather_list(ACTION, 0)
+        gather_list(STATE, 0)
         quantize_w1(0)
-        p_pass(ACTION, 0, FIRST)
-        p_pass(STATE, 0, FIRST)
-        p_pass(ACTION, 0, SECOND)
-        gather_words(STATE, 0, SECOND)
-        p_pass(STATE, 0, SECOND)
         quantize_w1(1)
-        gather_words(NEXT, 0, FIRST)
-
-        for half in (FIRST, SECOND):
-            for x in (ACTION, STATE):
-                gather_words(x, 1, half)
-                p_pass(x, 1, half)
-            predict(half)
-            if half == FIRST:
-                reorder_words(3, w3_raw, 4)
-        round_w4(1, "gpsimd")
+        for x in (ACTION, STATE):
+            p_pass(x, 0, FIRST)
+        gather_list(NEXT, 0)
+        for x in (ACTION, STATE):
+            gather_words(x, 1, FIRST)
+            p_pass(x, 1, FIRST)
+        round_w4(0, "scalar")
+        predict(FIRST)
         gather_words(NEXT, 1, FIRST)
         for c in range(HALF // CHUNK):
             features(c)
-        gather_words(NEXT, 0, SECOND)
+        for x in (ACTION, STATE):
+            gather_words(x, 1, SECOND)
+        for t in range(PACK):
+            for a in range(PASSES):
+                for x in (ACTION, STATE):
+                    p_pass(x, a, SECOND, (t,))
+        round_w4(2, "gpsimd")
+        round_w4(1, "scalar")
 
-        error(0)
+        for c in range(4):
+            subtract(c)
+            square(c)
         weigh(0, nc.gpsimd)
-        error(1)
-        round_w4(0, "scalar")
+        weigh(1, nc.gpsimd)
         gather_words(NEXT, 1, SECOND)
+        predict(SECOND)
         features(4)
         features(5)
-        error(2)
-        round_w4(2, "scalar")
-        weigh(1, nc.vector)
-        quantize_w4(0)
-        quantize_w4(1)
+        for b in range(3):
+            quantize_w4(b)
         quantize_h(0)
-        readout(0, (0, 1))
+        readout(0, (0, 1, 2))
+        features(6)
+        features(7)
 
-        last = GROUPS - 1
-        for group in range(1, GROUPS):
-            weigh(2 * group, nc.gpsimd)
-            error(2 * group + 1)
-            if group == 1:
-                features(6)
-                features(7)
-            finish(group - 1, 0, "scalar")
-            if group < last:
-                error(2 * group + 2)
-            finish(group - 1, 1, "vector")
-            weigh(2 * group + 1, nc.vector)
-            if group == 1:
-                quantize_w4(2)
-                readout(0, (2,))
-            finish(group - 1, 2, "scalar")
-            quantize_h(group)
-            if group < last:
-                readout(group, (0, 1, 2))
-        last_readout(last)
+        weigh(2, nc.gpsimd)
+        weigh(3, nc.gpsimd)
+        subtract(4)
+        subtract(5)
+        finish(0, 0, "scalar")
+        finish(0, 1, "scalar")
+        subtract(6)
+        subtract(7)
+        square(4)
+        square(5)
+        finish(0, 2, "scalar")
+        quantize_h(1)
+        readout(1, (0, 1, 2))
+        weigh(4, nc.gpsimd)
+        square(6)
+        square(7)
+        finish(1, 0, "vector")
+        finish(1, 1, "vector")
+        weigh(5, nc.vector)
+        finish(1, 2, "scalar")
+        quantize_h(2)
+        readout(2, (0, 1, 2))
+        weigh(6, nc.vector)
+        weigh(7, nc.vector)
+        finish(2, 0, "scalar")
+        finish(2, 1, "scalar")
+        quantize_h(3)
+        finish(2, 2, "vector")
+        last_readout(3)

@@ -31,10 +31,10 @@ RUN = 4
 STATE, ACTION, NEXT = 0, 1, 2
 FIRST, SECOND = 0, 1
 BANKS = 8
-QUEUE_DEPTH = {"vector": 18, "scalar": 8, "gpsimd": 9}
+QUEUE_DEPTH = {"vector": 17, "scalar": 8, "gpsimd": 9}
 SCALE_ROW0 = 96
 WEIGHT_OFFSET = {2: 0, 3: 8}
-MOVE_OFFSET = (0, 0, 4)
+MOVE_OFFSET = (0, 0)
 
 
 def tile_list_replay_curiosity_bonus_kernel(
@@ -55,14 +55,15 @@ def tile_list_replay_curiosity_bonus_kernel(
         lists = [keep.tile([P, S // 16], U16, name=f"list{x}") for x in range(3)]
         window = keep.tile([P, T // 4], I32, name="tsc")
         picked = keep.tile([P, 3 * S], U8, name="picked")
-        moves = [(0, STATE, NEXT), (1, STATE, NEXT + 1), (0, NEXT, NEXT + 1)]
+        moves = [(0, STATE, NEXT + 1), (1, STATE, NEXT + 1)]
         planes = {
             move: keep.tile([P, S // 4 * (move[2] - move[1])], I32, name=f"planes{i}", align_bytes=64)
             for i, move in enumerate(moves)
         }
         wsc_raw = {}
         nc.vector.memset(window[0:SCALE_ROW0, :], 0)
-        rows = keep.tile([P, P], F32, name="rows")
+        g_row = keep.tile([1, H], F32, name="g_row")
+        rows = keep.tile([P, H], F32, name="rows")
         nc.gpsimd.memset(rows[:], 0.0)
         ident = keep.tile([P, P], F32, name="ident")
         make_identity(nc, ident[:])
@@ -73,7 +74,7 @@ def tile_list_replay_curiosity_bonus_kernel(
         w1_raw = [keep.tile([P, PACK, H], F32, name=f"w1_raw{a}") for a in range(PASSES)]
         w2_raw = keep.tile([P, PASSES, H // 2], I32, name="w2_raw")
         w3_raw = keep.tile([P, PASSES, H], I32, name="w3_raw")
-        w4_parts = [(0, THIRD), (THIRD, N)]
+        w4_parts = [(0, N)]
         w4_raw = [keep.tile([P, PACK, n1 - n0], F32, name=f"w4_raw{n0}") for n0, n1 in w4_parts]
 
         def load_words(a):
@@ -101,17 +102,14 @@ def tile_list_replay_curiosity_bonus_kernel(
         nc.sync.dma_start(lists[ACTION][:], offs2)
         nc.sync.dma_start(lists[STATE][:], offs)
         nc.sync.dma_start(lists[NEXT][:], offs3)
-        nc.scalar.dma_start(
-            rows[0:PACK, :].rearrange("t (c i) -> t c i", i=4), g.rearrange("(c t i) -> t c i", t=PACK, i=4)
-        )
+        nc.scalar.dma_start(g_row[:], g.rearrange("(o r) -> o r", o=1))
         bias_rows = b4.rearrange("(u p) -> u p", p=P)
-        nc.scalar.dma_start(rows[PACK : 2 * PACK, :], bias_rows[0:PACK])
-        nc.scalar.dma_start(rows[2 * PACK : PACK + ROW_TILES, :], bias_rows[PACK:ROW_TILES])
+        nc.scalar.dma_start(rows[PACK : 2 * PACK, 0:P], bias_rows[0:PACK])
+        nc.scalar.dma_start(rows[2 * PACK : PACK + ROW_TILES, 0:P], bias_rows[PACK:ROW_TILES])
+        nc.vector.memset(planes[moves[0]][:], 0)
         load_weight_scales(2, w2_scales)
         load_weight_scales(3, w3_scales)
-        nc.vector.memset(planes[moves[0]][:], 0)
-        for move in moves[1:]:
-            nc.gpsimd.memset(planes[move][:], 0)
+        nc.gpsimd.memset(planes[moves[1]][:], 0)
         load_words(0)
         nc.sync.dma_start(w2_raw[:], w2_words.rearrange("a p n -> p a n").bitcast(I32))
         load_w1(0)
@@ -158,9 +156,16 @@ def tile_list_replay_curiosity_bonus_kernel(
             return planes[move][MOVE_OFFSET[moves.index(move)] :, :].bitcast(U8)[:, first : first + width]
 
         def spread_constants():
-            cols = bank([P, P], "cols")
-            nc.tensor.transpose(cols[:], rows[:], ident[:])
-            nc.scalar.activation(consts[:], cols[:, 0:PACK + ROW_TILES], ACT.Copy)
+            nc.scalar.activation(
+                rows[0:1, :].rearrange("o (t c i) -> o t c i", t=PACK, i=4),
+                g_row[:].rearrange("o (c t i) -> o t c i", t=PACK, i=4),
+                ACT.Copy,
+            )
+            cols = bank([P, PACK, P], "cols")
+            for t in range(PACK):
+                nc.tensor.transpose(cols[:, t, :], rows[:, P * t : P * (t + 1)], ident[:])
+            nc.scalar.activation(gain, cols[:, :, 0], ACT.Copy)
+            nc.scalar.activation(consts[:, PACK:], cols[:, 0, PACK : PACK + ROW_TILES], ACT.Copy)
 
         def gather_words(x, a, half):
             picked_words = queued("vector", [P, HALF], U32, f"gw{x}{a}{half}")
@@ -217,7 +222,7 @@ def tile_list_replay_curiosity_bonus_kernel(
 
         def round_w4(b, eng):
             w4_bf[b] = queued(eng, [P, THIRD, PACK], BF16, f"w4_bf{b}")
-            part = min(b, 1)
+            part = 0
             src = w4_raw[part][:, :, THIRD * (b - part) : THIRD * (b - part + 1)]
             if eng == "scalar":
                 nc.scalar.activation(
@@ -331,9 +336,7 @@ def tile_list_replay_curiosity_bonus_kernel(
         load_words(1)
         move_scales(moves[1])
         nc.sync.dma_start(w3_raw[:], w3_words.rearrange("a p n i -> p a (n i)").bitcast(I32))
-        move_scales(moves[2])
         load_w4(0)
-        load_w4(1)
         reorder_scales(2)
         reorder_words(2, w2_raw, 2)
         reorder_scales(3)
@@ -342,17 +345,19 @@ def tile_list_replay_curiosity_bonus_kernel(
         round_w1(0)
         round_w1(1)
 
-        gather_list(ACTION, 0)
-        gather_list(STATE, 0)
+        for x in (ACTION, STATE):
+            gather_words(x, 0, FIRST)
+        gather_list(NEXT, 0)
         quantize_w1(0)
         quantize_w1(1)
         for x in (ACTION, STATE):
             p_pass(x, 0, FIRST)
-        gather_list(NEXT, 0)
+        for x in (ACTION, STATE):
+            gather_words(x, 0, SECOND)
+            p_pass(x, 0, SECOND, range(PACK - 1))
         for x in (ACTION, STATE):
             gather_words(x, 1, FIRST)
             p_pass(x, 1, FIRST)
-        round_w4(0, "scalar")
         predict(FIRST)
         gather_words(NEXT, 1, FIRST)
         for c in range(HALF // CHUNK):
@@ -362,17 +367,22 @@ def tile_list_replay_curiosity_bonus_kernel(
         for t in range(PACK):
             for a in range(PASSES):
                 for x in (ACTION, STATE):
-                    p_pass(x, a, SECOND, (t,))
+                    if a == 1 or t == PACK - 1:
+                        p_pass(x, a, SECOND, (t,))
         round_w4(2, "gpsimd")
-        round_w4(1, "scalar")
+        round_w4(0, "scalar")
 
-        for c in range(4):
+        for c in range(2):
             subtract(c)
             square(c)
-        weigh(0, nc.gpsimd)
-        weigh(1, nc.gpsimd)
-        gather_words(NEXT, 1, SECOND)
+            weigh(c, nc.gpsimd)
+        for c in range(2, 4):
+            subtract(c)
+        round_w4(1, "scalar")
         predict(SECOND)
+        for c in range(2, 4):
+            square(c)
+        gather_words(NEXT, 1, SECOND)
         features(4)
         features(5)
         for b in range(3):
@@ -384,30 +394,20 @@ def tile_list_replay_curiosity_bonus_kernel(
 
         weigh(2, nc.gpsimd)
         weigh(3, nc.gpsimd)
-        subtract(4)
-        subtract(5)
+        for c in range(4, 8):
+            subtract(c)
         finish(0, 0, "scalar")
         finish(0, 1, "scalar")
-        subtract(6)
-        subtract(7)
-        square(4)
-        square(5)
-        finish(0, 2, "scalar")
+        finish(0, 2, "vector")
+        for c in range(4, 8):
+            square(c)
         quantize_h(1)
-        readout(1, (0, 1, 2))
-        weigh(4, nc.gpsimd)
-        square(6)
-        square(7)
-        finish(1, 0, "vector")
-        finish(1, 1, "vector")
-        weigh(5, nc.vector)
-        finish(1, 2, "scalar")
-        quantize_h(2)
-        readout(2, (0, 1, 2))
-        weigh(6, nc.vector)
-        weigh(7, nc.vector)
-        finish(2, 0, "scalar")
-        finish(2, 1, "scalar")
-        quantize_h(3)
-        finish(2, 2, "vector")
+        for group in (1, 2):
+            readout(group, (0, 1, 2))
+            weigh(2 * group + 2, nc.vector)
+            weigh(2 * group + 3, nc.vector)
+            finish(group, 0, "vector")
+            finish(group, 1, "scalar")
+            finish(group, 2, "scalar")
+            quantize_h(group + 1)
         last_readout(3)

@@ -31,6 +31,7 @@ RUN = 4
 STATE, ACTION, NEXT = 0, 1, 2
 FIRST, SECOND = 0, 1
 BANKS = 8
+EARLY_SLOTS = 2
 QUEUE_DEPTH = {"vector": 17, "scalar": 8, "gpsimd": 9}
 SCALE_ROW0 = 96
 WEIGHT_OFFSET = {2: 0, 3: 8}
@@ -74,7 +75,7 @@ def tile_list_replay_curiosity_bonus_kernel(
         w1_raw = [keep.tile([P, PACK, H], F32, name=f"w1_raw{a}") for a in range(PASSES)]
         w2_raw = keep.tile([P, PASSES, H // 2], I32, name="w2_raw")
         w3_raw = keep.tile([P, PASSES, H], I32, name="w3_raw")
-        w4_parts = [(0, N)]
+        w4_parts = [(0, 2 * THIRD), (2 * THIRD, N)]
         w4_raw = [keep.tile([P, PACK, n1 - n0], F32, name=f"w4_raw{n0}") for n0, n1 in w4_parts]
 
         def load_words(a):
@@ -215,15 +216,15 @@ def tile_list_replay_curiosity_bonus_kernel(
                 )
                 done[half, t] = done[half, t] + 1
 
-        def predict(half):
+        def predict(half, width):
             pred[half] = queued("scalar", [P, PACK, HALF], F32, f"pred{half}")
-            for t in range(PACK):
-                nc.scalar.activation(pred[half][:, t, :], acc[half, t][:], ACT.Tanh)
+            for j0 in range(0, HALF, width):
+                for t in range(PACK):
+                    nc.scalar.activation(pred[half][:, t, j0 : j0 + width], acc[half, t][:, j0 : j0 + width], ACT.Tanh)
 
         def round_w4(b, eng):
             w4_bf[b] = queued(eng, [P, THIRD, PACK], BF16, f"w4_bf{b}")
-            part = 0
-            src = w4_raw[part][:, :, THIRD * (b - part) : THIRD * (b - part + 1)]
+            src = w4_raw[b // 2][:, :, THIRD * (b % 2) : THIRD * (b % 2 + 1)]
             if eng == "scalar":
                 nc.scalar.activation(
                     w4_bf[b][:].rearrange("p (c i) t -> p c t i", i=4),
@@ -336,6 +337,7 @@ def tile_list_replay_curiosity_bonus_kernel(
         load_words(1)
         move_scales(moves[1])
         nc.sync.dma_start(w3_raw[:], w3_words.rearrange("a p n i -> p a (n i)").bitcast(I32))
+        load_w4(1)
         load_w4(0)
         reorder_scales(2)
         reorder_words(2, w2_raw, 2)
@@ -354,60 +356,66 @@ def tile_list_replay_curiosity_bonus_kernel(
             p_pass(x, 0, FIRST)
         for x in (ACTION, STATE):
             gather_words(x, 0, SECOND)
-            p_pass(x, 0, SECOND, range(PACK - 1))
+            p_pass(x, 0, SECOND, range(EARLY_SLOTS))
         for x in (ACTION, STATE):
             gather_words(x, 1, FIRST)
             p_pass(x, 1, FIRST)
-        predict(FIRST)
+        predict(FIRST, GROUP)
         gather_words(NEXT, 1, FIRST)
         for c in range(HALF // CHUNK):
             features(c)
-        for x in (ACTION, STATE):
-            gather_words(x, 1, SECOND)
-        for t in range(PACK):
-            for a in range(PASSES):
-                for x in (ACTION, STATE):
-                    if a == 1 or t == PACK - 1:
-                        p_pass(x, a, SECOND, (t,))
         round_w4(2, "gpsimd")
-        round_w4(0, "scalar")
-
+        gather_words(ACTION, 1, SECOND)
         for c in range(2):
             subtract(c)
             square(c)
             weigh(c, nc.gpsimd)
+        gather_words(STATE, 1, SECOND)
+        for x in (ACTION, STATE):
+            p_pass(x, 0, SECOND, range(EARLY_SLOTS, PACK))
+        for x in (ACTION, STATE):
+            p_pass(x, 1, SECOND)
+        round_w4(0, "scalar")
         for c in range(2, 4):
             subtract(c)
         round_w4(1, "scalar")
-        predict(SECOND)
         for c in range(2, 4):
             square(c)
+        predict(SECOND, HALF)
         gather_words(NEXT, 1, SECOND)
-        features(4)
-        features(5)
-        for b in range(3):
-            quantize_w4(b)
+        quantize_w4(0)
+        quantize_w4(1)
         quantize_h(0)
+        quantize_w4(2)
         readout(0, (0, 1, 2))
-        features(6)
-        features(7)
+        for c in range(HALF // CHUNK, S // CHUNK):
+            features(c)
 
         weigh(2, nc.gpsimd)
         weigh(3, nc.gpsimd)
-        for c in range(4, 8):
+        finish(0, 0, "vector")
+        finish(0, 1, "vector")
+        finish(0, 2, "scalar")
+        for c in (4, 5):
             subtract(c)
-        finish(0, 0, "scalar")
-        finish(0, 1, "scalar")
-        finish(0, 2, "vector")
-        for c in range(4, 8):
             square(c)
         quantize_h(1)
-        for group in (1, 2):
-            readout(group, (0, 1, 2))
-            weigh(2 * group + 2, nc.vector)
-            weigh(2 * group + 3, nc.vector)
-            finish(group, 0, "vector")
-            finish(group, 1, "scalar")
-            finish(group, 2, "scalar")
-            quantize_h(group + 1)
+        readout(1, (0, 1, 2))
+        weigh(4, nc.vector)
+        weigh(5, nc.vector)
+        finish(1, 0, "scalar")
+        finish(1, 1, "scalar")
+        subtract(6)
+        quantize_h(2)
+        readout(2, (0, 1, 2))
+        subtract(7)
+        square(6)
+        square(7)
+        finish(2, 0, "vector")
+        finish(1, 2, "scalar")
+        weigh(6, nc.vector)
+        weigh(7, nc.vector)
+        finish(2, 1, "scalar")
+        finish(2, 2, "scalar")
+        quantize_h(3)
         last_readout(3)

@@ -24,6 +24,7 @@ HALF = 512
 CHUNK = 128
 GROUP = 256
 GROUPS = S // GROUP
+NEIGHBOURS = 4
 THIRD = N // 3
 ROW_TILES = N // P
 QUADRANT = 32
@@ -33,9 +34,8 @@ FIRST, SECOND = 0, 1
 BANKS = 8
 EARLY_SLOTS = 2
 QUEUE_DEPTH = {"vector": 17, "scalar": 8, "gpsimd": 9}
-SCALE_ROW0 = 96
+SCALE_ROW0 = P - QUADRANT
 WEIGHT_OFFSET = {2: 0, 3: 8}
-MOVE_OFFSET = (0, 0)
 
 
 def tile_list_replay_curiosity_bonus_kernel(
@@ -56,11 +56,7 @@ def tile_list_replay_curiosity_bonus_kernel(
         lists = [keep.tile([P, S // 16], U16, name=f"list{x}") for x in range(3)]
         window = keep.tile([P, T // 4], I32, name="tsc")
         picked = keep.tile([P, 3 * S], U8, name="picked")
-        moves = [(0, STATE, NEXT + 1), (1, STATE, NEXT + 1)]
-        planes = {
-            move: keep.tile([P, S // 4 * (move[2] - move[1])], I32, name=f"planes{i}", align_bytes=64)
-            for i, move in enumerate(moves)
-        }
+        planes = [keep.tile([P, 3 * S // 4], I32, name=f"planes{a}", align_bytes=64) for a in range(PASSES)]
         wsc_raw = {}
         nc.vector.memset(window[0:SCALE_ROW0, :], 0)
         g_row = keep.tile([1, H], F32, name="g_row")
@@ -96,8 +92,9 @@ def tile_list_replay_curiosity_bonus_kernel(
 
         def load_w4(part):
             n0, n1 = w4_parts[part]
+            by_slot = w4.rearrange("(c t i) n -> t c i n", t=PACK, i=NEIGHBOURS)
             for t in range(PACK):
-                nc.sync.dma_start(w4_raw[part][:, t, :], w4.rearrange("(c t i) n -> t c i n", t=PACK, i=4)[t][:, :, n0:n1])
+                nc.sync.dma_start(w4_raw[part][:, t, :], by_slot[t][:, :, n0:n1])
 
         nc.sync.dma_start(window[SCALE_ROW0:P, :], tab_scales.rearrange("a q n -> (a q) n").bitcast(I32))
         nc.sync.dma_start(lists[ACTION][:], offs2)
@@ -107,10 +104,10 @@ def tile_list_replay_curiosity_bonus_kernel(
         bias_rows = b4.rearrange("(u p) -> u p", p=P)
         nc.scalar.dma_start(rows[PACK : 2 * PACK, 0:P], bias_rows[0:PACK])
         nc.scalar.dma_start(rows[2 * PACK : PACK + ROW_TILES, 0:P], bias_rows[PACK:ROW_TILES])
-        nc.vector.memset(planes[moves[0]][:], 0)
+        nc.vector.memset(planes[0][:], 0)
         load_weight_scales(2, w2_scales)
         load_weight_scales(3, w3_scales)
-        nc.gpsimd.memset(planes[moves[1]][:], 0)
+        nc.gpsimd.memset(planes[1][:], 0)
         load_words(0)
         nc.sync.dma_start(w2_raw[:], w2_words.rearrange("a p n -> p a n").bitcast(I32))
         load_w1(0)
@@ -142,31 +139,27 @@ def tile_list_replay_curiosity_bonus_kernel(
         def gather_scales(x):
             nc.vector.tensor_copy(picked[:, S * x : S * (x + 1)], window[:].bitcast(U8).indirect(lists[x][:]))
 
-        def move_scales(move):
-            a, x0, x1 = move
+        def move_scales(a):
             for r in range(RUN):
                 first = SCALE_ROW0 + 16 * a + r
                 nc.sync.dma_start(
-                    planes[move][MOVE_OFFSET[moves.index(move)] + r : P : QUADRANT, :],
-                    picked[first : first + 3 * RUN + 1 : RUN, S * x0 : S * x1].bitcast(I32),
+                    planes[a][r:P:QUADRANT, :], picked[first : first + 3 * RUN + 1 : RUN, :].bitcast(I32)
                 )
 
         def table_plane(x, a, j0, width):
-            move = [m for m in moves if m[0] == a and m[1] <= x < m[2]][0]
-            first = S * (x - move[1]) + j0
-            return planes[move][MOVE_OFFSET[moves.index(move)] :, :].bitcast(U8)[:, first : first + width]
+            return planes[a][:].bitcast(U8)[:, S * x + j0 : S * x + j0 + width]
 
         def spread_constants():
             nc.scalar.activation(
-                rows[0:1, :].rearrange("o (t c i) -> o t c i", t=PACK, i=4),
-                g_row[:].rearrange("o (c t i) -> o t c i", t=PACK, i=4),
+                rows[0:1, :].rearrange("o (t c i) -> o t c i", t=PACK, i=NEIGHBOURS),
+                g_row[:].rearrange("o (c t i) -> o t c i", t=PACK, i=NEIGHBOURS),
                 ACT.Copy,
             )
-            cols = bank([P, PACK, P], "cols")
+            turned = bank([P, PACK, P], "turned")
             for t in range(PACK):
-                nc.tensor.transpose(cols[:, t, :], rows[:, P * t : P * (t + 1)], ident[:])
-            nc.scalar.activation(gain, cols[:, :, 0], ACT.Copy)
-            nc.scalar.activation(consts[:, PACK:], cols[:, 0, PACK : PACK + ROW_TILES], ACT.Copy)
+                nc.tensor.transpose(turned[:, t, :], rows[:, P * t : P * (t + 1)], ident[:])
+            nc.scalar.activation(gain, turned[:, :, 0], ACT.Copy)
+            nc.scalar.activation(consts[:, PACK:], turned[:, 0, PACK : PACK + ROW_TILES], ACT.Copy)
 
         def gather_words(x, a, half):
             picked_words = queued("vector", [P, HALF], U32, f"gw{x}{a}{half}")
@@ -181,8 +174,8 @@ def tile_list_replay_curiosity_bonus_kernel(
                 gw[x, a, half] = picked_words[:, HALF * half : HALF * (half + 1)]
 
         def round_w1(a):
-            src = w1_raw[a][:].rearrange("p j (c t i) -> p t c j i", t=PACK, i=4)
-            w1_bf[a] = queued("scalar", [P, PACK, P // 4, 4, PACK], BF16, f"w1_bf{a}")
+            src = w1_raw[a][:].rearrange("p j (c t i) -> p t c j i", t=PACK, i=NEIGHBOURS)
+            w1_bf[a] = queued("scalar", [P, PACK, P // NEIGHBOURS, NEIGHBOURS, PACK], BF16, f"w1_bf{a}")
             for t in range(PACK):
                 nc.scalar.activation(w1_bf[a][:, t].rearrange("p c i j -> p c j i"), src[:, t], ACT.Copy)
 
@@ -220,17 +213,20 @@ def tile_list_replay_curiosity_bonus_kernel(
             pred[half] = queued("scalar", [P, PACK, HALF], F32, f"pred{half}")
             for j0 in range(0, HALF, width):
                 for t in range(PACK):
-                    nc.scalar.activation(pred[half][:, t, j0 : j0 + width], acc[half, t][:, j0 : j0 + width], ACT.Tanh)
+                    cols = slice(j0, j0 + width)
+                    nc.scalar.activation(pred[half][:, t, cols], acc[half, t][:, cols], ACT.Tanh)
 
         def round_w4(b, eng):
             w4_bf[b] = queued(eng, [P, THIRD, PACK], BF16, f"w4_bf{b}")
             src = w4_raw[b // 2][:, :, THIRD * (b % 2) : THIRD * (b % 2 + 1)]
+            by_fours = (
+                w4_bf[b][:].rearrange("p (c i) t -> p c t i", i=NEIGHBOURS),
+                src.rearrange("p t (c i) -> p c t i", i=NEIGHBOURS),
+            )
             if eng == "scalar":
-                nc.scalar.activation(
-                    w4_bf[b][:].rearrange("p (c i) t -> p c t i", i=4),
-                    src.rearrange("p t (c i) -> p c t i", i=4),
-                    ACT.Copy,
-                )
+                nc.scalar.activation(*by_fours, ACT.Copy)
+            elif eng == "vector":
+                nc.vector.tensor_copy(*by_fours)
             else:
                 nc.gpsimd.tensor_scalar(w4_bf[b][:], src.rearrange("p t n -> p n t"), 1.0, 0.0, ALU.mult, ALU.add)
 
@@ -270,8 +266,8 @@ def tile_list_replay_curiosity_bonus_kernel(
         def square(c):
             sq[c] = queued("scalar", [P, CHUNK, PACK], F32, f"sq{c}")
             nc.scalar.activation(
-                sq[c][:].rearrange("p (c i) t -> p c t i", i=4),
-                diff[c][:].rearrange("p t (c i) -> p c t i", i=4),
+                sq[c][:].rearrange("p (c i) t -> p c t i", i=NEIGHBOURS),
+                diff[c][:].rearrange("p t (c i) -> p c t i", i=NEIGHBOURS),
                 ACT.Square,
             )
 
@@ -312,10 +308,11 @@ def tile_list_replay_curiosity_bonus_kernel(
             y = ys[group, b]
             if eng == "vector":
                 nc.vector.tensor_tensor(res[:], y[:], bias.unsqueeze(2).to_broadcast([P, 2, GROUP]), ALU.add)
+                nc.sync.dma_start(out_v[:, 2 * b : 2 * b + 2, GROUP * group : GROUP * (group + 1)], res[:])
             else:
                 for e in range(2):
                     nc.scalar.activation(res[:, e, :], y[:, e, :], ACT.Identity, bias=bias[:, e : e + 1])
-            nc.sync.dma_start(out_v[:, 2 * b : 2 * b + 2, GROUP * group : GROUP * (group + 1)], res[:])
+                    nc.sync.dma_start(out_v[:, 2 * b + e, GROUP * group : GROUP * (group + 1)], res[:, e, :])
 
         def last_readout(group):
             y = [bank([P, GROUP], f"y{group}{u}") for u in range(ROW_TILES)]
@@ -333,9 +330,9 @@ def tile_list_replay_curiosity_bonus_kernel(
 
         for x in (ACTION, STATE, NEXT):
             gather_scales(x)
-        move_scales(moves[0])
+        move_scales(0)
         load_words(1)
-        move_scales(moves[1])
+        move_scales(1)
         nc.sync.dma_start(w3_raw[:], w3_words.rearrange("a p n i -> p a (n i)").bitcast(I32))
         load_w4(1)
         load_w4(0)
@@ -357,6 +354,7 @@ def tile_list_replay_curiosity_bonus_kernel(
         for x in (ACTION, STATE):
             gather_words(x, 0, SECOND)
             p_pass(x, 0, SECOND, range(EARLY_SLOTS))
+
         for x in (ACTION, STATE):
             gather_words(x, 1, FIRST)
             p_pass(x, 1, FIRST)
@@ -366,7 +364,7 @@ def tile_list_replay_curiosity_bonus_kernel(
             features(c)
         round_w4(2, "gpsimd")
         gather_words(ACTION, 1, SECOND)
-        for c in range(2):
+        for c in (0, 1):
             subtract(c)
             square(c)
             weigh(c, nc.gpsimd)
@@ -376,44 +374,47 @@ def tile_list_replay_curiosity_bonus_kernel(
         for x in (ACTION, STATE):
             p_pass(x, 1, SECOND)
         round_w4(0, "scalar")
-        for c in range(2, 4):
+        for c in (2, 3):
             subtract(c)
-        round_w4(1, "scalar")
-        for c in range(2, 4):
+        for c in (2, 3):
             square(c)
         predict(SECOND, HALF)
         gather_words(NEXT, 1, SECOND)
-        quantize_w4(0)
-        quantize_w4(1)
-        quantize_h(0)
+        features(4)
+        features(5)
+
+        round_w4(1, "vector")
         quantize_w4(2)
-        readout(0, (0, 1, 2))
-        for c in range(HALF // CHUNK, S // CHUNK):
-            features(c)
+        quantize_w4(0)
+        quantize_h(0)
+        quantize_w4(1)
+        readout(0, (2, 0, 1))
+        features(6)
+        features(7)
 
         weigh(2, nc.gpsimd)
         weigh(3, nc.gpsimd)
-        finish(0, 0, "vector")
-        finish(0, 1, "vector")
         finish(0, 2, "scalar")
+        finish(0, 0, "scalar")
         for c in (4, 5):
             subtract(c)
             square(c)
+        finish(0, 1, "vector")
+        subtract(6)
+        square(6)
         quantize_h(1)
         readout(1, (0, 1, 2))
+
         weigh(4, nc.vector)
         weigh(5, nc.vector)
-        finish(1, 0, "scalar")
-        finish(1, 1, "scalar")
-        subtract(6)
+        for b in range(3):
+            finish(1, b, "scalar")
+        subtract(7)
+        square(7)
         quantize_h(2)
         readout(2, (0, 1, 2))
-        subtract(7)
-        square(6)
-        square(7)
-        finish(2, 0, "vector")
-        finish(1, 2, "scalar")
         weigh(6, nc.vector)
+        finish(2, 0, "vector")
         weigh(7, nc.vector)
         finish(2, 1, "scalar")
         finish(2, 2, "scalar")

@@ -32,8 +32,8 @@ RUN = 4
 STATE, ACTION, NEXT = 0, 1, 2
 FIRST, SECOND = 0, 1
 BANKS = 8
-EARLY_SLOTS = 2
-QUEUE_DEPTH = {"vector": 17, "scalar": 8, "gpsimd": 9}
+PAIR = 2
+QUEUE_DEPTH = {"vector": 30, "scalar": 16, "gpsimd": 9}
 SCALE_ROW0 = P - QUADRANT
 WEIGHT_OFFSET = {2: 0, 3: 8}
 
@@ -71,8 +71,7 @@ def tile_list_replay_curiosity_bonus_kernel(
         w1_raw = [keep.tile([P, PACK, H], F32, name=f"w1_raw{a}") for a in range(PASSES)]
         w2_raw = keep.tile([P, PASSES, H // 2], I32, name="w2_raw")
         w3_raw = keep.tile([P, PASSES, H], I32, name="w3_raw")
-        w4_parts = [(0, 2 * THIRD), (2 * THIRD, N)]
-        w4_raw = [keep.tile([P, PACK, n1 - n0], F32, name=f"w4_raw{n0}") for n0, n1 in w4_parts]
+        w4_raw = [keep.tile([P, PACK, THIRD], F32, name=f"w4_raw{b}") for b in range(3)]
 
         def load_words(a):
             nc.sync.dma_start(words[a][:], tab_words[a].rearrange("p t i -> p (t i)").bitcast(I32))
@@ -90,11 +89,10 @@ def tile_list_replay_curiosity_bonus_kernel(
                     scales.rearrange("a (q r) n -> r q a n", r=RUN)[r].bitcast(I32),
                 )
 
-        def load_w4(part):
-            n0, n1 = w4_parts[part]
+        def load_w4(b):
             by_slot = w4.rearrange("(c t i) n -> t c i n", t=PACK, i=NEIGHBOURS)
             for t in range(PACK):
-                nc.sync.dma_start(w4_raw[part][:, t, :], by_slot[t][:, :, n0:n1])
+                nc.sync.dma_start(w4_raw[b][:, t, :], by_slot[t][:, :, THIRD * b : THIRD * (b + 1)])
 
         nc.sync.dma_start(window[SCALE_ROW0:P, :], tab_scales.rearrange("a q n -> (a q) n").bitcast(I32))
         nc.sync.dma_start(lists[ACTION][:], offs2)
@@ -121,20 +119,21 @@ def tile_list_replay_curiosity_bonus_kernel(
         gw, w1_bf, w1q, wp, wsc, acc, done = {}, {}, {}, {}, {}, {}, {}
         pred, feat, diff, sq, hb, hq, w4_bf, w4q, ys = {}, {}, {}, {}, {}, {}, {}, {}, {}
 
-        def reorder_scales(w):
-            wsc[w] = queued("gpsimd", [P, PASSES, H // 4], I32, f"wsc{w}")
-            nc.gpsimd.tensor_copy(
+        def reorder_scales(w, eng):
+            wsc[w] = queued(eng, [P, PASSES, H // 4], U32, f"wsc{w}")
+            move = nc.gpsimd.tensor_copy if eng == "gpsimd" else nc.scalar.copy
+            move(
                 wsc[w][:].rearrange("p a (t c) -> p a t c", t=PACK),
-                wsc_raw[w][:].rearrange("p a (c t) -> p a t c", t=PACK),
+                wsc_raw[w][:].bitcast(U32).rearrange("p a (c t) -> p a t c", t=PACK),
             )
 
-        def reorder_words(w, raw, span):
-            for a in range(PASSES):
-                wp[w, a] = queued("gpsimd", [P, P * span], I32, f"wp{w}{a}")
-                nc.gpsimd.tensor_copy(
-                    wp[w, a][:].rearrange("p (t c i) -> p t c i", t=PACK, i=span),
-                    raw[:, a, :].rearrange("p (c t i) -> p t c i", t=PACK, i=span),
-                )
+        def reorder_words(w, raw, span, a, eng):
+            wp[w, a] = queued(eng, [P, P * span], U32, f"wp{w}{a}")
+            move = nc.gpsimd.tensor_copy if eng == "gpsimd" else nc.scalar.copy
+            move(
+                wp[w, a][:].rearrange("p (t c i) -> p t c i", t=PACK, i=span),
+                raw[:, a, :].bitcast(U32).rearrange("p (c t i) -> p t c i", t=PACK, i=span),
+            )
 
         def gather_scales(x):
             nc.vector.tensor_copy(picked[:, S * x : S * (x + 1)], window[:].bitcast(U8).indirect(lists[x][:]))
@@ -161,17 +160,13 @@ def tile_list_replay_curiosity_bonus_kernel(
             nc.scalar.activation(gain, turned[:, :, 0], ACT.Copy)
             nc.scalar.activation(consts[:, PACK:], turned[:, 0, PACK : PACK + ROW_TILES], ACT.Copy)
 
-        def gather_words(x, a, half):
-            picked_words = queued("vector", [P, HALF], U32, f"gw{x}{a}{half}")
-            offsets = lists[x][:, HALF // 16 * half : HALF // 16 * (half + 1)]
+        def gather_words(x, a, groups):
+            j0, width = GROUP * groups[0], GROUP * len(groups)
+            picked_words = queued("vector", [P, width], U32, f"gw{x}{a}{groups[0]}")
+            offsets = lists[x][:, j0 // 16 : (j0 + width) // 16]
             nc.vector.tensor_copy(picked_words[:], words[a][:].bitcast(U32).indirect(offsets))
-            gw[x, a, half] = picked_words[:]
-
-        def gather_list(x, a):
-            picked_words = queued("vector", [P, S], U32, f"gw{x}{a}")
-            nc.vector.tensor_copy(picked_words[:], words[a][:].bitcast(U32).indirect(lists[x][:]))
-            for half in (FIRST, SECOND):
-                gw[x, a, half] = picked_words[:, HALF * half : HALF * (half + 1)]
+            for n, group in enumerate(groups):
+                gw[x, a, group] = picked_words[:, GROUP * n : GROUP * (n + 1)]
 
         def round_w1(a):
             src = w1_raw[a][:].rearrange("p j (c t i) -> p t c j i", t=PACK, i=NEIGHBOURS)
@@ -187,11 +182,12 @@ def tile_list_replay_curiosity_bonus_kernel(
                 in_=w1_bf[a][:].rearrange("p t c i j -> p (t c i j)"),
             )
 
-        def p_pass(x, a, half, slots=range(PACK)):
-            for t in slots:
-                if (half, t) not in acc:
-                    acc[half, t] = bank([P, HALF], f"acc{half}{t}")
-                    done[half, t] = 0
+        def p_pass(x, a, group):
+            for t in range(PACK):
+                key = group, t // PAIR
+                if key not in acc:
+                    acc[key] = bank([P, PAIR, GROUP], f"acc{group}{t}")
+                    done[key] = 0
                 m = slice(P * t, P * (t + 1))
                 if x == STATE:
                     lhs, lhs_s = w1q[a][:, m].bitcast(FP8X4), w1s[:, a, m]
@@ -199,26 +195,24 @@ def tile_list_replay_curiosity_bonus_kernel(
                     lhs = wp[2, a][:].bitcast(U8)[:, 2 * P * t : 2 * P * (t + 1)].bitcast(FP4X4)
                     lhs_s = wsc[2][:, a, :].bitcast(U8)[:, m]
                 nc.tensor.matmul_mx(
-                    acc[half, t][:],
+                    acc[key][:, t % PAIR, :],
                     lhsT=lhs,
                     lhsT_scale=lhs_s,
-                    rhs=gw[x, a, half].bitcast(FP8X4),
-                    rhs_scale=table_plane(x, a, HALF * half, HALF),
-                    start=(done[half, t] == 0),
-                    stop=(done[half, t] == 2 * PASSES - 1),
+                    rhs=gw[x, a, group].bitcast(FP8X4),
+                    rhs_scale=table_plane(x, a, GROUP * group, GROUP),
+                    start=(done[key] == 0),
+                    stop=(done[key] == 2 * PASSES * PAIR - 1),
                 )
-                done[half, t] = done[half, t] + 1
+                done[key] = done[key] + 1
 
-        def predict(half, width):
-            pred[half] = queued("scalar", [P, PACK, HALF], F32, f"pred{half}")
-            for j0 in range(0, HALF, width):
-                for t in range(PACK):
-                    cols = slice(j0, j0 + width)
-                    nc.scalar.activation(pred[half][:, t, cols], acc[half, t][:, cols], ACT.Tanh)
+        def predict(group):
+            pred[group] = queued("scalar", [P, PACK, GROUP], F32, f"pred{group}")
+            for b in range(PACK // PAIR):
+                nc.scalar.activation(pred[group][:, PAIR * b : PAIR * (b + 1), :], acc[group, b][:], ACT.Tanh)
 
         def round_w4(b, eng):
             w4_bf[b] = queued(eng, [P, THIRD, PACK], BF16, f"w4_bf{b}")
-            src = w4_raw[b // 2][:, :, THIRD * (b % 2) : THIRD * (b % 2 + 1)]
+            src = w4_raw[b][:]
             by_fours = (
                 w4_bf[b][:].rearrange("p (c i) t -> p c t i", i=NEIGHBOURS),
                 src.rearrange("p t (c i) -> p c t i", i=NEIGHBOURS),
@@ -238,12 +232,12 @@ def tile_list_replay_curiosity_bonus_kernel(
                 in_=w4_bf[b][:].rearrange("p n t -> p (n t)"),
             )
 
-        def place_in_half(c):
-            j0 = CHUNK * c % HALF
-            return CHUNK * c // HALF, slice(j0, j0 + CHUNK)
+        def place_in_group(c):
+            j0 = CHUNK * c % GROUP
+            return CHUNK * c // GROUP, slice(j0, j0 + CHUNK)
 
         def features(c):
-            half, cols = place_in_half(c)
+            group, cols = place_in_group(c)
             feat[c] = bank([P, PACK, CHUNK], f"feat{c}")
             for t in range(PACK):
                 for a in range(PASSES):
@@ -252,16 +246,16 @@ def tile_list_replay_curiosity_bonus_kernel(
                         feat[c][:, t, :],
                         lhsT=wp[3, a][:, m].bitcast(FP8X4),
                         lhsT_scale=wsc[3][WEIGHT_OFFSET[3] :, a, :].bitcast(U8)[:, m],
-                        rhs=gw[NEXT, a, half][:, cols].bitcast(FP8X4),
+                        rhs=gw[NEXT, a, group][:, cols].bitcast(FP8X4),
                         rhs_scale=table_plane(NEXT, a, CHUNK * c, CHUNK),
                         start=(a == 0),
                         stop=(a == PASSES - 1),
                     )
 
         def subtract(c):
-            half, cols = place_in_half(c)
+            group, cols = place_in_group(c)
             diff[c] = queued("vector", [P, PACK, CHUNK], F32, f"diff{c}")
-            nc.vector.tensor_tensor(diff[c][:], pred[half][:, :, cols], feat[c][:], ALU.subtract)
+            nc.vector.tensor_tensor(diff[c][:], pred[group][:, :, cols], feat[c][:], ALU.subtract)
 
         def square(c):
             sq[c] = queued("scalar", [P, CHUNK, PACK], F32, f"sq{c}")
@@ -273,6 +267,8 @@ def tile_list_replay_curiosity_bonus_kernel(
 
         def weigh(c, engine):
             group, c0 = c // 2, CHUNK * (c % 2)
+            if group == GROUPS - 1 and group not in hb:
+                hb[group] = queued("vector", [P, GROUP, PACK], BF16, f"hb{group}")
             if group not in hb:
                 hb[group] = line.tile([P, GROUP, PACK], BF16, name=f"hb{group}", tag="hb", bufs=1, align_bytes=64)
             engine.tensor_tensor(
@@ -334,89 +330,97 @@ def tile_list_replay_curiosity_bonus_kernel(
         load_words(1)
         move_scales(1)
         nc.sync.dma_start(w3_raw[:], w3_words.rearrange("a p n i -> p a (n i)").bitcast(I32))
-        load_w4(1)
-        load_w4(0)
-        reorder_scales(2)
-        reorder_words(2, w2_raw, 2)
-        reorder_scales(3)
-        reorder_words(3, w3_raw, 4)
+        for b in range(3):
+            load_w4(b)
         spread_constants()
         round_w1(0)
+        reorder_scales(2, "scalar")
+        for a in range(PASSES):
+            reorder_words(2, w2_raw, 2, a, "scalar")
+        reorder_scales(3, "gpsimd")
+        reorder_words(3, w3_raw, 4, 0, "gpsimd")
         round_w1(1)
+        reorder_words(3, w3_raw, 4, 1, "scalar")
 
-        for x in (ACTION, STATE):
-            gather_words(x, 0, FIRST)
-        gather_list(NEXT, 0)
-        quantize_w1(0)
-        quantize_w1(1)
-        for x in (ACTION, STATE):
-            p_pass(x, 0, FIRST)
-        for x in (ACTION, STATE):
-            gather_words(x, 0, SECOND)
-            p_pass(x, 0, SECOND, range(EARLY_SLOTS))
+        first, second = (0, 1), (2, 3)
 
+        def close_p(group):
+            for x in (ACTION, STATE):
+                gather_words(x, 1, (group,))
+                p_pass(x, 1, group)
+
+        for half in (first, second):
+            for x in (ACTION, STATE):
+                gather_words(x, 0, half)
+        for a, half in enumerate((first, second)):
+            quantize_w1(a)
+            gather_words(NEXT, 0, half)
         for x in (ACTION, STATE):
-            gather_words(x, 1, FIRST)
-            p_pass(x, 1, FIRST)
-        predict(FIRST, GROUP)
-        gather_words(NEXT, 1, FIRST)
-        for c in range(HALF // CHUNK):
-            features(c)
-        round_w4(2, "gpsimd")
-        gather_words(ACTION, 1, SECOND)
-        for c in (0, 1):
-            subtract(c)
-            square(c)
-            weigh(c, nc.gpsimd)
-        gather_words(STATE, 1, SECOND)
-        for x in (ACTION, STATE):
-            p_pass(x, 0, SECOND, range(EARLY_SLOTS, PACK))
-        for x in (ACTION, STATE):
-            p_pass(x, 1, SECOND)
-        round_w4(0, "scalar")
-        for c in (2, 3):
-            subtract(c)
-        for c in (2, 3):
-            square(c)
-        predict(SECOND, HALF)
-        gather_words(NEXT, 1, SECOND)
+            for group in range(GROUPS):
+                p_pass(x, 0, group)
+
+        close_p(0)
+        predict(0)
+        close_p(1)
+        gather_words(NEXT, 1, first)
+        features(0)
+        features(1)
+        predict(1)
+        round_w4(0, "gpsimd")
+        round_w4(1, "gpsimd")
+        gather_words(NEXT, 1, second)
+        features(2)
+        features(3)
+        subtract(0)
+        square(0)
+        subtract(1)
+        square(1)
+        weigh(0, nc.gpsimd)
+        weigh(1, nc.gpsimd)
+        close_p(2)
+        round_w4(2, "scalar")
         features(4)
         features(5)
-
-        round_w4(1, "vector")
-        quantize_w4(2)
+        subtract(2)
+        subtract(3)
+        predict(2)
+        close_p(3)
+        square(2)
+        square(3)
         quantize_w4(0)
-        quantize_h(0)
         quantize_w4(1)
-        readout(0, (2, 0, 1))
-        features(6)
-        features(7)
-
+        quantize_w4(2)
+        quantize_h(0)
+        readout(0, (0, 1, 2))
         weigh(2, nc.gpsimd)
         weigh(3, nc.gpsimd)
-        finish(0, 2, "scalar")
+        subtract(4)
+        subtract(5)
+        predict(3)
+        features(6)
+        features(7)
         finish(0, 0, "scalar")
-        for c in (4, 5):
-            subtract(c)
-            square(c)
+        square(4)
+        square(5)
         finish(0, 1, "vector")
         subtract(6)
-        square(6)
+        subtract(7)
+        finish(0, 2, "scalar")
         quantize_h(1)
         readout(1, (0, 1, 2))
-
         weigh(4, nc.vector)
         weigh(5, nc.vector)
-        for b in range(3):
-            finish(1, b, "scalar")
-        subtract(7)
+        square(6)
         square(7)
+        finish(1, 0, "scalar")
+        weigh(6, nc.vector)
         quantize_h(2)
         readout(2, (0, 1, 2))
-        weigh(6, nc.vector)
-        finish(2, 0, "vector")
+        finish(1, 1, "scalar")
         weigh(7, nc.vector)
+        finish(1, 2, "scalar")
+        finish(2, 0, "vector")
+        quantize_h(3)
         finish(2, 1, "scalar")
         finish(2, 2, "scalar")
-        quantize_h(3)
         last_readout(3)

@@ -71,7 +71,8 @@ def tile_list_replay_curiosity_bonus_kernel(
         w1_raw = [keep.tile([P, PACK, H], F32, name=f"w1_raw{a}") for a in range(PASSES)]
         w2_raw = keep.tile([P, PASSES, H // 2], I32, name="w2_raw")
         w3_raw = keep.tile([P, PASSES, H], I32, name="w3_raw")
-        w4_raw = [keep.tile([P, PACK, THIRD], F32, name=f"w4_raw{b}") for b in range(3)]
+        w4_parts = [(0, 2 * THIRD), (2 * THIRD, N)]
+        w4_raw = [keep.tile([P, PACK, n1 - n0], F32, name=f"w4_raw{n0}") for n0, n1 in w4_parts]
 
         def load_words(a):
             nc.sync.dma_start(words[a][:], tab_words[a].rearrange("p t i -> p (t i)").bitcast(I32))
@@ -89,10 +90,11 @@ def tile_list_replay_curiosity_bonus_kernel(
                     scales.rearrange("a (q r) n -> r q a n", r=RUN)[r].bitcast(I32),
                 )
 
-        def load_w4(b):
+        def load_w4(part):
+            n0, n1 = w4_parts[part]
             by_slot = w4.rearrange("(c t i) n -> t c i n", t=PACK, i=NEIGHBOURS)
             for t in range(PACK):
-                nc.sync.dma_start(w4_raw[b][:, t, :], by_slot[t][:, :, THIRD * b : THIRD * (b + 1)])
+                nc.sync.dma_start(w4_raw[part][:, t, :], by_slot[t][:, :, n0:n1])
 
         nc.sync.dma_start(window[SCALE_ROW0:P, :], tab_scales.rearrange("a q n -> (a q) n").bitcast(I32))
         nc.sync.dma_start(lists[ACTION][:], offs2)
@@ -212,7 +214,7 @@ def tile_list_replay_curiosity_bonus_kernel(
 
         def round_w4(b, eng):
             w4_bf[b] = queued(eng, [P, THIRD, PACK], BF16, f"w4_bf{b}")
-            src = w4_raw[b][:]
+            src = w4_raw[b // 2][:, :, THIRD * (b % 2) : THIRD * (b % 2 + 1)]
             by_fours = (
                 w4_bf[b][:].rearrange("p (c i) t -> p c t i", i=NEIGHBOURS),
                 src.rearrange("p t (c i) -> p c t i", i=NEIGHBOURS),
@@ -330,8 +332,8 @@ def tile_list_replay_curiosity_bonus_kernel(
         load_words(1)
         move_scales(1)
         nc.sync.dma_start(w3_raw[:], w3_words.rearrange("a p n i -> p a (n i)").bitcast(I32))
-        for b in range(3):
-            load_w4(b)
+        load_w4(1)
+        load_w4(0)
         spread_constants()
         round_w1(0)
         reorder_scales(2, "scalar")
@@ -366,8 +368,7 @@ def tile_list_replay_curiosity_bonus_kernel(
         features(0)
         features(1)
         predict(1)
-        round_w4(0, "gpsimd")
-        round_w4(1, "gpsimd")
+        round_w4(2, "gpsimd")
         gather_words(NEXT, 1, second)
         features(2)
         features(3)
@@ -378,7 +379,7 @@ def tile_list_replay_curiosity_bonus_kernel(
         weigh(0, nc.gpsimd)
         weigh(1, nc.gpsimd)
         close_p(2)
-        round_w4(2, "scalar")
+        round_w4(0, "scalar")
         features(4)
         features(5)
         subtract(2)
@@ -387,11 +388,12 @@ def tile_list_replay_curiosity_bonus_kernel(
         close_p(3)
         square(2)
         square(3)
-        quantize_w4(0)
-        quantize_w4(1)
+        round_w4(1, "vector")
         quantize_w4(2)
+        quantize_w4(0)
         quantize_h(0)
-        readout(0, (0, 1, 2))
+        quantize_w4(1)
+        readout(0, (2, 0))
         weigh(2, nc.gpsimd)
         weigh(3, nc.gpsimd)
         subtract(4)
@@ -399,19 +401,20 @@ def tile_list_replay_curiosity_bonus_kernel(
         predict(3)
         features(6)
         features(7)
-        finish(0, 0, "scalar")
+        readout(0, (1,))
+        finish(0, 2, "scalar")
         square(4)
         square(5)
-        finish(0, 1, "vector")
+        finish(0, 0, "vector")
         subtract(6)
         subtract(7)
-        finish(0, 2, "scalar")
+        finish(0, 1, "scalar")
+        square(6)
+        square(7)
         quantize_h(1)
         readout(1, (0, 1, 2))
         weigh(4, nc.vector)
         weigh(5, nc.vector)
-        square(6)
-        square(7)
         finish(1, 0, "scalar")
         weigh(6, nc.vector)
         quantize_h(2)

@@ -332,8 +332,8 @@ def tile_list_replay_curiosity_bonus_kernel(
         load_words(1)
         move_scales(1)
         nc.sync.dma_start(w3_raw[:], w3_words.rearrange("a p n i -> p a (n i)").bitcast(I32))
-        load_w4(1)
         load_w4(0)
+        load_w4(1)
         spread_constants()
         round_w1(0)
         reorder_scales(2, "scalar")
@@ -368,7 +368,8 @@ def tile_list_replay_curiosity_bonus_kernel(
         features(0)
         features(1)
         predict(1)
-        round_w4(2, "gpsimd")
+        round_w4(1, "gpsimd")
+        round_w4(0, "scalar")
         gather_words(NEXT, 1, second)
         features(2)
         features(3)
@@ -379,7 +380,7 @@ def tile_list_replay_curiosity_bonus_kernel(
         weigh(0, nc.gpsimd)
         weigh(1, nc.gpsimd)
         close_p(2)
-        round_w4(0, "scalar")
+        round_w4(2, "scalar")
         features(4)
         features(5)
         subtract(2)
@@ -388,12 +389,11 @@ def tile_list_replay_curiosity_bonus_kernel(
         close_p(3)
         square(2)
         square(3)
-        round_w4(1, "vector")
-        quantize_w4(2)
         quantize_w4(0)
-        quantize_h(0)
         quantize_w4(1)
-        readout(0, (2, 0))
+        quantize_w4(2)
+        quantize_h(0)
+        readout(0, (0, 1))
         weigh(2, nc.gpsimd)
         weigh(3, nc.gpsimd)
         subtract(4)
@@ -401,14 +401,14 @@ def tile_list_replay_curiosity_bonus_kernel(
         predict(3)
         features(6)
         features(7)
-        readout(0, (1,))
-        finish(0, 2, "scalar")
+        readout(0, (2,))
+        finish(0, 0, "scalar")
         square(4)
         square(5)
-        finish(0, 0, "vector")
+        finish(0, 1, "vector")
         subtract(6)
         subtract(7)
-        finish(0, 1, "scalar")
+        finish(0, 2, "scalar")
         square(6)
         square(7)
         quantize_h(1)

from contextlib import ExitStack

import concourse.mybir as mybir
from concourse.masks import make_identity

K, H, N, T, S = 1024, 512, 768, 4096, 1024
FLOPS = 2 * S * H * (3 * K + N)

F32 = mybir.dt.float32
BF16 = mybir.dt.bfloat16
I32 = mybir.dt.int32
U32 = mybir.dt.uint32
U16 = mybir.dt.uint16
U8 = mybir.dt.uint8
FP8X4 = mybir.dt.float8_e4m3fn_x4
FP4X4 = mybir.dt.float4_e2m1fn_x4
ACT = mybir.ActivationFunctionType
ALU = mybir.AluOpType

P = 128
PACK = 4
PASSES = K // (P * PACK)
HALF = 512
CHUNK = 128
GROUP = 256
GROUPS = S // GROUP
NEIGHBOURS = 4
THIRD = N // 3
ROW_TILES = N // P
QUADRANT = 32
RUN = 4
STATE, ACTION, NEXT = 0, 1, 2
FIRST, SECOND = 0, 1
BANKS = 8
PAIR = 2
QUEUE_DEPTH = {"vector": 30, "scalar": 16, "gpsimd": 9}
SCALE_ROW0 = P - QUADRANT
WEIGHT_OFFSET = {2: 0, 3: 8}


def tile_list_replay_curiosity_bonus_kernel(
    tc, tab_words, tab_scales, offs, offs2, offs3, w1, w2_words, w2_scales, w3_words, w3_scales, g, w4, b4, out
):
    nc = tc.nc
    with ExitStack() as ctx:
        keep = ctx.enter_context(tc.tile_pool(name="keep", bufs=1))
        line = ctx.enter_context(tc.tile_pool(name="line", bufs=1))
        psum = ctx.enter_context(tc.psum_pool(name="psum", bufs=1))

        def bank(shape, name):
            return psum.tile(shape, F32, name=name, tag="bank", bufs=BANKS)

        def queued(eng, shape, dtype, name):
            return line.tile(shape, dtype, name=name, tag=eng, bufs=QUEUE_DEPTH[eng], align_bytes=64)

        lists = [keep.tile([P, S // 16], U16, name=f"list{x}") for x in range(3)]
        window = keep.tile([P, T // 4], I32, name="tsc")
        picked = keep.tile([P, 3 * S], U8, name="picked")
        planes = [keep.tile([P, 3 * S // 4], I32, name=f"planes{a}", align_bytes=64) for a in range(PASSES)]
        wsc_raw = {}
        nc.vector.memset(window[0:SCALE_ROW0, :], 0)
        g_row = keep.tile([1, H], F32, name="g_row")
        rows = keep.tile([P, H], F32, name="rows")
        nc.gpsimd.memset(rows[:], 0.0)
        ident = keep.tile([P, P], F32, name="ident")
        make_identity(nc, ident[:])
        consts = keep.tile([P, PACK + ROW_TILES], F32, name="consts")
        gain = consts[:, 0:PACK]

        words = [keep.tile([P, T], I32, name=f"words{a}") for a in range(PASSES)]
        w1_raw = [keep.tile([P, PACK, H], F32, name=f"w1_raw{a}") for a in range(PASSES)]
        w2_raw = keep.tile([P, PASSES, H // 2], I32, name="w2_raw")
        w3_raw = keep.tile([P, PASSES, H], I32, name="w3_raw")
        w4_parts = [(0, 2 * THIRD), (2 * THIRD, N)]
        w4_raw = [keep.tile([P, PACK, n1 - n0], F32, name=f"w4_raw{n0}") for n0, n1 in w4_parts]

        def load_words(a):
            nc.sync.dma_start(words[a][:], tab_words[a].rearrange("p t i -> p (t i)").bitcast(I32))

        def load_w1(a):
            pass_rows = w1[P * PACK * a : P * PACK * (a + 1), :]
            nc.sync.dma_start(w1_raw[a][:], pass_rows.rearrange("(p j) r -> p j r", j=PACK))

        def load_weight_scales(w, scales):
            wsc_raw[w] = queued("gpsimd", [P, PASSES, H // 4], I32, f"wsc_raw{w}")
            nc.gpsimd.memset(wsc_raw[w][:], 0)
            for r in range(RUN):
                nc.gpsimd.dma_start(
                    wsc_raw[w][WEIGHT_OFFSET[w] + r : P : QUADRANT, :, :],
                    scales.rearrange("a (q r) n -> r q a n", r=RUN)[r].bitcast(I32),
                )

        def load_w4(part):
            n0, n1 = w4_parts[part]
            by_slot = w4.rearrange("(c t i) n -> t c i n", t=PACK, i=NEIGHBOURS)
            for t in range(PACK):
                nc.sync.dma_start(w4_raw[part][:, t, :], by_slot[t][:, :, n0:n1])

        nc.sync.dma_start(window[SCALE_ROW0:P, :], tab_scales.rearrange("a q n -> (a q) n").bitcast(I32))
        nc.sync.dma_start(lists[ACTION][:], offs2)
        nc.sync.dma_start(lists[STATE][:], offs)
        nc.sync.dma_start(lists[NEXT][:], offs3)
        nc.scalar.dma_start(g_row[:], g.rearrange("(o r) -> o r", o=1))
        bias_rows = b4.rearrange("(u p) -> u p", p=P)
        nc.scalar.dma_start(rows[PACK : 2 * PACK, 0:P], bias_rows[0:PACK])
        nc.scalar.dma_start(rows[2 * PACK : PACK + ROW_TILES, 0:P], bias_rows[PACK:ROW_TILES])
        nc.vector.memset(planes[0][:], 0)
        load_weight_scales(2, w2_scales)
        load_weight_scales(3, w3_scales)
        nc.gpsimd.memset(planes[1][:], 0)
        load_words(0)
        nc.sync.dma_start(w2_raw[:], w2_words.rearrange("a p n -> p a n").bitcast(I32))
        load_w1(0)
        load_w1(1)

        w1s = keep.tile([P, PASSES, H], U8, name="w1s", align_bytes=64)
        w4s = keep.tile([P, N], U8, name="w4s", align_bytes=64)
        hs = [keep.tile([P, GROUP], U8, name=f"hs{i}", align_bytes=64) for i in range(GROUPS)]
        out_v = out.rearrange("(u p) j -> p u j", p=P)

        gw, w1_bf, w1q, wp, wsc, acc, done = {}, {}, {}, {}, {}, {}, {}
        pred, feat, diff, sq, hb, hq, w4_bf, w4q, ys = {}, {}, {}, {}, {}, {}, {}, {}, {}

        def reorder_scales(w, eng):
            wsc[w] = queued(eng, [P, PASSES, H // 4], U32, f"wsc{w}")
            move = nc.gpsimd.tensor_copy if eng == "gpsimd" else nc.scalar.copy
            move(
                wsc[w][:].rearrange("p a (t c) -> p a t c", t=PACK),
                wsc_raw[w][:].bitcast(U32).rearrange("p a (c t) -> p a t c", t=PACK),
            )

        def reorder_words(w, raw, span, a, eng):
            wp[w, a] = queued(eng, [P, P * span], U32, f"wp{w}{a}")
            move = nc.gpsimd.tensor_copy if eng == "gpsimd" else nc.scalar.copy
            move(
                wp[w, a][:].rearrange("p (t c i) -> p t c i", t=PACK, i=span),
                raw[:, a, :].bitcast(U32).rearrange("p (c t i) -> p t c i", t=PACK, i=span),
            )

        def gather_scales(x):
            nc.vector.tensor_copy(picked[:, S * x : S * (x + 1)], window[:].bitcast(U8).indirect(lists[x][:]))

        def move_scales(a):
            for r in range(RUN):
                first = SCALE_ROW0 + 16 * a + r
                nc.sync.dma_start(
                    planes[a][r:P:QUADRANT, :], picked[first : first + 3 * RUN + 1 : RUN, :].bitcast(I32)
                )

        def table_plane(x, a, j0, width):
            return planes[a][:].bitcast(U8)[:, S * x + j0 : S * x + j0 + width]

        def spread_constants():
            nc.scalar.activation(
                rows[0:1, :].rearrange("o (t c i) -> o t c i", t=PACK, i=NEIGHBOURS),
                g_row[:].rearrange("o (c t i) -> o t c i", t=PACK, i=NEIGHBOURS),
                ACT.Copy,
            )
            turned = bank([P, PACK, P], "turned")
            for t in range(PACK):
                nc.tensor.transpose(turned[:, t, :], rows[:, P * t : P * (t + 1)], ident[:])
            nc.scalar.activation(gain, turned[:, :, 0], ACT.Copy)
            nc.scalar.activation(consts[:, PACK:], turned[:, 0, PACK : PACK + ROW_TILES], ACT.Copy)

        def gather_words(x, a, groups):
            j0, width = GROUP * groups[0], GROUP * len(groups)
            picked_words = queued("vector", [P, width], U32, f"gw{x}{a}{groups[0]}")
            offsets = lists[x][:, j0 // 16 : (j0 + width) // 16]
            nc.vector.tensor_copy(picked_words[:], words[a][:].bitcast(U32).indirect(offsets))
            for n, group in enumerate(groups):
                gw[x, a, group] = picked_words[:, GROUP * n : GROUP * (n + 1)]

        def round_w1(a):
            src = w1_raw[a][:].rearrange("p j (c t i) -> p t c j i", t=PACK, i=NEIGHBOURS)
            w1_bf[a] = queued("scalar", [P, PACK, P // NEIGHBOURS, NEIGHBOURS, PACK], BF16, f"w1_bf{a}")
            for t in range(PACK):
                nc.scalar.activation(w1_bf[a][:, t].rearrange("p c i j -> p c j i"), src[:, t], ACT.Copy)

        def quantize_w1(a):
            w1q[a] = queued("vector", [P, H], U32, f"w1q{a}")
            nc.vector.quantize_mx(
                out=w1q[a][:].bitcast(FP8X4),
                scales=w1s[:, a, :],
                in_=w1_bf[a][:].rearrange("p t c i j -> p (t c i j)"),
            )

        def p_pass(x, a, group):
            for t in range(PACK):
                key = group, t // PAIR
                if key not in acc:
                    acc[key] = bank([P, PAIR, GROUP], f"acc{group}{t}")
                    done[key] = 0
                m = slice(P * t, P * (t + 1))
                if x == STATE:
                    lhs, lhs_s = w1q[a][:, m].bitcast(FP8X4), w1s[:, a, m]
                else:
                    lhs = wp[2, a][:].bitcast(U8)[:, 2 * P * t : 2 * P * (t + 1)].bitcast(FP4X4)
                    lhs_s = wsc[2][:, a, :].bitcast(U8)[:, m]
                nc.tensor.matmul_mx(
                    acc[key][:, t % PAIR, :],
                    lhsT=lhs,
                    lhsT_scale=lhs_s,
                    rhs=gw[x, a, group].bitcast(FP8X4),
                    rhs_scale=table_plane(x, a, GROUP * group, GROUP),
                    start=(done[key] == 0),
                    stop=(done[key] == 2 * PASSES * PAIR - 1),
                )
                done[key] = done[key] + 1

        def predict(group):
            pred[group] = queued("scalar", [P, PACK, GROUP], F32, f"pred{group}")
            for b in range(PACK // PAIR):
                nc.scalar.activation(pred[group][:, PAIR * b : PAIR * (b + 1), :], acc[group, b][:], ACT.Tanh)

        def round_w4(b, eng):
            w4_bf[b] = queued(eng, [P, THIRD, PACK], BF16, f"w4_bf{b}")
            src = w4_raw[b // 2][:, :, THIRD * (b % 2) : THIRD * (b % 2 + 1)]
            by_fours = (
                w4_bf[b][:].rearrange("p (c i) t -> p c t i", i=NEIGHBOURS),
                src.rearrange("p t (c i) -> p c t i", i=NEIGHBOURS),
            )
            if eng == "scalar":
                nc.scalar.activation(*by_fours, ACT.Copy)
            elif eng == "vector":
                nc.vector.tensor_copy(*by_fours)
            else:
                nc.gpsimd.tensor_scalar(w4_bf[b][:], src.rearrange("p t n -> p n t"), 1.0, 0.0, ALU.mult, ALU.add)

        def quantize_w4(b):
            w4q[b] = queued("vector", [P, THIRD], U32, f"w4q{b}")
            nc.vector.quantize_mx(
                out=w4q[b][:].bitcast(FP8X4),
                scales=w4s[:, THIRD * b : THIRD * (b + 1)],
                in_=w4_bf[b][:].rearrange("p n t -> p (n t)"),
            )

        def place_in_group(c):
            j0 = CHUNK * c % GROUP
            return CHUNK * c // GROUP, slice(j0, j0 + CHUNK)

        def features(c):
            group, cols = place_in_group(c)
            feat[c] = bank([P, PACK, CHUNK], f"feat{c}")
            for t in range(PACK):
                for a in range(PASSES):
                    m = slice(P * t, P * (t + 1))
                    nc.tensor.matmul_mx(
                        feat[c][:, t, :],
                        lhsT=wp[3, a][:, m].bitcast(FP8X4),
                        lhsT_scale=wsc[3][WEIGHT_OFFSET[3] :, a, :].bitcast(U8)[:, m],
                        rhs=gw[NEXT, a, group][:, cols].bitcast(FP8X4),
                        rhs_scale=table_plane(NEXT, a, CHUNK * c, CHUNK),
                        start=(a == 0),
                        stop=(a == PASSES - 1),
                    )

        def subtract(c):
            group, cols = place_in_group(c)
            diff[c] = queued("vector", [P, PACK, CHUNK], F32, f"diff{c}")
            nc.vector.tensor_tensor(diff[c][:], pred[group][:, :, cols], feat[c][:], ALU.subtract)

        def square(c):
            sq[c] = queued("scalar", [P, CHUNK, PACK], F32, f"sq{c}")
            nc.scalar.activation(
                sq[c][:].rearrange("p (c i) t -> p c t i", i=NEIGHBOURS),
                diff[c][:].rearrange("p t (c i) -> p c t i", i=NEIGHBOURS),
                ACT.Square,
            )

        def weigh(c, engine):
            group, c0 = c // 2, CHUNK * (c % 2)
            if group == GROUPS - 1 and group not in hb:
                hb[group] = queued("vector", [P, GROUP, PACK], BF16, f"hb{group}")
            if group not in hb:
                hb[group] = line.tile([P, GROUP, PACK], BF16, name=f"hb{group}", tag="hb", bufs=1, align_bytes=64)
            engine.tensor_tensor(
                hb[group][:, c0 : c0 + CHUNK, :], sq[c][:], gain.unsqueeze(1).to_broadcast([P, CHUNK, PACK]), ALU.mult
            )

        def quantize_h(group):
            hq[group] = queued("vector", [P, GROUP], U32, f"hq{group}")
            nc.vector.quantize_mx(
                out=hq[group][:].bitcast(FP8X4), scales=hs[group][:], in_=hb[group][:].rearrange("p j t -> p (j t)")
            )

        def product(y, group, u):
            nc.tensor.matmul_mx(
                y,
                lhsT=w4q[u // 2][:, P * (u % 2) : P * (u % 2 + 1)].bitcast(FP8X4),
                lhsT_scale=w4s[:, P * u : P * (u + 1)],
                rhs=hq[group][:].bitcast(FP8X4),
                rhs_scale=hs[group][:],
                start=True,
                stop=True,
            )

        def readout(group, thirds):
            for b in thirds:
                ys[group, b] = bank([P, 2, GROUP], f"y{group}{b}")
                for e in range(2):
                    product(ys[group, b][:, e, :], group, 2 * b + e)

        def finish(group, b, eng):
            res = queued(eng, [P, 2, GROUP], F32, f"res{group}{b}")
            bias = consts[:, PACK + 2 * b : PACK + 2 * b + 2]
            y = ys[group, b]
            if eng == "vector":
                nc.vector.tensor_tensor(res[:], y[:], bias.unsqueeze(2).to_broadcast([P, 2, GROUP]), ALU.add)
                nc.sync.dma_start(out_v[:, 2 * b : 2 * b + 2, GROUP * group : GROUP * (group + 1)], res[:])
            else:
                for e in range(2):
                    nc.scalar.activation(res[:, e, :], y[:, e, :], ACT.Identity, bias=bias[:, e : e + 1])
                    nc.sync.dma_start(out_v[:, 2 * b + e, GROUP * group : GROUP * (group + 1)], res[:, e, :])

        def last_readout(group):
            y = [bank([P, GROUP], f"y{group}{u}") for u in range(ROW_TILES)]
            for u in range(ROW_TILES):
                product(y[u][:], group, u)
            for u in range(ROW_TILES):
                eng = ("vector", "scalar")[u % 2]
                res = queued(eng, [P, GROUP], F32, f"res{group}{u}")
                bias = consts[:, PACK + u : PACK + u + 1]
                if eng == "vector":
                    nc.vector.tensor_scalar(res[:], y[u][:], bias, None, ALU.add)
                else:
                    nc.scalar.activation(res[:], y[u][:], ACT.Identity, bias=bias)
                nc.sync.dma_start(out_v[:, u, GROUP * group : GROUP * (group + 1)], res[:])

        for x in (ACTION, STATE, NEXT):
            gather_scales(x)
        move_scales(0)
        load_words(1)
        move_scales(1)
        nc.sync.dma_start(w3_raw[:], w3_words.rearrange("a p n i -> p a (n i)").bitcast(I32))
        load_w4(0)
        load_w4(1)
        spread_constants()
        round_w1(0)
        reorder_scales(2, "scalar")
        for a in range(PASSES):
            reorder_words(2, w2_raw, 2, a, "scalar")
        reorder_scales(3, "gpsimd")
        reorder_words(3, w3_raw, 4, 0, "gpsimd")
        round_w1(1)
        reorder_words(3, w3_raw, 4, 1, "scalar")

        first, second = (0, 1), (2, 3)

        def close_p(group):
            for x in (ACTION, STATE):
                gather_words(x, 1, (group,))
                p_pass(x, 1, group)

        for half in (first, second):
            for x in (ACTION, STATE):
                gather_words(x, 0, half)
        for a, half in enumerate((first, second)):
            quantize_w1(a)
            gather_words(NEXT, 0, half)
        for x in (ACTION, STATE):
            for group in range(GROUPS):
                p_pass(x, 0, group)

        close_p(0)
        predict(0)
        close_p(1)
        gather_words(NEXT, 1, first)
        features(0)
        features(1)
        predict(1)
        round_w4(1, "gpsimd")
        round_w4(0, "scalar")
        gather_words(NEXT, 1, second)
        features(2)
        features(3)
        subtract(0)
        square(0)
        subtract(1)
        square(1)
        weigh(0, nc.gpsimd)
        weigh(1, nc.gpsimd)
        close_p(2)
        round_w4(2, "scalar")
        features(4)
        features(5)
        subtract(2)
        subtract(3)
        predict(2)
        close_p(3)
        square(2)
        square(3)
        quantize_w4(0)
        quantize_w4(1)
        quantize_w4(2)
        quantize_h(0)
        readout(0, (0, 1))
        weigh(2, nc.gpsimd)
        weigh(3, nc.gpsimd)
        subtract(4)
        subtract(5)
        predict(3)
        features(6)
        features(7)
        readout(0, (2,))
        finish(0, 0, "scalar")
        square(4)
        square(5)
        finish(0, 1, "vector")
        subtract(6)
        subtract(7)
        finish(0, 2, "scalar")
        square(6)
        square(7)
        quantize_h(1)
        readout(1, (0, 1, 2))
        weigh(4, nc.vector)
        weigh(5, nc.vector)
        finish(1, 0, "scalar")
        weigh(6, nc.vector)
        quantize_h(2)
        readout(2, (0, 1, 2))
        finish(1, 1, "scalar")
        weigh(7, nc.vector)
        finish(1, 2, "scalar")
        finish(2, 0, "vector")
        quantize_h(3)
        finish(2, 1, "scalar")
        finish(2, 2, "scalar")
        last_readout(3)
